import numpy as np
import ml_dtypes


def mxq(x, axis, fmt="e4m3"):
    dtype, down = {"e4m3": (ml_dtypes.float8_e4m3fn, 7), "e5m2": (ml_dtypes.float8_e5m2, 14)}[fmt]
    v = np.moveaxis(np.asarray(x, np.float32).astype(ml_dtypes.bfloat16).astype(np.float64), axis, -1)
    blocks = v.reshape(v.shape[:-1] + (-1, 32))
    amax = np.abs(blocks).max(-1, keepdims=True)
    byte = np.maximum(np.where(amax > 0, np.frexp(amax)[1] - 1 + 127, 0) - down, 1)
    scale = np.exp2(byte - 127.0)
    codes = (blocks / scale).astype(np.float32).astype(dtype).astype(np.float64)
    return np.moveaxis((codes * scale).reshape(v.shape), -1, axis)


WIDE = False


def mx_kscale(k):
    if not WIDE:
        return np.ones(k)
    levels = np.array([10, -10, 5, -5, 0])
    if k % 512:
        return np.exp2(np.random.permutation(np.resize(levels, k // 32))).repeat(32)
    a = np.empty((k // 512, 16))
    for p in range(k // 512):
        a[p, :8] = np.random.permutation(np.resize(levels, 8))
        for g in range(8):
            far = levels[np.abs(levels - a[p, g]) >= 10]
            a[p, g + 8] = far[np.random.randint(len(far))]
    return np.exp2(a.ravel()).repeat(32)


def f64(x):
    return np.asarray(x).astype(np.float64)


def striped(idx):
    return np.tile(np.asarray(idx).reshape(-1, 16).T, (8, 1)).astype(np.uint16)


def unstriped(offs):
    return offs[:16].T.reshape(-1).astype(np.int64)


E2M1 = np.array([0.0, 0.5, 1.0, 1.5, 2.0, 3.0, 4.0, 6.0, -0.0, -0.5, -1.0, -1.5, -2.0, -3.0, -4.0, -6.0])


def pack_weight(w, fmt):
    k, n = w.shape
    w = f64(np.asarray(w, np.float32).astype(ml_dtypes.bfloat16)).reshape(k // 32, 32, n)
    amax = np.abs(w).max(1)
    if fmt == "e4m3":
        byte = np.frexp(amax)[1] - 1 + 127 - 7
    else:
        mant, ex = np.frexp(amax / 6.0)
        byte = np.where(mant > 0.5, ex, ex - 1) + 127
    byte = np.clip(np.where(amax > 0, byte, 1), 1, 254)
    scaled = (w * np.exp2(127.0 - byte)[:, None, :]).reshape(k, n).astype(np.float32)
    by_word = np.ascontiguousarray(scaled.reshape(k // 512, 128, 4, n).transpose(0, 1, 3, 2))
    if fmt == "e4m3":
        words = by_word.astype(ml_dtypes.float8_e4m3fn).view(np.uint8)
    else:
        c = by_word.astype(ml_dtypes.float4_e2m1fn).view(np.uint8) & 0xF
        words = (c[..., 0::2] | (c[..., 1::2] << 4)).reshape(k // 512, 128, 2 * n)
    return np.ascontiguousarray(words), np.ascontiguousarray(byte.astype(np.uint8).reshape(k // 512, 16, n))


def unpack_weight(words, scales, fmt):
    g, _, n = scales.shape
    words = np.ascontiguousarray(words).reshape(g, 128, n, -1)
    if fmt == "e4m3":
        vals = words.view(ml_dtypes.float8_e4m3fn).astype(np.float64)
    else:
        nib = np.empty((g, 128, n, 4), np.uint8)
        nib[..., 0::2] = words & 0xF
        nib[..., 1::2] = words >> 4
        vals = E2M1[nib]
    vals = vals * np.repeat(np.exp2(scales.astype(np.float64) - 127.0), 8, axis=1)[..., None]
    return vals.transpose(0, 1, 3, 2).reshape(g * 512, n)


B, N, T, D, DV, NQ = 1, 1536, 4096, 512, 128, 256
PAGE = 512
DRAFT = 128


def setup_inputs():
    n = np.random.standard_normal
    pages = np.random.permutation(T // PAGE)[:B * N // PAGE]
    idx = (pages[:, None] * PAGE + np.arange(PAGE)[None, :]).reshape(-1)
    s = mx_kscale(D)[:, None]
    u = np.ones(T)
    u[idx] = mx_kscale(B * N)
    r = np.random.uniform(0.5, 2.0, T)
    qp = [pack_weight(x, "e4m3") for x in n((B, D, NQ)) * s * (1.00 / np.sqrt(D))]
    k = n((D, T)) / s
    v = n((DV, T)) / (u * r)
    kp = pack_weight(k, "e4m3")
    vp = pack_weight(v.T, "e4m3")
    when = np.zeros(T)
    when[idx] = np.concatenate([np.concatenate([np.arange(N - DRAFT), N - DRAFT + np.random.randint(0, 16, DRAFT)]) for b in range(B)])
    return {
        "q_words": np.stack([x[0] for x in qp]),
        "q_scales": np.stack([x[1] for x in qp]),
        "k_words": kp[0],
        "k_scales": kp[1],
        "v_words": vp[0],
        "v_scales": vp[1],
        "vs": np.tile(u * r, (128, 1)).astype(np.float32),
        "pos": np.tile(when, (128, 1)).astype(np.float32),
        "qpos": np.random.randint(N - DRAFT, N - DRAFT + 16, (B, NQ, 1)).astype(np.float32),
        "offs": striped(idx),
        "voffs": striped((pages[:, None] * DV + np.arange(DV)[None, :]).reshape(-1)),
    }


def reference(q_words, q_scales, k_words, k_scales, v_words, v_scales, vs, pos, qpos, offs, voffs):
    idx = unstriped(offs)
    k = unpack_weight(k_words, k_scales, "e4m3")
    v = unpack_weight(v_words, v_scales, "e4m3")
    v = v.reshape(T // 512, 512, DV)[unstriped(voffs)[::DV] // DV].reshape(B, N, DV)
    pick = lambda x: x[:, idx].reshape(x.shape[0], B, N).transpose(1, 0, 2)
    q = np.stack([unpack_weight(q_words[b], q_scales[b], "e4m3") for b in range(B)])
    score = q.transpose(0, 2, 1) @ pick(k)
    score = np.where(pick(f64(pos))[:, :1, :] <= f64(qpos), score, -30000.0)
    m = score.max(-1, keepdims=True)
    p = np.exp(score - m)
    total = p.sum(-1, keepdims=True)
    w = p * pick(f64(vs))[:, :1, :]
    y = mxq(w, 2, "e4m3") @ v
    y = y / total
    return y

@@ -1,0 +1,207 @@
+from contextlib import ExitStack
+
+import concourse.mybir as mybir
+from concourse.masks import make_identity
+
+N, T, D, DV, NQ = 1536, 4096, 512, 128, 256
+PAGE = 512
+P = 128
+PACK = 4
+PAGES = N // PAGE
+POOL_PAGES = T // PAGE
+Q_TILES = NQ // P
+MASKED = 30000.0
+STEEP = 2.0 ** 80
+
+FLOPS = 2 * NQ * N * D + 2 * NQ * N * DV
+
+F32 = mybir.dt.float32
+BF16 = mybir.dt.bfloat16
+I32 = mybir.dt.int32
+U32 = mybir.dt.uint32
+U16 = mybir.dt.uint16
+U8 = mybir.dt.uint8
+FP8X4 = mybir.dt.float8_e4m3fn_x4
+ALU = mybir.AluOpType
+ACT = mybir.ActivationFunctionType
+
+
+def tile_attend_pkv8q_soft_draft_kernel(
+    tc, q_words, q_scales, k_words, k_scales, v_words, v_scales, vs, pos, qpos, offs, voffs, out
+):
+    nc = tc.nc
+    with ExitStack() as ctx:
+        keep = ctx.enter_context(tc.tile_pool(name="keep", bufs=1))
+        psum = ctx.enter_context(tc.psum_pool(name="psum", bufs=1))
+
+        def sb(shape, dtype, name):
+            return keep.tile(shape, dtype, name=name, align_bytes=64)
+
+        def scale_rows(plane, quad):
+            return plane[32 * quad : 32 * quad + 4, :].bitcast(I32)
+
+        slots = keep.tile([P, N // 16], U16, name="slots")
+        nc.sync.dma_start(slots[:], offs)
+        qw = sb([P, NQ], U32, "qw")
+        nc.sync.dma_start(qw[:].bitcast(I32), q_words[0, 0].rearrange("g q r -> g (q r)").bitcast(I32))
+        qpos_rows = sb([P, NQ], F32, "qpos_rows")
+        nc.sync.dma_start(qpos_rows[:], qpos[0].rearrange("q o -> (q o)").partition_broadcast(P))
+        vcols = keep.tile([P, PAGES * DV // 16], U16, name="vcols")
+        nc.sync.dma_start(vcols[:], voffs)
+
+        ks_pool = keep.tile([P, T], U8, name="ks_pool", tag="ks_then_vs", align_bytes=64)
+        nc.vector.memset(ks_pool[:].bitcast(I32), 0)
+        for quad in range(4):
+            nc.sync.dma_start(scale_rows(ks_pool, quad), k_scales[0, 4 * quad : 4 * quad + 4, :].bitcast(I32))
+
+        warm_in = keep.tile([P, 1], F32, name="warm_in", tag="warm_then_kw", align_bytes=64)
+        nc.vector.memset(warm_in[:], 0.0)
+        warm_out = sb([P, 1], F32, "warm_out")
+        nc.scalar.activation(warm_out[:], warm_in[:], ACT.Exp)
+        kw_pool = keep.tile([P, T], U32, name="kw_pool", tag="warm_then_kw", align_bytes=64)
+        nc.sync.dma_start(kw_pool[:].bitcast(I32), k_words[0].rearrange("g t r -> g (t r)").bitcast(I32))
+
+        pos_pool = keep.tile([P, T], F32, name="pos_pool", tag="pos_then_vw", align_bytes=64)
+        nc.vector.memset(pos_pool[:], 0.0)
+        nc.scalar.dma_start(pos_pool[0:1, :], pos[0:1, :])
+
+        qs = sb([P, NQ], U8, "qs")
+        nc.vector.memset(qs[:].bitcast(I32), 0)
+        for quad in range(4):
+            nc.sync.dma_start(scale_rows(qs, quad), q_scales[0, 0, 4 * quad : 4 * quad + 4, :].bitcast(I32))
+        vsc_pool = sb([P, POOL_PAGES * DV], U8, "vsc_pool")
+        nc.vector.memset(vsc_pool[:].bitcast(I32), 0)
+        for quad in range(4):
+            nc.sync.dma_start(
+                scale_rows(vsc_pool, quad).rearrange("f (u e) -> f u e", u=POOL_PAGES),
+                v_scales[:, 4 * quad : 4 * quad + 4, :].rearrange("u f e -> f u e").bitcast(I32),
+            )
+
+        ident = sb([P, P], F32, "ident")
+        make_identity(nc, ident[:])
+
+        def page_slots(g):
+            return slots[:, g * PAGE // 16 : (g + 1) * PAGE // 16]
+
+        ks = sb([P, N], U8, "ks")
+        nc.vector.tensor_copy(ks[:], ks_pool[:].indirect(slots[:]))
+        vs_pool = keep.tile([P, T], F32, name="vs_pool", tag="ks_then_vs", align_bytes=64)
+        nc.sync.dma_start(vs_pool[:], vs)
+
+        hidden = []
+        for g in range(PAGES):
+            pos_row = sb([P, PAGE], F32, "pos_row%d" % g)
+            nc.vector.tensor_copy(pos_row[:], pos_pool[:].indirect(page_slots(g)))
+            turned = psum.tile([P, PACK, P], F32, name="turned", tag="turn", bufs=2)
+            for j in range(PACK):
+                nc.tensor.transpose(turned[:, j, :], pos_row[:, j * P : (j + 1) * P], ident[:])
+            pos_cols = sb([P, PACK], F32, "pos_cols%d" % g)
+            nc.scalar.activation(pos_cols[:], turned[:, :, 0], ACT.Copy, scale=STEEP)
+            for j in range(PACK):
+                r = sb([P, NQ], F32, "hidden%d_%d" % (g, j))
+                nc.scalar.activation(r[:], qpos_rows[:], ACT.Relu, bias=pos_cols[:, j : j + 1], scale=-STEEP)
+                hidden.append(r)
+
+        vw_pool = keep.tile([P, POOL_PAGES * DV], U32, name="vw_pool", tag="pos_then_vw", align_bytes=64)
+        nc.sync.dma_start(
+            vw_pool[:].bitcast(I32).rearrange("g (u e) -> g u e", e=DV),
+            v_words.rearrange("u g e r -> g u (e r)").bitcast(I32),
+        )
+
+        neg = []
+        for g in range(PAGES):
+            kw = sb([P, PAGE], U32, "kw%d" % g)
+            nc.vector.tensor_copy(kw[:], kw_pool[:].indirect(page_slots(g)))
+            for half in range(2):
+                a = psum.tile([P, 2, NQ], F32, name="a", tag="a", bufs=2)
+                for jj in range(2):
+                    j = 2 * half + jj
+                    nc.tensor.matmul_mx(
+                        out=a[:, jj, :],
+                        lhsT=kw[:, j * P : (j + 1) * P].bitcast(FP8X4),
+                        lhsT_scale=ks[:, g * PAGE + j * P : g * PAGE + (j + 1) * P],
+                        rhs=qw[:].bitcast(FP8X4),
+                        rhs_scale=qs[:],
+                        start=True,
+                        stop=True,
+                    )
+                na = sb([P, 2, NQ], F32, "neg%d_%d" % (g, half))
+                nc.scalar.activation(na[:], a[:], ACT.Copy, scale=-1.0)
+                neg.append(na)
+
+        vs_row = sb([P, N], F32, "vs_row")
+        nc.vector.tensor_copy(vs_row[:], vs_pool[:].indirect(slots[:]))
+
+        down = {}
+        low = {}
+        for g in range(PAGES):
+            for u in range(Q_TILES):
+                x = psum.tile([P, PAGE], F32, name="x", tag="x", bufs=3)
+                for j in range(PACK):
+                    cols = slice(u * P, (u + 1) * P)
+                    nc.tensor.matmul(x[:, j * P : (j + 1) * P], hidden[PACK * g + j][:, cols], ident[:], start=True, stop=False, is_transpose=True)
+                    nc.tensor.matmul(x[:, j * P : (j + 1) * P], neg[2 * g + j // 2][:, j % 2, cols], ident[:], start=False, stop=True, is_transpose=True)
+                down[u, g] = sb([P, PACK, P], F32, "down%d_%d" % (u, g))
+                low[u, g] = sb([P, 1], F32, "low%d_%d" % (u, g))
+                nc.vector.tensor_scalar(
+                    down[u, g][:],
+                    x[:].rearrange("q (s t) -> q t s", t=PACK),
+                    MASKED,
+                    low[u, g - 1][:] if g else MASKED,
+                    op0=ALU.min,
+                    op1=ALU.min,
+                    accum_out=low[u, g][:],
+                )
+
+        vs_cols = []
+        for g in range(PAGES):
+            turned = psum.tile([P, PACK, P], F32, name="turned", tag="turn", bufs=2)
+            for t in range(PACK):
+                nc.tensor.transpose(turned[:, t, :], vs_row[:, g * PAGE + t : (g + 1) * PAGE : PACK], ident[:])
+            c = sb([P, PACK], F32, "vs_cols%d" % g)
+            nc.scalar.copy(c[:], turned[:, :, 0])
+            vs_cols.append(c)
+
+        vw = sb([P, PAGES * DV], U32, "vw")
+        nc.vector.tensor_copy(vw[:], vw_pool[:].indirect(vcols[:]))
+        vsc = sb([P, PAGES * DV], U8, "vsc")
+        nc.vector.tensor_copy(vsc[:], vsc_pool[:].indirect(vcols[:]))
+
+        for u in range(Q_TILES):
+            sums = sb([P, PAGES], F32, "sums%d" % u)
+            weights = []
+            for g in range(PAGES):
+                p = sb([P, PACK, P], F32, "p%d_%d" % (u, g))
+                nc.scalar.activation(p[:], down[u, g][:], ACT.Exp, bias=low[u, PAGES - 1][:], scale=-1.0, accum_out=sums[:, g : g + 1])
+                turned = psum.tile([P, PACK, P], F32, name="turned", tag="turn", bufs=2)
+                for t in range(PACK):
+                    nc.tensor.transpose(turned[:, t, :], p[:, t, :], ident[:])
+                w = sb([P, P, PACK], BF16, "w%d_%d" % (u, g))
+                nc.vector.tensor_tensor(
+                    w[:],
+                    turned[:].rearrange("s t q -> s q t"),
+                    vs_cols[g][:].unsqueeze(1).to_broadcast([P, P, PACK]),
+                    ALU.mult,
+                )
+                weights.append(w)
+            y = psum.tile([P, DV], F32, name="y", tag="y", bufs=1)
+            for g in range(PAGES):
+                codes = sb([P, P], U32, "codes%d_%d" % (u, g))
+                scales = sb([P, P], U8, "scales%d_%d" % (u, g))
+                nc.vector.quantize_mx(out=codes[:].bitcast(FP8X4), scales=scales[:], in_=weights[g][:].rearrange("s q t -> s (q t)"))
+                nc.tensor.matmul_mx(
+                    out=y[:],
+                    lhsT=codes[:].bitcast(FP8X4),
+                    lhsT_scale=scales[:],
+                    rhs=vw[:, g * DV : (g + 1) * DV].bitcast(FP8X4),
+                    rhs_scale=vsc[:, g * DV : (g + 1) * DV],
+                    start=(g == 0),
+                    stop=(g == PAGES - 1),
+                )
+            total = sb([P, 1], F32, "total%d" % u)
+            nc.vector.tensor_reduce(total[:], sums[:], mybir.AxisListType.X, ALU.add)
+            inverse = sb([P, 1], F32, "inverse%d" % u)
+            nc.vector.reciprocal(inverse[:], total[:])
+            result = sb([P, DV], F32, "result%d" % u)
+            nc.scalar.activation(result[:], y[:], ACT.Copy, scale=inverse[:])
+            nc.sync.dma_start(out[0, u * P : (u + 1) * P, :], result[:])

@@ -50,35 +50,36 @@ def tile_attend_pkv8q_soft_draft_kernel(
         nc.sync.dma_start(vcols[:], voffs)
 
         ks_pool = keep.tile([P, T], U8, name="ks_pool", tag="ks_then_vs", align_bytes=64)
-        nc.vector.memset(ks_pool[:].bitcast(I32), 0)
+        nc.gpsimd.memset(ks_pool[:].bitcast(I32), 0)
         for quad in range(4):
             nc.sync.dma_start(scale_rows(ks_pool, quad), k_scales[0, 4 * quad : 4 * quad + 4, :].bitcast(I32))
 
+        qs = sb([P, NQ], U8, "qs")
+        nc.gpsimd.memset(qs[:].bitcast(I32), 0)
+        for quad in range(4):
+            nc.sync.dma_start(scale_rows(qs, quad), q_scales[0, 0, 4 * quad : 4 * quad + 4, :].bitcast(I32))
+
+        pos_pool = keep.tile([P, T], F32, name="pos_pool", tag="pos_then_vw", align_bytes=64)
+        nc.gpsimd.memset(pos_pool[:], 0.0)
+        nc.sync.dma_start(pos_pool[0:1, :], pos[0:1, :])
+
         warm_in = keep.tile([P, 1], F32, name="warm_in", tag="warm_then_kw", align_bytes=64)
-        nc.vector.memset(warm_in[:], 0.0)
+        nc.gpsimd.memset(warm_in[:], 0.0)
         warm_out = sb([P, 1], F32, "warm_out")
         nc.scalar.activation(warm_out[:], warm_in[:], ACT.Exp)
         kw_pool = keep.tile([P, T], U32, name="kw_pool", tag="warm_then_kw", align_bytes=64)
         nc.sync.dma_start(kw_pool[:].bitcast(I32), k_words[0].rearrange("g t r -> g (t r)").bitcast(I32))
 
-        pos_pool = keep.tile([P, T], F32, name="pos_pool", tag="pos_then_vw", align_bytes=64)
-        nc.vector.memset(pos_pool[:], 0.0)
-        nc.scalar.dma_start(pos_pool[0:1, :], pos[0:1, :])
+        ident = sb([P, P], F32, "ident")
+        make_identity(nc, ident[:])
 
-        qs = sb([P, NQ], U8, "qs")
-        nc.vector.memset(qs[:].bitcast(I32), 0)
-        for quad in range(4):
-            nc.sync.dma_start(scale_rows(qs, quad), q_scales[0, 0, 4 * quad : 4 * quad + 4, :].bitcast(I32))
         vsc_pool = sb([P, POOL_PAGES * DV], U8, "vsc_pool")
-        nc.vector.memset(vsc_pool[:].bitcast(I32), 0)
+        nc.gpsimd.memset(vsc_pool[:].bitcast(I32), 0)
         for quad in range(4):
             nc.sync.dma_start(
                 scale_rows(vsc_pool, quad).rearrange("f (u e) -> f u e", u=POOL_PAGES),
                 v_scales[:, 4 * quad : 4 * quad + 4, :].rearrange("u f e -> f u e").bitcast(I32),
             )
-
-        ident = sb([P, P], F32, "ident")
-        make_identity(nc, ident[:])
 
         def page_slots(g):
             return slots[:, g * PAGE // 16 : (g + 1) * PAGE // 16]
@@ -136,7 +137,7 @@ def tile_attend_pkv8q_soft_draft_kernel(
         low = {}
         for g in range(PAGES):
             for u in range(Q_TILES):
-                x = psum.tile([P, PAGE], F32, name="x", tag="x", bufs=3)
+                x = psum.tile([P, PAGE], F32, name="x", tag="x", bufs=4)
                 for j in range(PACK):
                     cols = slice(u * P, (u + 1) * P)
                     nc.tensor.matmul(x[:, j * P : (j + 1) * P], hidden[PACK * g + j][:, cols], ident[:], start=True, stop=False, is_transpose=True)
@@ -155,7 +156,7 @@ def tile_attend_pkv8q_soft_draft_kernel(
 
         vs_cols = []
         for g in range(PAGES):
-            turned = psum.tile([P, PACK, P], F32, name="turned", tag="turn", bufs=2)
+            turned = psum.tile([P, PACK, P], F32, name="turned", tag="x", bufs=4)
             for t in range(PACK):
                 nc.tensor.transpose(turned[:, t, :], vs_row[:, g * PAGE + t : (g + 1) * PAGE : PACK], ident[:])
             c = sb([P, PACK], F32, "vs_cols%d" % g)
@@ -184,7 +185,7 @@ def tile_attend_pkv8q_soft_draft_kernel(
                     ALU.mult,
                 )
                 weights.append(w)
-            y = psum.tile([P, DV], F32, name="y", tag="y", bufs=1)
+            y = psum.tile([P, DV], F32, name="y", tag="a", bufs=2)
             for g in range(PAGES):
                 codes = sb([P, P], U32, "codes%d_%d" % (u, g))
                 scales = sb([P, P], U8, "scales%d_%d" % (u, g))

@@ -42,37 +42,40 @@ def tile_attend_pkv8q_soft_draft_kernel(
 
         slots = keep.tile([P, N // 16], U16, name="slots")
         nc.sync.dma_start(slots[:], offs)
-        qw = sb([P, NQ], U32, "qw")
-        nc.sync.dma_start(qw[:].bitcast(I32), q_words[0, 0].rearrange("g q r -> g (q r)").bitcast(I32))
-        qpos_rows = sb([P, NQ], F32, "qpos_rows")
-        nc.sync.dma_start(qpos_rows[:], qpos[0].rearrange("q o -> (q o)").partition_broadcast(P))
         vcols = keep.tile([P, PAGES * DV // 16], U16, name="vcols")
         nc.sync.dma_start(vcols[:], voffs)
+        vw_pool = sb([P, POOL_PAGES * DV], U32, "vw_pool")
+        nc.sync.dma_start(
+            vw_pool[:].bitcast(I32).rearrange("g (u e) -> g u e", e=DV),
+            v_words.rearrange("u g e r -> g u (e r)").bitcast(I32),
+        )
+
+        qw = sb([P, NQ], U32, "qw")
+        nc.sync.dma_start(qw[:].bitcast(I32), q_words[0, 0].rearrange("g q r -> g (q r)").bitcast(I32))
 
         ks_pool = keep.tile([P, T], U8, name="ks_pool", tag="ks_then_vs", align_bytes=64)
         nc.gpsimd.memset(ks_pool[:].bitcast(I32), 0)
         for quad in range(4):
             nc.sync.dma_start(scale_rows(ks_pool, quad), k_scales[0, 4 * quad : 4 * quad + 4, :].bitcast(I32))
 
-        qs = sb([P, NQ], U8, "qs")
-        nc.gpsimd.memset(qs[:].bitcast(I32), 0)
-        for quad in range(4):
-            nc.sync.dma_start(scale_rows(qs, quad), q_scales[0, 0, 4 * quad : 4 * quad + 4, :].bitcast(I32))
-
-        pos_pool = keep.tile([P, T], F32, name="pos_pool", tag="pos_then_vw", align_bytes=64)
-        nc.gpsimd.memset(pos_pool[:], 0.0)
-        nc.sync.dma_start(pos_pool[0:1, :], pos[0:1, :])
-
         warm_in = keep.tile([P, 1], F32, name="warm_in", tag="warm_then_kw", align_bytes=64)
         nc.gpsimd.memset(warm_in[:], 0.0)
-        warm_out = sb([P, 1], F32, "warm_out")
+        warm_out = keep.tile([P, 1], F32, name="warm_out", tag="warm_then_qpos", align_bytes=64)
         nc.scalar.activation(warm_out[:], warm_in[:], ACT.Exp)
         kw_pool = keep.tile([P, T], U32, name="kw_pool", tag="warm_then_kw", align_bytes=64)
         nc.sync.dma_start(kw_pool[:].bitcast(I32), k_words[0].rearrange("g t r -> g (t r)").bitcast(I32))
 
-        ident = sb([P, P], F32, "ident")
-        make_identity(nc, ident[:])
+        qpos_rows = keep.tile([P, NQ], F32, name="qpos_rows", tag="warm_then_qpos", align_bytes=64)
+        nc.sync.dma_start(qpos_rows[:], qpos[0].rearrange("q o -> (q o)").partition_broadcast(P))
 
+        pos_pool = sb([P, T], F32, "pos_pool")
+        nc.gpsimd.memset(pos_pool[:], 0.0)
+        nc.scalar.dma_start(pos_pool[0:1, :], pos[0:1, :])
+
+        qs = sb([P, NQ], U8, "qs")
+        nc.gpsimd.memset(qs[:].bitcast(I32), 0)
+        for quad in range(4):
+            nc.scalar.dma_start(scale_rows(qs, quad), q_scales[0, 0, 4 * quad : 4 * quad + 4, :].bitcast(I32))
         vsc_pool = sb([P, POOL_PAGES * DV], U8, "vsc_pool")
         nc.gpsimd.memset(vsc_pool[:].bitcast(I32), 0)
         for quad in range(4):
@@ -80,6 +83,12 @@ def tile_attend_pkv8q_soft_draft_kernel(
                 scale_rows(vsc_pool, quad).rearrange("f (u e) -> f u e", u=POOL_PAGES),
                 v_scales[:, 4 * quad : 4 * quad + 4, :].rearrange("u f e -> f u e").bitcast(I32),
             )
+
+        ident = sb([P, P], F32, "ident")
+        make_identity(nc, ident[:])
+
+        vw = sb([P, PAGES * DV], U32, "vw")
+        nc.vector.tensor_copy(vw[:], vw_pool[:].indirect(vcols[:]))
 
         def page_slots(g):
             return slots[:, g * PAGE // 16 : (g + 1) * PAGE // 16]
@@ -93,7 +102,7 @@ def tile_attend_pkv8q_soft_draft_kernel(
         for g in range(PAGES):
             pos_row = sb([P, PAGE], F32, "pos_row%d" % g)
             nc.vector.tensor_copy(pos_row[:], pos_pool[:].indirect(page_slots(g)))
-            turned = psum.tile([P, PACK, P], F32, name="turned", tag="turn", bufs=2)
+            turned = psum.tile([P, PACK, P], F32, name="turned", tag="early", bufs=2)
             for j in range(PACK):
                 nc.tensor.transpose(turned[:, j, :], pos_row[:, j * P : (j + 1) * P], ident[:])
             pos_cols = sb([P, PACK], F32, "pos_cols%d" % g)
@@ -103,18 +112,12 @@ def tile_attend_pkv8q_soft_draft_kernel(
                 nc.scalar.activation(r[:], qpos_rows[:], ACT.Relu, bias=pos_cols[:, j : j + 1], scale=-STEEP)
                 hidden.append(r)
 
-        vw_pool = keep.tile([P, POOL_PAGES * DV], U32, name="vw_pool", tag="pos_then_vw", align_bytes=64)
-        nc.sync.dma_start(
-            vw_pool[:].bitcast(I32).rearrange("g (u e) -> g u e", e=DV),
-            v_words.rearrange("u g e r -> g u (e r)").bitcast(I32),
-        )
-
         neg = []
         for g in range(PAGES):
             kw = sb([P, PAGE], U32, "kw%d" % g)
             nc.vector.tensor_copy(kw[:], kw_pool[:].indirect(page_slots(g)))
             for half in range(2):
-                a = psum.tile([P, 2, NQ], F32, name="a", tag="a", bufs=2)
+                a = psum.tile([P, 2, NQ], F32, name="a", tag="early", bufs=2)
                 for jj in range(2):
                     j = 2 * half + jj
                     nc.tensor.matmul_mx(
@@ -135,17 +138,21 @@ def tile_attend_pkv8q_soft_draft_kernel(
 
         down = {}
         low = {}
-        for g in range(PAGES):
-            for u in range(Q_TILES):
-                x = psum.tile([P, PAGE], F32, name="x", tag="x", bufs=4)
+        page_down = [
+            keep.tile([P, Q_TILES, PACK, P], F32, name="page_down", tag="down%d" % g if g else "ks_then_vs", align_bytes=64)
+            for g in range(PAGES)
+        ]
+        for u in range(Q_TILES):
+            for g in range(PAGES):
+                down[u, g] = page_down[g][:, u]
+                x = psum.tile([P, PAGE], F32, name="x", tag="early", bufs=2) if g == PAGES - 1 else psum.tile([P, PAGE], F32, name="x", tag="x", bufs=4)
                 for j in range(PACK):
                     cols = slice(u * P, (u + 1) * P)
                     nc.tensor.matmul(x[:, j * P : (j + 1) * P], hidden[PACK * g + j][:, cols], ident[:], start=True, stop=False, is_transpose=True)
                     nc.tensor.matmul(x[:, j * P : (j + 1) * P], neg[2 * g + j // 2][:, j % 2, cols], ident[:], start=False, stop=True, is_transpose=True)
-                down[u, g] = sb([P, PACK, P], F32, "down%d_%d" % (u, g))
                 low[u, g] = sb([P, 1], F32, "low%d_%d" % (u, g))
                 nc.vector.tensor_scalar(
-                    down[u, g][:],
+                    down[u, g],
                     x[:].rearrange("q (s t) -> q t s", t=PACK),
                     MASKED,
                     low[u, g - 1][:] if g else MASKED,
@@ -156,15 +163,13 @@ def tile_attend_pkv8q_soft_draft_kernel(
 
         vs_cols = []
         for g in range(PAGES):
-            turned = psum.tile([P, PACK, P], F32, name="turned", tag="x", bufs=4)
+            turned = psum.tile([P, PACK, P], F32, name="turned", tag="turn", bufs=2)
             for t in range(PACK):
                 nc.tensor.transpose(turned[:, t, :], vs_row[:, g * PAGE + t : (g + 1) * PAGE : PACK], ident[:])
             c = sb([P, PACK], F32, "vs_cols%d" % g)
             nc.scalar.copy(c[:], turned[:, :, 0])
             vs_cols.append(c)
 
-        vw = sb([P, PAGES * DV], U32, "vw")
-        nc.vector.tensor_copy(vw[:], vw_pool[:].indirect(vcols[:]))
         vsc = sb([P, PAGES * DV], U8, "vsc")
         nc.vector.tensor_copy(vsc[:], vsc_pool[:].indirect(vcols[:]))
 
@@ -173,7 +178,7 @@ def tile_attend_pkv8q_soft_draft_kernel(
             weights = []
             for g in range(PAGES):
                 p = sb([P, PACK, P], F32, "p%d_%d" % (u, g))
-                nc.scalar.activation(p[:], down[u, g][:], ACT.Exp, bias=low[u, PAGES - 1][:], scale=-1.0, accum_out=sums[:, g : g + 1])
+                nc.scalar.activation(p[:], down[u, g], ACT.Exp, bias=low[u, PAGES - 1][:], scale=-1.0, accum_out=sums[:, g : g + 1])
                 turned = psum.tile([P, PACK, P], F32, name="turned", tag="turn", bufs=2)
                 for t in range(PACK):
                     nc.tensor.transpose(turned[:, t, :], p[:, t, :], ident[:])
@@ -185,7 +190,7 @@ def tile_attend_pkv8q_soft_draft_kernel(
                     ALU.mult,
                 )
                 weights.append(w)
-            y = psum.tile([P, DV], F32, name="y", tag="a", bufs=2)
+            y = psum.tile([P, DV], F32, name="y", tag="x", bufs=4)
             for g in range(PAGES):
                 codes = sb([P, P], U32, "codes%d_%d" % (u, g))
                 scales = sb([P, P], U8, "scales%d_%d" % (u, g))

@@ -44,22 +44,17 @@ def tile_attend_pkv8q_soft_draft_kernel(
         nc.sync.dma_start(slots[:], offs)
         vcols = keep.tile([P, PAGES * DV // 16], U16, name="vcols")
         nc.sync.dma_start(vcols[:], voffs)
-        vw_pool = sb([P, POOL_PAGES * DV], U32, "vw_pool")
-        nc.sync.dma_start(
-            vw_pool[:].bitcast(I32).rearrange("g (u e) -> g u e", e=DV),
-            v_words.rearrange("u g e r -> g u (e r)").bitcast(I32),
-        )
 
         qw = sb([P, NQ], U32, "qw")
         nc.sync.dma_start(qw[:].bitcast(I32), q_words[0, 0].rearrange("g q r -> g (q r)").bitcast(I32))
 
         ks_pool = keep.tile([P, T], U8, name="ks_pool", tag="ks_then_vs", align_bytes=64)
-        nc.gpsimd.memset(ks_pool[:].bitcast(I32), 0)
+        nc.vector.memset(ks_pool[:].bitcast(I32), 0)
         for quad in range(4):
             nc.sync.dma_start(scale_rows(ks_pool, quad), k_scales[0, 4 * quad : 4 * quad + 4, :].bitcast(I32))
 
         warm_in = keep.tile([P, 1], F32, name="warm_in", tag="warm_then_kw", align_bytes=64)
-        nc.gpsimd.memset(warm_in[:], 0.0)
+        nc.vector.memset(warm_in[:], 0.0)
         warm_out = keep.tile([P, 1], F32, name="warm_out", tag="warm_then_qpos", align_bytes=64)
         nc.scalar.activation(warm_out[:], warm_in[:], ACT.Exp)
         kw_pool = keep.tile([P, T], U32, name="kw_pool", tag="warm_then_kw", align_bytes=64)
@@ -68,16 +63,16 @@ def tile_attend_pkv8q_soft_draft_kernel(
         qpos_rows = keep.tile([P, NQ], F32, name="qpos_rows", tag="warm_then_qpos", align_bytes=64)
         nc.sync.dma_start(qpos_rows[:], qpos[0].rearrange("q o -> (q o)").partition_broadcast(P))
 
-        pos_pool = sb([P, T], F32, "pos_pool")
-        nc.gpsimd.memset(pos_pool[:], 0.0)
+        pos_pool = keep.tile([P, T], F32, name="pos_pool", tag="pos_then_vw", align_bytes=64)
+        nc.vector.memset(pos_pool[:], 0.0)
         nc.scalar.dma_start(pos_pool[0:1, :], pos[0:1, :])
 
         qs = sb([P, NQ], U8, "qs")
-        nc.gpsimd.memset(qs[:].bitcast(I32), 0)
+        nc.vector.memset(qs[:].bitcast(I32), 0)
         for quad in range(4):
             nc.scalar.dma_start(scale_rows(qs, quad), q_scales[0, 0, 4 * quad : 4 * quad + 4, :].bitcast(I32))
         vsc_pool = sb([P, POOL_PAGES * DV], U8, "vsc_pool")
-        nc.gpsimd.memset(vsc_pool[:].bitcast(I32), 0)
+        nc.vector.memset(vsc_pool[:].bitcast(I32), 0)
         for quad in range(4):
             nc.sync.dma_start(
                 scale_rows(vsc_pool, quad).rearrange("f (u e) -> f u e", u=POOL_PAGES),
@@ -86,9 +81,6 @@ def tile_attend_pkv8q_soft_draft_kernel(
 
         ident = sb([P, P], F32, "ident")
         make_identity(nc, ident[:])
-
-        vw = sb([P, PAGES * DV], U32, "vw")
-        nc.vector.tensor_copy(vw[:], vw_pool[:].indirect(vcols[:]))
 
         def page_slots(g):
             return slots[:, g * PAGE // 16 : (g + 1) * PAGE // 16]
@@ -112,6 +104,12 @@ def tile_attend_pkv8q_soft_draft_kernel(
                 nc.scalar.activation(r[:], qpos_rows[:], ACT.Relu, bias=pos_cols[:, j : j + 1], scale=-STEEP)
                 hidden.append(r)
 
+        vw_pool = keep.tile([P, POOL_PAGES * DV], U32, name="vw_pool", tag="pos_then_vw", align_bytes=64)
+        nc.sync.dma_start(
+            vw_pool[:].bitcast(I32).rearrange("g (u e) -> g u e", e=DV),
+            v_words.rearrange("u g e r -> g u (e r)").bitcast(I32),
+        )
+
         neg = []
         for g in range(PAGES):
             kw = sb([P, PAGE], U32, "kw%d" % g)
@@ -133,8 +131,13 @@ def tile_attend_pkv8q_soft_draft_kernel(
                 nc.scalar.activation(na[:], a[:], ACT.Copy, scale=-1.0)
                 neg.append(na)
 
-        vs_row = sb([P, N], F32, "vs_row")
-        nc.vector.tensor_copy(vs_row[:], vs_pool[:].indirect(slots[:]))
+        vs_cols = []
+        for g in range(PAGES):
+            vs_row = sb([P, PAGE], F32, "vs_row%d" % g)
+            nc.vector.tensor_copy(vs_row[:], vs_pool[:].indirect(page_slots(g)))
+            c = sb([P, PACK], F32, "vs_cols%d" % g)
+            nc.sync.dma_start(c[:], vs_row[0:1, :])
+            vs_cols.append(c)
 
         down = {}
         low = {}
@@ -161,15 +164,8 @@ def tile_attend_pkv8q_soft_draft_kernel(
                     accum_out=low[u, g][:],
                 )
 
-        vs_cols = []
-        for g in range(PAGES):
-            turned = psum.tile([P, PACK, P], F32, name="turned", tag="turn", bufs=2)
-            for t in range(PACK):
-                nc.tensor.transpose(turned[:, t, :], vs_row[:, g * PAGE + t : (g + 1) * PAGE : PACK], ident[:])
-            c = sb([P, PACK], F32, "vs_cols%d" % g)
-            nc.scalar.copy(c[:], turned[:, :, 0])
-            vs_cols.append(c)
-
+        vw = sb([P, PAGES * DV], U32, "vw")
+        nc.vector.tensor_copy(vw[:], vw_pool[:].indirect(vcols[:]))
         vsc = sb([P, PAGES * DV], U8, "vsc")
         nc.vector.tensor_copy(vsc[:], vsc_pool[:].indirect(vcols[:]))
 

@@ -1,7 +1,6 @@
 from contextlib import ExitStack
 
 import concourse.mybir as mybir
-from concourse.masks import make_identity
 
 N, T, D, DV, NQ = 1536, 4096, 512, 128, 256
 PAGE = 512
@@ -10,6 +9,7 @@ PACK = 4
 PAGES = N // PAGE
 POOL_PAGES = T // PAGE
 Q_TILES = NQ // P
+ROW = P - 1
 MASKED = 30000.0
 STEEP = 2.0 ** 80
 
@@ -32,45 +32,49 @@ def tile_attend_pkv8q_soft_draft_kernel(
     nc = tc.nc
     with ExitStack() as ctx:
         keep = ctx.enter_context(tc.tile_pool(name="keep", bufs=1))
+        shared = ctx.enter_context(tc.tile_pool(name="shared", bufs=1))
         psum = ctx.enter_context(tc.psum_pool(name="psum", bufs=1))
 
-        def sb(shape, dtype, name):
-            return keep.tile(shape, dtype, name=name, align_bytes=64)
+        def sb(shape, dtype, name, tag=""):
+            return keep.tile(shape, dtype, name=name, tag=tag or name, align_bytes=64)
+
+        def bank(shape, name, tag):
+            return psum.tile(shape, F32, name=name, tag=tag, bufs=6 if tag == "wide" else 2)
 
         def scale_rows(plane, quad):
             return plane[32 * quad : 32 * quad + 4, :].bitcast(I32)
 
         slots = keep.tile([P, N // 16], U16, name="slots")
         nc.sync.dma_start(slots[:], offs)
-        vcols = keep.tile([P, PAGES * DV // 16], U16, name="vcols")
-        nc.sync.dma_start(vcols[:], voffs)
 
-        qw = sb([P, NQ], U32, "qw")
-        nc.sync.dma_start(qw[:].bitcast(I32), q_words[0, 0].rearrange("g q r -> g (q r)").bitcast(I32))
-
-        ks_pool = keep.tile([P, T], U8, name="ks_pool", tag="ks_then_vs", align_bytes=64)
+        ks_pool = sb([P, T], U8, "ks_pool", "ks_then_vw")
         nc.vector.memset(ks_pool[:].bitcast(I32), 0)
+        qs = sb([P, NQ], U8, "qs")
+        nc.vector.memset(qs[:].bitcast(I32), 0)
+        pos_pool = shared.tile([P, T], F32, name="pos_pool", offset=0, align_bytes=64)
+        nc.vector.memset(pos_pool[0:ROW, :], 0.0)
+        nc.sync.dma_start(pos_pool[ROW:P, :], pos[0:1, :])
         for quad in range(4):
             nc.sync.dma_start(scale_rows(ks_pool, quad), k_scales[0, 4 * quad : 4 * quad + 4, :].bitcast(I32))
 
-        warm_in = keep.tile([P, 1], F32, name="warm_in", tag="warm_then_kw", align_bytes=64)
-        nc.vector.memset(warm_in[:], 0.0)
-        warm_out = keep.tile([P, 1], F32, name="warm_out", tag="warm_then_qpos", align_bytes=64)
-        nc.scalar.activation(warm_out[:], warm_in[:], ACT.Exp)
-        kw_pool = keep.tile([P, T], U32, name="kw_pool", tag="warm_then_kw", align_bytes=64)
+        zeros = sb([P, P], F32, "zeros", "zeros_then_kw")
+        nc.gpsimd.memset(zeros[:], 0.0)
+        ident = sb([P, P], F32, "ident")
+        nc.gpsimd.affine_select(
+            out=ident[:], in_=zeros[:], compare_op=ALU.not_equal, fill=1.0, base=0, pattern=[[-1, P]], channel_multiplier=1
+        )
+        kw_pool = sb([P, T], U32, "kw_pool", "zeros_then_kw")
         nc.sync.dma_start(kw_pool[:].bitcast(I32), k_words[0].rearrange("g t r -> g (t r)").bitcast(I32))
 
-        qpos_rows = keep.tile([P, NQ], F32, name="qpos_rows", tag="warm_then_qpos", align_bytes=64)
-        nc.sync.dma_start(qpos_rows[:], qpos[0].rearrange("q o -> (q o)").partition_broadcast(P))
-
-        pos_pool = keep.tile([P, T], F32, name="pos_pool", tag="pos_then_vw", align_bytes=64)
-        nc.vector.memset(pos_pool[:], 0.0)
-        nc.scalar.dma_start(pos_pool[0:1, :], pos[0:1, :])
-
-        qs = sb([P, NQ], U8, "qs")
-        nc.vector.memset(qs[:].bitcast(I32), 0)
+        qpos_cols = sb([P, Q_TILES], F32, "qpos_cols")
+        nc.scalar.dma_start(qpos_cols[:], qpos[0].rearrange("(p e) o -> p (e o)", e=Q_TILES))
+        qw = sb([P, NQ], U32, "qw")
+        nc.scalar.dma_start(qw[:].bitcast(I32), q_words[0, 0].rearrange("g q r -> g (q r)").bitcast(I32))
         for quad in range(4):
             nc.scalar.dma_start(scale_rows(qs, quad), q_scales[0, 0, 4 * quad : 4 * quad + 4, :].bitcast(I32))
+
+        vcols = keep.tile([P, PAGES * DV // 16], U16, name="vcols")
+        nc.sync.dma_start(vcols[:], voffs)
         vsc_pool = sb([P, POOL_PAGES * DV], U8, "vsc_pool")
         nc.vector.memset(vsc_pool[:].bitcast(I32), 0)
         for quad in range(4):
@@ -79,43 +83,54 @@ def tile_attend_pkv8q_soft_draft_kernel(
                 v_scales[:, 4 * quad : 4 * quad + 4, :].rearrange("u f e -> f u e").bitcast(I32),
             )
 
-        ident = sb([P, P], F32, "ident")
-        make_identity(nc, ident[:])
-
         def page_slots(g):
             return slots[:, g * PAGE // 16 : (g + 1) * PAGE // 16]
 
-        ks = sb([P, N], U8, "ks")
-        nc.vector.tensor_copy(ks[:], ks_pool[:].indirect(slots[:]))
-        vs_pool = keep.tile([P, T], F32, name="vs_pool", tag="ks_then_vs", align_bytes=64)
-        nc.sync.dma_start(vs_pool[:], vs)
+        spread = bank([P, Q_TILES, P], "spread", "early")
+        for e in range(Q_TILES):
+            nc.tensor.transpose(spread[:, e, :], qpos_cols[:, e : e + 1].to_broadcast([P, P]), ident[:])
+        qpos_rows = sb([P, P, Q_TILES], F32, "qpos_rows")
+        nc.scalar.activation(qpos_rows[:], spread[:].rearrange("s e p -> s p e"), ACT.Copy)
 
-        hidden = []
+        x = {}
         for g in range(PAGES):
             pos_row = sb([P, PAGE], F32, "pos_row%d" % g)
             nc.vector.tensor_copy(pos_row[:], pos_pool[:].indirect(page_slots(g)))
-            turned = psum.tile([P, PACK, P], F32, name="turned", tag="early", bufs=2)
+            turned = bank([P, PACK, P], "turned", "early")
             for j in range(PACK):
                 nc.tensor.transpose(turned[:, j, :], pos_row[:, j * P : (j + 1) * P], ident[:])
             pos_cols = sb([P, PACK], F32, "pos_cols%d" % g)
-            nc.scalar.activation(pos_cols[:], turned[:, :, 0], ACT.Copy, scale=STEEP)
+            nc.scalar.activation(pos_cols[:], turned[:, :, ROW], ACT.Copy, scale=STEEP)
+            hidden = sb([P, PACK, NQ], F32, "hidden%d" % g)
             for j in range(PACK):
-                r = sb([P, NQ], F32, "hidden%d_%d" % (g, j))
-                nc.scalar.activation(r[:], qpos_rows[:], ACT.Relu, bias=pos_cols[:, j : j + 1], scale=-STEEP)
-                hidden.append(r)
+                nc.scalar.activation(
+                    hidden[:, j, :], qpos_rows[:].rearrange("s p e -> s (p e)"), ACT.Relu, bias=pos_cols[:, j : j + 1], scale=-STEEP
+                )
+            for u in range(Q_TILES):
+                x[u, g] = bank([P, PAGE], "x", "wide")
+            for j in range(PACK):
+                for u in range(Q_TILES):
+                    nc.tensor.matmul(
+                        x[u, g][:, j * P : (j + 1) * P], hidden[:, j, u * P : (u + 1) * P], ident[:],
+                        start=(j == 0), stop=False, is_transpose=True,
+                    )
 
-        vw_pool = keep.tile([P, POOL_PAGES * DV], U32, name="vw_pool", tag="pos_then_vw", align_bytes=64)
+        vs_pool = shared.tile([P, T], F32, name="vs_pool", offset=N, align_bytes=64)
+        nc.sync.dma_start(vs_pool[:], vs)
+
+        ks = shared.tile([P, N], U8, name="ks", offset=0, align_bytes=64)
+        nc.vector.tensor_copy(ks[:], ks_pool[:].indirect(slots[:]))
+        vw_pool = sb([P, POOL_PAGES * DV], U32, "vw_pool", "ks_then_vw")
         nc.sync.dma_start(
             vw_pool[:].bitcast(I32).rearrange("g (u e) -> g u e", e=DV),
             v_words.rearrange("u g e r -> g u (e r)").bitcast(I32),
         )
 
-        neg = []
         for g in range(PAGES):
             kw = sb([P, PAGE], U32, "kw%d" % g)
             nc.vector.tensor_copy(kw[:], kw_pool[:].indirect(page_slots(g)))
             for half in range(2):
-                a = psum.tile([P, 2, NQ], F32, name="a", tag="early", bufs=2)
+                a = bank([P, 2, NQ], "a", "early")
                 for jj in range(2):
                     j = 2 * half + jj
                     nc.tensor.matmul_mx(
@@ -127,9 +142,15 @@ def tile_attend_pkv8q_soft_draft_kernel(
                         start=True,
                         stop=True,
                     )
-                na = sb([P, 2, NQ], F32, "neg%d_%d" % (g, half))
-                nc.scalar.activation(na[:], a[:], ACT.Copy, scale=-1.0)
-                neg.append(na)
+                neg = sb([P, 2, NQ], F32, "neg%d_%d" % (g, half))
+                nc.scalar.activation(neg[:], a[:], ACT.Copy, scale=-1.0)
+                for u in range(Q_TILES):
+                    for jj in range(2):
+                        j = 2 * half + jj
+                        nc.tensor.matmul(
+                            x[u, g][:, j * P : (j + 1) * P], neg[:, jj, u * P : (u + 1) * P], ident[:],
+                            start=False, stop=(j == PACK - 1), is_transpose=True,
+                        )
 
         vs_cols = []
         for g in range(PAGES):
@@ -139,24 +160,14 @@ def tile_attend_pkv8q_soft_draft_kernel(
             nc.sync.dma_start(c[:], vs_row[0:1, :])
             vs_cols.append(c)
 
-        down = {}
+        down = shared.tile([P, Q_TILES, PAGES, PACK, P], F32, name="down", offset=N, align_bytes=64)
         low = {}
-        page_down = [
-            keep.tile([P, Q_TILES, PACK, P], F32, name="page_down", tag="down%d" % g if g else "ks_then_vs", align_bytes=64)
-            for g in range(PAGES)
-        ]
-        for u in range(Q_TILES):
-            for g in range(PAGES):
-                down[u, g] = page_down[g][:, u]
-                x = psum.tile([P, PAGE], F32, name="x", tag="early", bufs=2) if g == PAGES - 1 else psum.tile([P, PAGE], F32, name="x", tag="x", bufs=4)
-                for j in range(PACK):
-                    cols = slice(u * P, (u + 1) * P)
-                    nc.tensor.matmul(x[:, j * P : (j + 1) * P], hidden[PACK * g + j][:, cols], ident[:], start=True, stop=False, is_transpose=True)
-                    nc.tensor.matmul(x[:, j * P : (j + 1) * P], neg[2 * g + j // 2][:, j % 2, cols], ident[:], start=False, stop=True, is_transpose=True)
+        for g in range(PAGES):
+            for u in range(Q_TILES):
                 low[u, g] = sb([P, 1], F32, "low%d_%d" % (u, g))
                 nc.vector.tensor_scalar(
-                    down[u, g],
-                    x[:].rearrange("q (s t) -> q t s", t=PACK),
+                    down[:, u, g],
+                    x[u, g][:].rearrange("q (s t) -> q t s", t=PACK),
                     MASKED,
                     low[u, g - 1][:] if g else MASKED,
                     op0=ALU.min,
@@ -164,9 +175,9 @@ def tile_attend_pkv8q_soft_draft_kernel(
                     accum_out=low[u, g][:],
                 )
 
-        vw = sb([P, PAGES * DV], U32, "vw")
+        vw = shared.tile([P, PAGES * DV], U32, name="vw", offset=N + 8 * N, align_bytes=64)
         nc.vector.tensor_copy(vw[:], vw_pool[:].indirect(vcols[:]))
-        vsc = sb([P, PAGES * DV], U8, "vsc")
+        vsc = shared.tile([P, PAGES * DV], U8, name="vsc", offset=N + 9 * N, align_bytes=64)
         nc.vector.tensor_copy(vsc[:], vsc_pool[:].indirect(vcols[:]))
 
         for u in range(Q_TILES):
@@ -174,8 +185,8 @@ def tile_attend_pkv8q_soft_draft_kernel(
             weights = []
             for g in range(PAGES):
                 p = sb([P, PACK, P], F32, "p%d_%d" % (u, g))
-                nc.scalar.activation(p[:], down[u, g], ACT.Exp, bias=low[u, PAGES - 1][:], scale=-1.0, accum_out=sums[:, g : g + 1])
-                turned = psum.tile([P, PACK, P], F32, name="turned", tag="turn", bufs=2)
+                nc.scalar.activation(p[:], down[:, u, g], ACT.Exp, bias=low[u, PAGES - 1][:], scale=-1.0, accum_out=sums[:, g : g + 1])
+                turned = bank([P, PACK, P], "turned", "wide")
                 for t in range(PACK):
                     nc.tensor.transpose(turned[:, t, :], p[:, t, :], ident[:])
                 w = sb([P, P, PACK], BF16, "w%d_%d" % (u, g))
@@ -186,7 +197,7 @@ def tile_attend_pkv8q_soft_draft_kernel(
                     ALU.mult,
                 )
                 weights.append(w)
-            y = psum.tile([P, DV], F32, name="y", tag="x", bufs=4)
+            y = bank([P, DV], "y", "early")
             for g in range(PAGES):
                 codes = sb([P, P], U32, "codes%d_%d" % (u, g))
                 scales = sb([P, P], U8, "scales%d_%d" % (u, g))

@@ -10,6 +10,10 @@ PAGES = N // PAGE
 POOL_PAGES = T // PAGE
 Q_TILES = NQ // P
 ROW = P - 1
+QS_AT = 4 * T
+POS_AT = QS_AT + NQ
+VS_AT = POS_AT + N
+KS_AT = VS_AT + 4 * T
 MASKED = 30000.0
 STEEP = 2.0 ** 80
 
@@ -47,23 +51,23 @@ def tile_attend_pkv8q_soft_draft_kernel(
         slots = keep.tile([P, N // 16], U16, name="slots")
         nc.sync.dma_start(slots[:], offs)
 
-        ks_pool = sb([P, T], U8, "ks_pool", "ks_then_vw")
+        ks_pool = shared.tile([P, T], U8, name="ks_pool", offset=KS_AT, align_bytes=64)
         nc.vector.memset(ks_pool[:].bitcast(I32), 0)
-        qs = sb([P, NQ], U8, "qs")
-        nc.vector.memset(qs[:].bitcast(I32), 0)
-        pos_pool = shared.tile([P, T], F32, name="pos_pool", offset=0, align_bytes=64)
-        nc.vector.memset(pos_pool[0:ROW, :], 0.0)
-        nc.sync.dma_start(pos_pool[ROW:P, :], pos[0:1, :])
-        for quad in range(4):
-            nc.sync.dma_start(scale_rows(ks_pool, quad), k_scales[0, 4 * quad : 4 * quad + 4, :].bitcast(I32))
-
-        zeros = sb([P, P], F32, "zeros", "zeros_then_kw")
-        nc.gpsimd.memset(zeros[:], 0.0)
+        zeros = shared.tile([P, P], F32, name="zeros", offset=QS_AT - P, align_bytes=64)
+        nc.vector.memset(zeros[:], 0.0)
         ident = sb([P, P], F32, "ident")
         nc.gpsimd.affine_select(
             out=ident[:], in_=zeros[:], compare_op=ALU.not_equal, fill=1.0, base=0, pattern=[[-1, P]], channel_multiplier=1
         )
-        kw_pool = sb([P, T], U32, "kw_pool", "zeros_then_kw")
+        pos_pool = shared.tile([P, T], F32, name="pos_pool", offset=POS_AT, align_bytes=64)
+        nc.vector.memset(pos_pool[0:ROW, :], 0.0)
+        nc.sync.dma_start(pos_pool[ROW:P, :], pos[0:1, :])
+        qs = shared.tile([P, NQ], U8, name="qs", offset=QS_AT, align_bytes=64)
+        nc.vector.memset(qs[:].bitcast(I32), 0)
+        for quad in range(4):
+            nc.sync.dma_start(scale_rows(ks_pool, quad), k_scales[0, 4 * quad : 4 * quad + 4, :].bitcast(I32))
+
+        kw_pool = shared.tile([P, T], U32, name="kw_pool", offset=0, align_bytes=64)
         nc.sync.dma_start(kw_pool[:].bitcast(I32), k_words[0].rearrange("g t r -> g (t r)").bitcast(I32))
 
         qpos_cols = sb([P, Q_TILES], F32, "qpos_cols")
@@ -71,18 +75,10 @@ def tile_attend_pkv8q_soft_draft_kernel(
         qw = sb([P, NQ], U32, "qw")
         nc.scalar.dma_start(qw[:].bitcast(I32), q_words[0, 0].rearrange("g q r -> g (q r)").bitcast(I32))
         for quad in range(4):
-            nc.scalar.dma_start(scale_rows(qs, quad), q_scales[0, 0, 4 * quad : 4 * quad + 4, :].bitcast(I32))
+            nc.sync.dma_start(scale_rows(qs, quad), q_scales[0, 0, 4 * quad : 4 * quad + 4, :].bitcast(I32))
 
         vcols = keep.tile([P, PAGES * DV // 16], U16, name="vcols")
         nc.sync.dma_start(vcols[:], voffs)
-        vsc_pool = sb([P, POOL_PAGES * DV], U8, "vsc_pool")
-        nc.vector.memset(vsc_pool[:].bitcast(I32), 0)
-        for quad in range(4):
-            nc.sync.dma_start(
-                scale_rows(vsc_pool, quad).rearrange("f (u e) -> f u e", u=POOL_PAGES),
-                v_scales[:, 4 * quad : 4 * quad + 4, :].rearrange("u f e -> f u e").bitcast(I32),
-            )
-
         def page_slots(g):
             return slots[:, g * PAGE // 16 : (g + 1) * PAGE // 16]
 
@@ -115,16 +111,24 @@ def tile_attend_pkv8q_soft_draft_kernel(
                         start=(j == 0), stop=False, is_transpose=True,
                     )
 
-        vs_pool = shared.tile([P, T], F32, name="vs_pool", offset=N, align_bytes=64)
+        vs_pool = shared.tile([P, T], F32, name="vs_pool", offset=VS_AT, align_bytes=64)
         nc.sync.dma_start(vs_pool[:], vs)
 
-        ks = shared.tile([P, N], U8, name="ks", offset=0, align_bytes=64)
+        ks = shared.tile([P, N], U8, name="ks", offset=POS_AT, align_bytes=64)
         nc.vector.tensor_copy(ks[:], ks_pool[:].indirect(slots[:]))
-        vw_pool = sb([P, POOL_PAGES * DV], U32, "vw_pool", "ks_then_vw")
+        vw_pool = shared.tile([P, POOL_PAGES * DV], U32, name="vw_pool", offset=KS_AT + POOL_PAGES * DV, align_bytes=64)
         nc.sync.dma_start(
             vw_pool[:].bitcast(I32).rearrange("g (u e) -> g u e", e=DV),
             v_words.rearrange("u g e r -> g u (e r)").bitcast(I32),
         )
+
+        vsc_pool = shared.tile([P, POOL_PAGES * DV], U8, name="vsc_pool", offset=KS_AT, align_bytes=64)
+        nc.gpsimd.memset(vsc_pool[:].bitcast(I32), 0)
+        for quad in range(4):
+            nc.sync.dma_start(
+                scale_rows(vsc_pool, quad).rearrange("f (u e) -> f u e", u=POOL_PAGES),
+                v_scales[:, 4 * quad : 4 * quad + 4, :].rearrange("u f e -> f u e").bitcast(I32),
+            )
 
         for g in range(PAGES):
             kw = sb([P, PAGE], U32, "kw%d" % g)
@@ -160,7 +164,7 @@ def tile_attend_pkv8q_soft_draft_kernel(
             nc.sync.dma_start(c[:], vs_row[0:1, :])
             vs_cols.append(c)
 
-        down = shared.tile([P, Q_TILES, PAGES, PACK, P], F32, name="down", offset=N, align_bytes=64)
+        down = shared.tile([P, Q_TILES, PAGES, PACK, P], F32, name="down", offset=VS_AT, align_bytes=64)
         low = {}
         for g in range(PAGES):
             for u in range(Q_TILES):
@@ -175,9 +179,9 @@ def tile_attend_pkv8q_soft_draft_kernel(
                     accum_out=low[u, g][:],
                 )
 
-        vw = shared.tile([P, PAGES * DV], U32, name="vw", offset=N + 8 * N, align_bytes=64)
+        vw = shared.tile([P, PAGES * DV], U32, name="vw", offset=VS_AT + 8 * N, align_bytes=64)
         nc.vector.tensor_copy(vw[:], vw_pool[:].indirect(vcols[:]))
-        vsc = shared.tile([P, PAGES * DV], U8, name="vsc", offset=N + 9 * N, align_bytes=64)
+        vsc = shared.tile([P, PAGES * DV], U8, name="vsc", offset=VS_AT + 9 * N, align_bytes=64)
         nc.vector.tensor_copy(vsc[:], vsc_pool[:].indirect(vcols[:]))
 
         for u in range(Q_TILES):

@@ -42,36 +42,43 @@ def tile_attend_pkv8q_soft_draft_kernel(
         def sb(shape, dtype, name, tag=""):
             return keep.tile(shape, dtype, name=name, tag=tag or name, align_bytes=64)
 
+        def placed(shape, dtype, name, offset):
+            return shared.tile(shape, dtype, name=name, offset=offset, align_bytes=64)
+
         def bank(shape, name, tag):
             return psum.tile(shape, F32, name=name, tag=tag, bufs=6 if tag == "wide" else 2)
 
         def scale_rows(plane, quad):
             return plane[32 * quad : 32 * quad + 4, :].bitcast(I32)
 
+        def page_slots(g):
+            return slots[:, g * PAGE // 16 : (g + 1) * PAGE // 16]
+
         slots = keep.tile([P, N // 16], U16, name="slots")
         nc.sync.dma_start(slots[:], offs)
 
-        ks_pool = shared.tile([P, T], U8, name="ks_pool", offset=KS_AT, align_bytes=64)
+        ks_pool = placed([P, T], U8, "ks_pool", KS_AT)
         nc.vector.memset(ks_pool[:].bitcast(I32), 0)
-        zeros = shared.tile([P, P], F32, name="zeros", offset=QS_AT - P, align_bytes=64)
+        zeros = placed([P, P], F32, "zeros", QS_AT - P)
         nc.vector.memset(zeros[:], 0.0)
         ident = sb([P, P], F32, "ident")
         nc.gpsimd.affine_select(
             out=ident[:], in_=zeros[:], compare_op=ALU.not_equal, fill=1.0, base=0, pattern=[[-1, P]], channel_multiplier=1
         )
-        pos_pool = shared.tile([P, T], F32, name="pos_pool", offset=POS_AT, align_bytes=64)
+        pos_pool = placed([P, T], F32, "pos_pool", POS_AT)
         nc.vector.memset(pos_pool[0:ROW, :], 0.0)
         nc.sync.dma_start(pos_pool[ROW:P, :], pos[0:1, :])
-        qs = shared.tile([P, NQ], U8, name="qs", offset=QS_AT, align_bytes=64)
+        qs = placed([P, NQ], U8, "qs", QS_AT)
         nc.vector.memset(qs[:].bitcast(I32), 0)
         for quad in range(4):
             nc.sync.dma_start(scale_rows(ks_pool, quad), k_scales[0, 4 * quad : 4 * quad + 4, :].bitcast(I32))
 
-        kw_pool = shared.tile([P, T], U32, name="kw_pool", offset=0, align_bytes=64)
+        kw_pool = placed([P, T], U32, "kw_pool", 0)
         nc.sync.dma_start(kw_pool[:].bitcast(I32), k_words[0].rearrange("g t r -> g (t r)").bitcast(I32))
 
         qpos_cols = sb([P, Q_TILES], F32, "qpos_cols")
-        nc.scalar.dma_start(qpos_cols[:], qpos[0].rearrange("(p e) o -> p (e o)", e=Q_TILES))
+        with nc.allow_non_contiguous_dma(reason="one place a partition and query tile"):
+            nc.scalar.dma_start(qpos_cols[:], qpos[0].rearrange("(u p) o -> p (u o)", p=P))
         qw = sb([P, NQ], U32, "qw")
         nc.scalar.dma_start(qw[:].bitcast(I32), q_words[0, 0].rearrange("g q r -> g (q r)").bitcast(I32))
         for quad in range(4):
@@ -79,16 +86,11 @@ def tile_attend_pkv8q_soft_draft_kernel(
 
         vcols = keep.tile([P, PAGES * DV // 16], U16, name="vcols")
         nc.sync.dma_start(vcols[:], voffs)
-        def page_slots(g):
-            return slots[:, g * PAGE // 16 : (g + 1) * PAGE // 16]
 
-        spread = bank([P, Q_TILES, P], "spread", "early")
-        for e in range(Q_TILES):
-            nc.tensor.transpose(spread[:, e, :], qpos_cols[:, e : e + 1].to_broadcast([P, P]), ident[:])
-        qpos_rows = sb([P, P, Q_TILES], F32, "qpos_rows")
-        nc.scalar.activation(qpos_rows[:], spread[:].rearrange("s e p -> s p e"), ACT.Copy)
+        limit = sb([P, Q_TILES], F32, "limit")
+        nc.scalar.activation(limit[:], qpos_cols[:], ACT.Copy, scale=-STEEP)
 
-        x = {}
+        hidden = {}
         for g in range(PAGES):
             pos_row = sb([P, PAGE], F32, "pos_row%d" % g)
             nc.vector.tensor_copy(pos_row[:], pos_pool[:].indirect(page_slots(g)))
@@ -96,92 +98,72 @@ def tile_attend_pkv8q_soft_draft_kernel(
             for j in range(PACK):
                 nc.tensor.transpose(turned[:, j, :], pos_row[:, j * P : (j + 1) * P], ident[:])
             pos_cols = sb([P, PACK], F32, "pos_cols%d" % g)
-            nc.scalar.activation(pos_cols[:], turned[:, :, ROW], ACT.Copy, scale=STEEP)
-            hidden = sb([P, PACK, NQ], F32, "hidden%d" % g)
+            nc.scalar.activation(pos_cols[:], turned[:, :, ROW], ACT.Copy)
+            spread = bank([P, PAGE], "spread", "early")
             for j in range(PACK):
-                nc.scalar.activation(
-                    hidden[:, j, :], qpos_rows[:].rearrange("s p e -> s (p e)"), ACT.Relu, bias=pos_cols[:, j : j + 1], scale=-STEEP
-                )
+                nc.tensor.transpose(spread[:, j * P : (j + 1) * P], pos_cols[:, j : j + 1].to_broadcast([P, P]), ident[:])
             for u in range(Q_TILES):
-                x[u, g] = bank([P, PAGE], "x", "wide")
-            for j in range(PACK):
-                for u in range(Q_TILES):
-                    nc.tensor.matmul(
-                        x[u, g][:, j * P : (j + 1) * P], hidden[:, j, u * P : (u + 1) * P], ident[:],
-                        start=(j == 0), stop=False, is_transpose=True,
-                    )
+                hidden[u, g] = sb([P, PACK, P], F32, "hidden%d_%d" % (u, g))
+                nc.scalar.activation(
+                    hidden[u, g][:], spread[:].rearrange("q (s t) -> q t s", t=PACK), ACT.Relu, bias=limit[:, u : u + 1], scale=STEEP
+                )
 
-        vs_pool = shared.tile([P, T], F32, name="vs_pool", offset=VS_AT, align_bytes=64)
+        vs_pool = placed([P, T], F32, "vs_pool", VS_AT)
         nc.sync.dma_start(vs_pool[:], vs)
 
-        ks = shared.tile([P, N], U8, name="ks", offset=POS_AT, align_bytes=64)
+        ks = placed([P, N], U8, "ks", POS_AT)
         nc.vector.tensor_copy(ks[:], ks_pool[:].indirect(slots[:]))
-        vw_pool = shared.tile([P, POOL_PAGES * DV], U32, name="vw_pool", offset=KS_AT + POOL_PAGES * DV, align_bytes=64)
+        vw_pool = placed([P, POOL_PAGES * DV], U32, "vw_pool", KS_AT + POOL_PAGES * DV)
         nc.sync.dma_start(
             vw_pool[:].bitcast(I32).rearrange("g (u e) -> g u e", e=DV),
             v_words.rearrange("u g e r -> g u (e r)").bitcast(I32),
         )
-
-        vsc_pool = shared.tile([P, POOL_PAGES * DV], U8, name="vsc_pool", offset=KS_AT, align_bytes=64)
-        nc.gpsimd.memset(vsc_pool[:].bitcast(I32), 0)
+        vsc_pool = placed([P, POOL_PAGES * DV], U8, "vsc_pool", KS_AT)
+        nc.vector.memset(vsc_pool[:].bitcast(I32), 0)
         for quad in range(4):
             nc.sync.dma_start(
                 scale_rows(vsc_pool, quad).rearrange("f (u e) -> f u e", u=POOL_PAGES),
                 v_scales[:, 4 * quad : 4 * quad + 4, :].rearrange("u f e -> f u e").bitcast(I32),
             )
 
+        a = {}
         for g in range(PAGES):
             kw = sb([P, PAGE], U32, "kw%d" % g)
             nc.vector.tensor_copy(kw[:], kw_pool[:].indirect(page_slots(g)))
-            for half in range(2):
-                a = bank([P, 2, NQ], "a", "early")
-                for jj in range(2):
-                    j = 2 * half + jj
-                    nc.tensor.matmul_mx(
-                        out=a[:, jj, :],
-                        lhsT=kw[:, j * P : (j + 1) * P].bitcast(FP8X4),
-                        lhsT_scale=ks[:, g * PAGE + j * P : g * PAGE + (j + 1) * P],
-                        rhs=qw[:].bitcast(FP8X4),
-                        rhs_scale=qs[:],
-                        start=True,
-                        stop=True,
-                    )
-                neg = sb([P, 2, NQ], F32, "neg%d_%d" % (g, half))
-                nc.scalar.activation(neg[:], a[:], ACT.Copy, scale=-1.0)
-                for u in range(Q_TILES):
-                    for jj in range(2):
-                        j = 2 * half + jj
-                        nc.tensor.matmul(
-                            x[u, g][:, j * P : (j + 1) * P], neg[:, jj, u * P : (u + 1) * P], ident[:],
-                            start=False, stop=(j == PACK - 1), is_transpose=True,
-                        )
+            for u in range(Q_TILES):
+                a[u, g] = bank([P, PAGE], "a", "wide")
+                nc.tensor.matmul_mx(
+                    out=a[u, g][:],
+                    lhsT=qw[:, u * P : (u + 1) * P].bitcast(FP8X4),
+                    lhsT_scale=qs[:, u * P : (u + 1) * P],
+                    rhs=kw[:].bitcast(FP8X4),
+                    rhs_scale=ks[:, g * PAGE : (g + 1) * PAGE],
+                    start=True,
+                    stop=True,
+                )
 
+        down = []
+        low = []
         vs_cols = []
+        for u in range(Q_TILES):
+            x = placed([P, PAGES, PACK, P], F32, "x%d" % u, 4 * N * u)
+            for g in range(PAGES):
+                nc.vector.tensor_tensor(x[:, g], hidden[u, g][:], a[u, g][:].rearrange("q (s t) -> q t s", t=PACK), ALU.subtract)
+            down.append(sb([P, PAGES, PACK, P], F32, "down%d" % u))
+            low.append(sb([P, 1], F32, "low%d" % u))
+            nc.vector.tensor_scalar(down[u][:], x[:], MASKED, MASKED, op0=ALU.min, op1=ALU.min, accum_out=low[u][:])
+
+        vs_rows = placed([P, N], F32, "vs_rows", 4 * N)
         for g in range(PAGES):
-            vs_row = sb([P, PAGE], F32, "vs_row%d" % g)
-            nc.vector.tensor_copy(vs_row[:], vs_pool[:].indirect(page_slots(g)))
+            vs_row = vs_rows[:, g * PAGE : (g + 1) * PAGE]
+            nc.vector.tensor_copy(vs_row, vs_pool[:].indirect(page_slots(g)))
             c = sb([P, PACK], F32, "vs_cols%d" % g)
             nc.sync.dma_start(c[:], vs_row[0:1, :])
             vs_cols.append(c)
 
-        down = shared.tile([P, Q_TILES, PAGES, PACK, P], F32, name="down", offset=VS_AT, align_bytes=64)
-        low = {}
-        for g in range(PAGES):
-            for u in range(Q_TILES):
-                low[u, g] = sb([P, 1], F32, "low%d_%d" % (u, g))
-                nc.vector.tensor_scalar(
-                    down[:, u, g],
-                    x[u, g][:].rearrange("q (s t) -> q t s", t=PACK),
-                    MASKED,
-                    low[u, g - 1][:] if g else MASKED,
-                    op0=ALU.min,
-                    op1=ALU.min,
-                    accum_out=low[u, g][:],
-                )
-
-        vw = shared.tile([P, PAGES * DV], U32, name="vw", offset=VS_AT + 8 * N, align_bytes=64)
+        vw = placed([P, PAGES * DV], U32, "vw", VS_AT)
         nc.vector.tensor_copy(vw[:], vw_pool[:].indirect(vcols[:]))
-        vsc = shared.tile([P, PAGES * DV], U8, name="vsc", offset=VS_AT + 9 * N, align_bytes=64)
+        vsc = placed([P, PAGES * DV], U8, "vsc", VS_AT + N)
         nc.vector.tensor_copy(vsc[:], vsc_pool[:].indirect(vcols[:]))
 
         for u in range(Q_TILES):
@@ -189,7 +171,7 @@ def tile_attend_pkv8q_soft_draft_kernel(
             weights = []
             for g in range(PAGES):
                 p = sb([P, PACK, P], F32, "p%d_%d" % (u, g))
-                nc.scalar.activation(p[:], down[:, u, g], ACT.Exp, bias=low[u, PAGES - 1][:], scale=-1.0, accum_out=sums[:, g : g + 1])
+                nc.scalar.activation(p[:], down[u][:, g], ACT.Exp, bias=low[u][:], scale=-1.0, accum_out=sums[:, g : g + 1])
                 turned = bank([P, PACK, P], "turned", "wide")
                 for t in range(PACK):
                     nc.tensor.transpose(turned[:, t, :], p[:, t, :], ident[:])

@@ -1,6 +1,7 @@
 from contextlib import ExitStack
 
 import concourse.mybir as mybir
+from concourse.masks import make_identity
 
 N, T, D, DV, NQ = 1536, 4096, 512, 128, 256
 PAGE = 512
@@ -10,10 +11,11 @@ PAGES = N // PAGE
 POOL_PAGES = T // PAGE
 Q_TILES = NQ // P
 ROW = P - 1
-QS_AT = 4 * T
-POS_AT = QS_AT + NQ
+POS_AT = 4 * T
 VS_AT = POS_AT + N
 KS_AT = VS_AT + 4 * T
+DIRECT_PAGES = [0]
+TURNED_PAGES = [1, 2]
 MASKED = 30000.0
 STEEP = 2.0 ** 80
 
@@ -56,57 +58,71 @@ def tile_attend_pkv8q_soft_draft_kernel(
 
         slots = keep.tile([P, N // 16], U16, name="slots")
         nc.sync.dma_start(slots[:], offs)
-
-        ks_pool = placed([P, T], U8, "ks_pool", KS_AT)
-        nc.vector.memset(ks_pool[:].bitcast(I32), 0)
-        zeros = placed([P, P], F32, "zeros", QS_AT - P)
-        nc.vector.memset(zeros[:], 0.0)
-        ident = sb([P, P], F32, "ident")
-        nc.gpsimd.affine_select(
-            out=ident[:], in_=zeros[:], compare_op=ALU.not_equal, fill=1.0, base=0, pattern=[[-1, P]], channel_multiplier=1
-        )
         pos_pool = placed([P, T], F32, "pos_pool", POS_AT)
-        nc.vector.memset(pos_pool[0:ROW, :], 0.0)
         nc.sync.dma_start(pos_pool[ROW:P, :], pos[0:1, :])
-        qs = placed([P, NQ], U8, "qs", QS_AT)
-        nc.vector.memset(qs[:].bitcast(I32), 0)
-        for quad in range(4):
-            nc.sync.dma_start(scale_rows(ks_pool, quad), k_scales[0, 4 * quad : 4 * quad + 4, :].bitcast(I32))
-
         kw_pool = placed([P, T], U32, "kw_pool", 0)
         nc.sync.dma_start(kw_pool[:].bitcast(I32), k_words[0].rearrange("g t r -> g (t r)").bitcast(I32))
+        vcols = keep.tile([P, PAGES * DV // 16], U16, name="vcols")
+        nc.sync.dma_start(vcols[:], voffs)
 
         qpos_cols = sb([P, Q_TILES], F32, "qpos_cols")
         with nc.allow_non_contiguous_dma(reason="one place a partition and query tile"):
             nc.scalar.dma_start(qpos_cols[:], qpos[0].rearrange("(u p) o -> p (u o)", p=P))
         qw = sb([P, NQ], U32, "qw")
         nc.scalar.dma_start(qw[:].bitcast(I32), q_words[0, 0].rearrange("g q r -> g (q r)").bitcast(I32))
+
+        ks_pool = placed([P, T], U8, "ks_pool", KS_AT)
+        nc.vector.memset(ks_pool[:].bitcast(I32), 0)
+        for quad in range(4):
+            nc.scalar.dma_start(scale_rows(ks_pool, quad), k_scales[0, 4 * quad : 4 * quad + 4, :].bitcast(I32))
+        nc.vector.memset(pos_pool[0:ROW, :], 0.0)
+        qs = sb([P, NQ], U8, "qs")
+        nc.vector.memset(qs[:].bitcast(I32), 0)
         for quad in range(4):
             nc.sync.dma_start(scale_rows(qs, quad), q_scales[0, 0, 4 * quad : 4 * quad + 4, :].bitcast(I32))
 
-        vcols = keep.tile([P, PAGES * DV // 16], U16, name="vcols")
-        nc.sync.dma_start(vcols[:], voffs)
+        ident = sb([P, P], F32, "ident")
+        make_identity(nc, ident[:])
 
         limit = sb([P, Q_TILES], F32, "limit")
         nc.scalar.activation(limit[:], qpos_cols[:], ACT.Copy, scale=-STEEP)
+        spread = bank([P, NQ], "spread", "early")
+        for u in range(Q_TILES):
+            nc.tensor.transpose(spread[:, u * P : (u + 1) * P], qpos_cols[:, u : u + 1].to_broadcast([P, P]), ident[:])
+        qpos_rows = sb([P, NQ], F32, "qpos_rows")
+        nc.scalar.activation(qpos_rows[:], spread[:], ACT.Copy)
 
         hidden = {}
-        for g in range(PAGES):
+        x = {}
+        for g in TURNED_PAGES + DIRECT_PAGES:
             pos_row = sb([P, PAGE], F32, "pos_row%d" % g)
             nc.vector.tensor_copy(pos_row[:], pos_pool[:].indirect(page_slots(g)))
             turned = bank([P, PACK, P], "turned", "early")
             for j in range(PACK):
                 nc.tensor.transpose(turned[:, j, :], pos_row[:, j * P : (j + 1) * P], ident[:])
             pos_cols = sb([P, PACK], F32, "pos_cols%d" % g)
-            nc.scalar.activation(pos_cols[:], turned[:, :, ROW], ACT.Copy)
-            spread = bank([P, PAGE], "spread", "early")
-            for j in range(PACK):
-                nc.tensor.transpose(spread[:, j * P : (j + 1) * P], pos_cols[:, j : j + 1].to_broadcast([P, P]), ident[:])
-            for u in range(Q_TILES):
-                hidden[u, g] = sb([P, PACK, P], F32, "hidden%d_%d" % (u, g))
-                nc.scalar.activation(
-                    hidden[u, g][:], spread[:].rearrange("q (s t) -> q t s", t=PACK), ACT.Relu, bias=limit[:, u : u + 1], scale=STEEP
-                )
+            nc.scalar.activation(pos_cols[:], turned[:, :, ROW], ACT.Copy, scale=STEEP)
+            if g in DIRECT_PAGES:
+                spread = bank([P, PAGE], "spread", "early")
+                for j in range(PACK):
+                    nc.tensor.transpose(spread[:, j * P : (j + 1) * P], pos_cols[:, j : j + 1].to_broadcast([P, P]), ident[:])
+                for u in range(Q_TILES):
+                    hidden[u, g] = sb([P, PACK, P], F32, "hidden%d_%d" % (u, g))
+                    nc.scalar.activation(
+                        hidden[u, g][:], spread[:].rearrange("q (s t) -> q t s", t=PACK), ACT.Relu, bias=limit[:, u : u + 1]
+                    )
+            else:
+                across = sb([P, PACK, NQ], F32, "across%d" % g)
+                for j in range(PACK):
+                    nc.scalar.activation(across[:, j, :], qpos_rows[:], ACT.Relu, bias=pos_cols[:, j : j + 1], scale=-STEEP)
+                for u in range(Q_TILES):
+                    x[u, g] = bank([P, PAGE], "x", "wide")
+                for j in range(PACK):
+                    for u in range(Q_TILES):
+                        nc.tensor.matmul(
+                            x[u, g][:, j * P : (j + 1) * P], across[:, j, u * P : (u + 1) * P], ident[:],
+                            start=(j == 0), stop=False, is_transpose=True,
+                        )
 
         vs_pool = placed([P, T], F32, "vs_pool", VS_AT)
         nc.sync.dma_start(vs_pool[:], vs)
@@ -127,33 +143,66 @@ def tile_attend_pkv8q_soft_draft_kernel(
             )
 
         a = {}
-        for g in range(PAGES):
+        for g in DIRECT_PAGES + TURNED_PAGES:
             kw = sb([P, PAGE], U32, "kw%d" % g)
             nc.vector.tensor_copy(kw[:], kw_pool[:].indirect(page_slots(g)))
+            if g in DIRECT_PAGES:
+                for u in range(Q_TILES):
+                    a[u, g] = bank([P, PAGE], "a", "wide")
+                    nc.tensor.matmul_mx(
+                        out=a[u, g][:],
+                        lhsT=qw[:, u * P : (u + 1) * P].bitcast(FP8X4),
+                        lhsT_scale=qs[:, u * P : (u + 1) * P],
+                        rhs=kw[:].bitcast(FP8X4),
+                        rhs_scale=ks[:, g * PAGE : (g + 1) * PAGE],
+                        start=True,
+                        stop=True,
+                    )
+                continue
+            for half in range(2):
+                scores = bank([P, 2, NQ], "scores", "early")
+                for jj in range(2):
+                    j = 2 * half + jj
+                    nc.tensor.matmul_mx(
+                        out=scores[:, jj, :],
+                        lhsT=kw[:, j * P : (j + 1) * P].bitcast(FP8X4),
+                        lhsT_scale=ks[:, g * PAGE + j * P : g * PAGE + (j + 1) * P],
+                        rhs=qw[:].bitcast(FP8X4),
+                        rhs_scale=qs[:],
+                        start=True,
+                        stop=True,
+                    )
+                neg = sb([P, 2, NQ], F32, "neg%d_%d" % (g, half))
+                nc.scalar.activation(neg[:], scores[:], ACT.Copy, scale=-1.0)
+                for u in range(Q_TILES):
+                    for jj in range(2):
+                        j = 2 * half + jj
+                        nc.tensor.matmul(
+                            x[u, g][:, j * P : (j + 1) * P], neg[:, jj, u * P : (u + 1) * P], ident[:],
+                            start=False, stop=(j == PACK - 1), is_transpose=True,
+                        )
+
+        down = {}
+        low = [MASKED] * Q_TILES
+
+        def lowest(u, g, source):
+            lower = sb([P, 1], F32, "low%d_%d" % (u, g))
+            nc.vector.tensor_scalar(down[u, g][:], source, MASKED, low[u], op0=ALU.min, op1=ALU.min, accum_out=lower[:])
+            low[u] = lower[:]
+
+        summed = placed([P, Q_TILES, len(DIRECT_PAGES), PACK, P], F32, "summed", 0)
+        for i, g in enumerate(DIRECT_PAGES):
             for u in range(Q_TILES):
-                a[u, g] = bank([P, PAGE], "a", "wide")
-                nc.tensor.matmul_mx(
-                    out=a[u, g][:],
-                    lhsT=qw[:, u * P : (u + 1) * P].bitcast(FP8X4),
-                    lhsT_scale=qs[:, u * P : (u + 1) * P],
-                    rhs=kw[:].bitcast(FP8X4),
-                    rhs_scale=ks[:, g * PAGE : (g + 1) * PAGE],
-                    start=True,
-                    stop=True,
+                nc.vector.tensor_tensor(
+                    summed[:, u, i], hidden[u, g][:], a[u, g][:].rearrange("q (s t) -> q t s", t=PACK), ALU.subtract
                 )
+        for i, g in enumerate(DIRECT_PAGES):
+            for u in range(Q_TILES):
+                down[u, g] = sb([P, PACK, P], F32, "down%d_%d" % (u, g))
+                lowest(u, g, summed[:, u, i])
 
-        down = []
-        low = []
         vs_cols = []
-        for u in range(Q_TILES):
-            x = placed([P, PAGES, PACK, P], F32, "x%d" % u, 4 * N * u)
-            for g in range(PAGES):
-                nc.vector.tensor_tensor(x[:, g], hidden[u, g][:], a[u, g][:].rearrange("q (s t) -> q t s", t=PACK), ALU.subtract)
-            down.append(sb([P, PAGES, PACK, P], F32, "down%d" % u))
-            low.append(sb([P, 1], F32, "low%d" % u))
-            nc.vector.tensor_scalar(down[u][:], x[:], MASKED, MASKED, op0=ALU.min, op1=ALU.min, accum_out=low[u][:])
-
-        vs_rows = placed([P, N], F32, "vs_rows", 4 * N)
+        vs_rows = placed([P, N], F32, "vs_rows", 0)
         for g in range(PAGES):
             vs_row = vs_rows[:, g * PAGE : (g + 1) * PAGE]
             nc.vector.tensor_copy(vs_row, vs_pool[:].indirect(page_slots(g)))
@@ -161,9 +210,14 @@ def tile_attend_pkv8q_soft_draft_kernel(
             nc.sync.dma_start(c[:], vs_row[0:1, :])
             vs_cols.append(c)
 
-        vw = placed([P, PAGES * DV], U32, "vw", VS_AT)
+        for i, g in enumerate(TURNED_PAGES):
+            for u in range(Q_TILES):
+                down[u, g] = placed([P, PACK, P], F32, "down%d_%d" % (u, g), VS_AT + 4 * PAGE * (Q_TILES * i + u))
+                lowest(u, g, x[u, g][:].rearrange("q (s t) -> q t s", t=PACK))
+
+        vw = placed([P, PAGES * DV], U32, "vw", VS_AT + 8 * N)
         nc.vector.tensor_copy(vw[:], vw_pool[:].indirect(vcols[:]))
-        vsc = placed([P, PAGES * DV], U8, "vsc", VS_AT + N)
+        vsc = placed([P, PAGES * DV], U8, "vsc", VS_AT + 9 * N)
         nc.vector.tensor_copy(vsc[:], vsc_pool[:].indirect(vcols[:]))
 
         for u in range(Q_TILES):
@@ -171,7 +225,7 @@ def tile_attend_pkv8q_soft_draft_kernel(
             weights = []
             for g in range(PAGES):
                 p = sb([P, PACK, P], F32, "p%d_%d" % (u, g))
-                nc.scalar.activation(p[:], down[u][:, g], ACT.Exp, bias=low[u][:], scale=-1.0, accum_out=sums[:, g : g + 1])
+                nc.scalar.activation(p[:], down[u, g][:], ACT.Exp, bias=low[u], scale=-1.0, accum_out=sums[:, g : g + 1])
                 turned = bank([P, PACK, P], "turned", "wide")
                 for t in range(PACK):
                     nc.tensor.transpose(turned[:, t, :], p[:, t, :], ident[:])
@@ -198,7 +252,8 @@ def tile_attend_pkv8q_soft_draft_kernel(
                     stop=(g == PAGES - 1),
                 )
             total = sb([P, 1], F32, "total%d" % u)
-            nc.vector.tensor_reduce(total[:], sums[:], mybir.AxisListType.X, ALU.add)
+            parts = sb([P, PAGES], F32, "parts%d" % u)
+            nc.scalar.activation(parts[:], sums[:], ACT.Copy, accum_out=total[:])
             inverse = sb([P, 1], F32, "inverse%d" % u)
             nc.vector.reciprocal(inverse[:], total[:])
             result = sb([P, DV], F32, "result%d" % u)

@@ -12,8 +12,10 @@ POOL_PAGES = T // PAGE
 Q_TILES = NQ // P
 ROW = P - 1
 POS_AT = 4 * T
-VS_AT = POS_AT + N
+VS_AT = POS_AT
 KS_AT = VS_AT + 4 * T
+ROWS_AT = KS_AT + T
+P_AT = ROWS_AT + 4 * N
 DIRECT_PAGES = [0]
 TURNED_PAGES = [1, 2]
 MASKED = 30000.0
@@ -47,8 +49,8 @@ def tile_attend_pkv8q_soft_draft_kernel(
         def placed(shape, dtype, name, offset):
             return shared.tile(shape, dtype, name=name, offset=offset, align_bytes=64)
 
-        def bank(shape, name, tag):
-            return psum.tile(shape, F32, name=name, tag=tag, bufs=6 if tag == "wide" else 2)
+        def bank(shape, name, number):
+            return psum.tile(shape, F32, name=name, tag="bank%d" % number)
 
         def scale_rows(plane, quad):
             return plane[32 * quad : 32 * quad + 4, :].bitcast(I32)
@@ -81,12 +83,20 @@ def tile_attend_pkv8q_soft_draft_kernel(
         for quad in range(4):
             nc.sync.dma_start(scale_rows(qs, quad), q_scales[0, 0, 4 * quad : 4 * quad + 4, :].bitcast(I32))
 
+        vsc_pool = sb([P, POOL_PAGES * DV], U8, "vsc_pool")
+        nc.vector.memset(vsc_pool[:].bitcast(I32), 0)
+        for quad in range(4):
+            nc.sync.dma_start(
+                scale_rows(vsc_pool, quad).rearrange("f (u e) -> f u e", u=POOL_PAGES),
+                v_scales[:, 4 * quad : 4 * quad + 4, :].rearrange("u f e -> f u e").bitcast(I32),
+            )
+
         ident = sb([P, P], F32, "ident")
         make_identity(nc, ident[:])
 
         limit = sb([P, Q_TILES], F32, "limit")
         nc.scalar.activation(limit[:], qpos_cols[:], ACT.Copy, scale=-STEEP)
-        spread = bank([P, NQ], "spread", "early")
+        spread = bank([P, NQ], "spread", 6)
         for u in range(Q_TILES):
             nc.tensor.transpose(spread[:, u * P : (u + 1) * P], qpos_cols[:, u : u + 1].to_broadcast([P, P]), ident[:])
         qpos_rows = sb([P, NQ], F32, "qpos_rows")
@@ -94,16 +104,16 @@ def tile_attend_pkv8q_soft_draft_kernel(
 
         hidden = {}
         x = {}
-        for g in TURNED_PAGES + DIRECT_PAGES:
-            pos_row = sb([P, PAGE], F32, "pos_row%d" % g)
+        for i, g in enumerate(TURNED_PAGES + DIRECT_PAGES):
+            pos_row = placed([P, PAGE], F32, "pos_row%d" % g, ROWS_AT + 4 * PAGE * i)
             nc.vector.tensor_copy(pos_row[:], pos_pool[:].indirect(page_slots(g)))
-            turned = bank([P, PACK, P], "turned", "early")
+            turned = bank([P, PACK, P], "turned", 7 - i % 2)
             for j in range(PACK):
                 nc.tensor.transpose(turned[:, j, :], pos_row[:, j * P : (j + 1) * P], ident[:])
             pos_cols = sb([P, PACK], F32, "pos_cols%d" % g)
             nc.scalar.activation(pos_cols[:], turned[:, :, ROW], ACT.Copy, scale=STEEP)
             if g in DIRECT_PAGES:
-                spread = bank([P, PAGE], "spread", "early")
+                spread = bank([P, PAGE], "spread", 6)
                 for j in range(PACK):
                     nc.tensor.transpose(spread[:, j * P : (j + 1) * P], pos_cols[:, j : j + 1].to_broadcast([P, P]), ident[:])
                 for u in range(Q_TILES):
@@ -116,7 +126,7 @@ def tile_attend_pkv8q_soft_draft_kernel(
                 for j in range(PACK):
                     nc.scalar.activation(across[:, j, :], qpos_rows[:], ACT.Relu, bias=pos_cols[:, j : j + 1], scale=-STEEP)
                 for u in range(Q_TILES):
-                    x[u, g] = bank([P, PAGE], "x", "wide")
+                    x[u, g] = bank([P, PAGE], "x", Q_TILES * i + u)
                 for j in range(PACK):
                     for u in range(Q_TILES):
                         nc.tensor.matmul(
@@ -127,60 +137,18 @@ def tile_attend_pkv8q_soft_draft_kernel(
         vs_pool = placed([P, T], F32, "vs_pool", VS_AT)
         nc.sync.dma_start(vs_pool[:], vs)
 
-        ks = placed([P, N], U8, "ks", POS_AT)
+        ks = placed([P, N], U8, "ks", ROWS_AT)
         nc.vector.tensor_copy(ks[:], ks_pool[:].indirect(slots[:]))
-        vw_pool = placed([P, POOL_PAGES * DV], U32, "vw_pool", KS_AT + POOL_PAGES * DV)
+        vw_pool = placed([P, POOL_PAGES * DV], U32, "vw_pool", KS_AT)
         nc.sync.dma_start(
             vw_pool[:].bitcast(I32).rearrange("g (u e) -> g u e", e=DV),
             v_words.rearrange("u g e r -> g u (e r)").bitcast(I32),
         )
-        vsc_pool = placed([P, POOL_PAGES * DV], U8, "vsc_pool", KS_AT)
-        nc.vector.memset(vsc_pool[:].bitcast(I32), 0)
-        for quad in range(4):
-            nc.sync.dma_start(
-                scale_rows(vsc_pool, quad).rearrange("f (u e) -> f u e", u=POOL_PAGES),
-                v_scales[:, 4 * quad : 4 * quad + 4, :].rearrange("u f e -> f u e").bitcast(I32),
-            )
 
-        a = {}
+        kw = {}
         for g in DIRECT_PAGES + TURNED_PAGES:
-            kw = sb([P, PAGE], U32, "kw%d" % g)
-            nc.vector.tensor_copy(kw[:], kw_pool[:].indirect(page_slots(g)))
-            if g in DIRECT_PAGES:
-                for u in range(Q_TILES):
-                    a[u, g] = bank([P, PAGE], "a", "wide")
-                    nc.tensor.matmul_mx(
-                        out=a[u, g][:],
-                        lhsT=qw[:, u * P : (u + 1) * P].bitcast(FP8X4),
-                        lhsT_scale=qs[:, u * P : (u + 1) * P],
-                        rhs=kw[:].bitcast(FP8X4),
-                        rhs_scale=ks[:, g * PAGE : (g + 1) * PAGE],
-                        start=True,
-                        stop=True,
-                    )
-                continue
-            for half in range(2):
-                scores = bank([P, 2, NQ], "scores", "early")
-                for jj in range(2):
-                    j = 2 * half + jj
-                    nc.tensor.matmul_mx(
-                        out=scores[:, jj, :],
-                        lhsT=kw[:, j * P : (j + 1) * P].bitcast(FP8X4),
-                        lhsT_scale=ks[:, g * PAGE + j * P : g * PAGE + (j + 1) * P],
-                        rhs=qw[:].bitcast(FP8X4),
-                        rhs_scale=qs[:],
-                        start=True,
-                        stop=True,
-                    )
-                neg = sb([P, 2, NQ], F32, "neg%d_%d" % (g, half))
-                nc.scalar.activation(neg[:], scores[:], ACT.Copy, scale=-1.0)
-                for u in range(Q_TILES):
-                    for jj in range(2):
-                        j = 2 * half + jj
-                        nc.tensor.matmul(
-                            x[u, g][:, j * P : (j + 1) * P], neg[:, jj, u * P : (u + 1) * P], ident[:],
-                            start=False, stop=(j == PACK - 1), is_transpose=True,
-                        )
+            kw[g] = sb([P, PAGE], U32, "kw%d" % g)
+            nc.vector.tensor_copy(kw[g][:], kw_pool[:].indirect(page_slots(g)))
 
         down = {}
         low = [MASKED] * Q_TILES
@@ -190,16 +158,51 @@ def tile_attend_pkv8q_soft_draft_kernel(
             nc.vector.tensor_scalar(down[u, g][:], source, MASKED, low[u], op0=ALU.min, op1=ALU.min, accum_out=lower[:])
             low[u] = lower[:]
 
-        summed = placed([P, Q_TILES, len(DIRECT_PAGES), PACK, P], F32, "summed", 0)
-        for i, g in enumerate(DIRECT_PAGES):
+        summed = {}
+        for g in DIRECT_PAGES:
             for u in range(Q_TILES):
-                nc.vector.tensor_tensor(
-                    summed[:, u, i], hidden[u, g][:], a[u, g][:].rearrange("q (s t) -> q t s", t=PACK), ALU.subtract
+                a = bank([P, PAGE], "a", 4 + u)
+                nc.tensor.matmul_mx(
+                    out=a[:],
+                    lhsT=qw[:, u * P : (u + 1) * P].bitcast(FP8X4),
+                    lhsT_scale=qs[:, u * P : (u + 1) * P],
+                    rhs=kw[g][:].bitcast(FP8X4),
+                    rhs_scale=ks[:, g * PAGE : (g + 1) * PAGE],
+                    start=True,
+                    stop=True,
                 )
-        for i, g in enumerate(DIRECT_PAGES):
+                summed[u, g] = placed([P, PACK, P], F32, "summed%d" % u, 4 * N * u)
+                nc.vector.tensor_tensor(summed[u, g][:], hidden[u, g][:], a[:].rearrange("q (s t) -> q t s", t=PACK), ALU.subtract)
             for u in range(Q_TILES):
                 down[u, g] = sb([P, PACK, P], F32, "down%d_%d" % (u, g))
-                lowest(u, g, summed[:, u, i])
+                lowest(u, g, summed[u, g][:])
+
+        neg = {}
+        for i, g in enumerate(TURNED_PAGES):
+            for half in range(2):
+                scores = bank([P, 2, NQ], "scores", (7 - half, 4 + half)[i])
+                for jj in range(2):
+                    j = 2 * half + jj
+                    nc.tensor.matmul_mx(
+                        out=scores[:, jj, :],
+                        lhsT=kw[g][:, j * P : (j + 1) * P].bitcast(FP8X4),
+                        lhsT_scale=ks[:, g * PAGE + j * P : g * PAGE + (j + 1) * P],
+                        rhs=qw[:].bitcast(FP8X4),
+                        rhs_scale=qs[:],
+                        start=True,
+                        stop=True,
+                    )
+                neg[g, half] = sb([P, 2, NQ], F32, "neg%d_%d" % (g, half))
+                nc.scalar.activation(neg[g, half][:], scores[:], ACT.Copy, scale=-1.0)
+        for g in TURNED_PAGES:
+            for half in range(2):
+                for u in range(Q_TILES):
+                    for jj in range(2):
+                        j = 2 * half + jj
+                        nc.tensor.matmul(
+                            x[u, g][:, j * P : (j + 1) * P], neg[g, half][:, jj, u * P : (u + 1) * P], ident[:],
+                            start=False, stop=(j == PACK - 1), is_transpose=True,
+                        )
 
         vs_cols = []
         vs_rows = placed([P, N], F32, "vs_rows", 0)
@@ -220,28 +223,49 @@ def tile_attend_pkv8q_soft_draft_kernel(
         vsc = placed([P, PAGES * DV], U8, "vsc", VS_AT + 9 * N)
         nc.vector.tensor_copy(vsc[:], vsc_pool[:].indirect(vcols[:]))
 
+        units = [(u, g) for u in range(Q_TILES) for g in range(PAGES)]
+        sums = [sb([P, PAGES], F32, "sums%d" % u) for u in range(Q_TILES)]
+        weights = []
+        quantised = []
+
+        def weigh(k):
+            u, g = units[k]
+            p = placed([P, PACK, P], F32, "p%d" % k, P_AT + 4 * PAGE * k)
+            nc.scalar.activation(p[:], down[u, g][:], ACT.Exp, bias=low[u], scale=-1.0, accum_out=sums[u][:, g : g + 1])
+            turned = bank([P, PACK, P], "turned", (6 + k) % 8)
+            for t in range(PACK):
+                nc.tensor.transpose(turned[:, t, :], p[:, t, :], ident[:])
+            w = sb([P, P, PACK], BF16, "w%d" % k)
+            nc.vector.tensor_tensor(
+                w[:],
+                turned[:].rearrange("s t q -> s q t"),
+                vs_cols[g][:].unsqueeze(1).to_broadcast([P, P, PACK]),
+                ALU.mult,
+            )
+            weights.append(w)
+
+        def quantise(k):
+            codes = placed([P, P], U32, "codes%d" % k, P_AT + 4 * PAGE * (k + 1))
+            scales = sb([P, P], U8, "scales%d" % k)
+            nc.vector.quantize_mx(out=codes[:].bitcast(FP8X4), scales=scales[:], in_=weights[k][:].rearrange("s q t -> s (q t)"))
+            quantised.append((codes, scales))
+
+        weigh(0)
+        for k in range(1, len(units)):
+            weigh(k)
+            quantise(k - 1)
+        total = sb([P, Q_TILES], F32, "total")
         for u in range(Q_TILES):
-            sums = sb([P, PAGES], F32, "sums%d" % u)
-            weights = []
+            parts = sb([P, PAGES], F32, "parts%d" % u)
+            nc.scalar.activation(parts[:], sums[u][:], ACT.Copy, accum_out=total[:, u : u + 1])
+        inverse = sb([P, Q_TILES], F32, "inverse")
+        nc.vector.reciprocal(inverse[:], total[:])
+        quantise(len(units) - 1)
+
+        for u in range(Q_TILES):
+            y = bank([P, DV], "y", 2 - u)
             for g in range(PAGES):
-                p = sb([P, PACK, P], F32, "p%d_%d" % (u, g))
-                nc.scalar.activation(p[:], down[u, g][:], ACT.Exp, bias=low[u], scale=-1.0, accum_out=sums[:, g : g + 1])
-                turned = bank([P, PACK, P], "turned", "wide")
-                for t in range(PACK):
-                    nc.tensor.transpose(turned[:, t, :], p[:, t, :], ident[:])
-                w = sb([P, P, PACK], BF16, "w%d_%d" % (u, g))
-                nc.vector.tensor_tensor(
-                    w[:],
-                    turned[:].rearrange("s t q -> s q t"),
-                    vs_cols[g][:].unsqueeze(1).to_broadcast([P, P, PACK]),
-                    ALU.mult,
-                )
-                weights.append(w)
-            y = bank([P, DV], "y", "early")
-            for g in range(PAGES):
-                codes = sb([P, P], U32, "codes%d_%d" % (u, g))
-                scales = sb([P, P], U8, "scales%d_%d" % (u, g))
-                nc.vector.quantize_mx(out=codes[:].bitcast(FP8X4), scales=scales[:], in_=weights[g][:].rearrange("s q t -> s (q t)"))
+                codes, scales = quantised[PAGES * u + g]
                 nc.tensor.matmul_mx(
                     out=y[:],
                     lhsT=codes[:].bitcast(FP8X4),
@@ -251,11 +275,6 @@ def tile_attend_pkv8q_soft_draft_kernel(
                     start=(g == 0),
                     stop=(g == PAGES - 1),
                 )
-            total = sb([P, 1], F32, "total%d" % u)
-            parts = sb([P, PAGES], F32, "parts%d" % u)
-            nc.scalar.activation(parts[:], sums[:], ACT.Copy, accum_out=total[:])
-            inverse = sb([P, 1], F32, "inverse%d" % u)
-            nc.vector.reciprocal(inverse[:], total[:])
             result = sb([P, DV], F32, "result%d" % u)
-            nc.scalar.activation(result[:], y[:], ACT.Copy, scale=inverse[:])
+            nc.scalar.activation(result[:], y[:], ACT.Copy, scale=inverse[:, u : u + 1])
             nc.sync.dma_start(out[0, u * P : (u + 1) * P, :], result[:])

@@ -14,7 +14,7 @@ ROW = P - 1
 POS_AT = 4 * T
 VS_AT = POS_AT
 KS_AT = VS_AT + 4 * T
-ROWS_AT = KS_AT + T
+ROWS_AT = KS_AT + 5 * POOL_PAGES * DV
 P_AT = ROWS_AT + 4 * N
 DIRECT_PAGES = [0]
 TURNED_PAGES = [1, 2]
@@ -83,14 +83,6 @@ def tile_attend_pkv8q_soft_draft_kernel(
         for quad in range(4):
             nc.sync.dma_start(scale_rows(qs, quad), q_scales[0, 0, 4 * quad : 4 * quad + 4, :].bitcast(I32))
 
-        vsc_pool = sb([P, POOL_PAGES * DV], U8, "vsc_pool")
-        nc.vector.memset(vsc_pool[:].bitcast(I32), 0)
-        for quad in range(4):
-            nc.sync.dma_start(
-                scale_rows(vsc_pool, quad).rearrange("f (u e) -> f u e", u=POOL_PAGES),
-                v_scales[:, 4 * quad : 4 * quad + 4, :].rearrange("u f e -> f u e").bitcast(I32),
-            )
-
         ident = sb([P, P], F32, "ident")
         make_identity(nc, ident[:])
 
@@ -139,11 +131,19 @@ def tile_attend_pkv8q_soft_draft_kernel(
 
         ks = placed([P, N], U8, "ks", ROWS_AT)
         nc.vector.tensor_copy(ks[:], ks_pool[:].indirect(slots[:]))
-        vw_pool = placed([P, POOL_PAGES * DV], U32, "vw_pool", KS_AT)
+        vw_pool = placed([P, POOL_PAGES * DV], U32, "vw_pool", KS_AT + POOL_PAGES * DV)
         nc.sync.dma_start(
             vw_pool[:].bitcast(I32).rearrange("g (u e) -> g u e", e=DV),
             v_words.rearrange("u g e r -> g u (e r)").bitcast(I32),
         )
+
+        vsc_pool = placed([P, POOL_PAGES * DV], U8, "vsc_pool", ROWS_AT + 4 * PAGE * (PAGES - 1))
+        nc.vector.memset(vsc_pool[:].bitcast(I32), 0)
+        for quad in range(4):
+            nc.sync.dma_start(
+                scale_rows(vsc_pool, quad).rearrange("f (u e) -> f u e", u=POOL_PAGES),
+                v_scales[:, 4 * quad : 4 * quad + 4, :].rearrange("u f e -> f u e").bitcast(I32),
+            )
 
         kw = {}
         for g in DIRECT_PAGES + TURNED_PAGES:

@@ -95,17 +95,29 @@ def tile_attend_pkv8q_soft_draft_kernel(
         nc.scalar.activation(qpos_rows[:], spread[:], ACT.Copy)
 
         hidden = {}
+        across = {}
         x = {}
-        for i, g in enumerate(TURNED_PAGES + DIRECT_PAGES):
+
+        def open_sums(g, first_bank):
+            for u in range(Q_TILES):
+                x[u, g] = bank([P, PAGE], "x", first_bank + u)
+            for j in range(PACK):
+                for u in range(Q_TILES):
+                    nc.tensor.matmul(
+                        x[u, g][:, j * P : (j + 1) * P], across[g][:, j, u * P : (u + 1) * P], ident[:],
+                        start=(j == 0), stop=False, is_transpose=True,
+                    )
+
+        for i, g in enumerate(DIRECT_PAGES + TURNED_PAGES):
             pos_row = placed([P, PAGE], F32, "pos_row%d" % g, ROWS_AT + 4 * PAGE * i)
             nc.vector.tensor_copy(pos_row[:], pos_pool[:].indirect(page_slots(g)))
-            turned = bank([P, PACK, P], "turned", 7 - i % 2)
+            turned = bank([P, PACK, P], "turned", (7, 3, 6)[i])
             for j in range(PACK):
                 nc.tensor.transpose(turned[:, j, :], pos_row[:, j * P : (j + 1) * P], ident[:])
             pos_cols = sb([P, PACK], F32, "pos_cols%d" % g)
             nc.scalar.activation(pos_cols[:], turned[:, :, ROW], ACT.Copy, scale=STEEP)
             if g in DIRECT_PAGES:
-                spread = bank([P, PAGE], "spread", 6)
+                spread = bank([P, PAGE], "spread", 2)
                 for j in range(PACK):
                     nc.tensor.transpose(spread[:, j * P : (j + 1) * P], pos_cols[:, j : j + 1].to_broadcast([P, P]), ident[:])
                 for u in range(Q_TILES):
@@ -114,17 +126,11 @@ def tile_attend_pkv8q_soft_draft_kernel(
                         hidden[u, g][:], spread[:].rearrange("q (s t) -> q t s", t=PACK), ACT.Relu, bias=limit[:, u : u + 1]
                     )
             else:
-                across = sb([P, PACK, NQ], F32, "across%d" % g)
+                across[g] = sb([P, PACK, NQ], F32, "across%d" % g)
                 for j in range(PACK):
-                    nc.scalar.activation(across[:, j, :], qpos_rows[:], ACT.Relu, bias=pos_cols[:, j : j + 1], scale=-STEEP)
-                for u in range(Q_TILES):
-                    x[u, g] = bank([P, PAGE], "x", Q_TILES * i + u)
-                for j in range(PACK):
-                    for u in range(Q_TILES):
-                        nc.tensor.matmul(
-                            x[u, g][:, j * P : (j + 1) * P], across[:, j, u * P : (u + 1) * P], ident[:],
-                            start=(j == 0), stop=False, is_transpose=True,
-                        )
+                    nc.scalar.activation(across[g][:, j, :], qpos_rows[:], ACT.Relu, bias=pos_cols[:, j : j + 1], scale=-STEEP)
+                if g == TURNED_PAGES[0]:
+                    open_sums(g, 0)
 
         vs_pool = placed([P, T], F32, "vs_pool", VS_AT)
         nc.sync.dma_start(vs_pool[:], vs)
@@ -180,7 +186,7 @@ def tile_attend_pkv8q_soft_draft_kernel(
         neg = {}
         for i, g in enumerate(TURNED_PAGES):
             for half in range(2):
-                scores = bank([P, 2, NQ], "scores", (7 - half, 4 + half)[i])
+                scores = bank([P, 2, NQ], "scores", (7 - half, 2 + half)[i])
                 for jj in range(2):
                     j = 2 * half + jj
                     nc.tensor.matmul_mx(
@@ -194,6 +200,7 @@ def tile_attend_pkv8q_soft_draft_kernel(
                     )
                 neg[g, half] = sb([P, 2, NQ], F32, "neg%d_%d" % (g, half))
                 nc.scalar.activation(neg[g, half][:], scores[:], ACT.Copy, scale=-1.0)
+        open_sums(TURNED_PAGES[1], 4)
         for g in TURNED_PAGES:
             for half in range(2):
                 for u in range(Q_TILES):
@@ -206,11 +213,10 @@ def tile_attend_pkv8q_soft_draft_kernel(
 
         vs_cols = []
         vs_rows = placed([P, N], F32, "vs_rows", 0)
+        nc.vector.tensor_copy(vs_rows[:], vs_pool[:].indirect(slots[:]))
         for g in range(PAGES):
-            vs_row = vs_rows[:, g * PAGE : (g + 1) * PAGE]
-            nc.vector.tensor_copy(vs_row, vs_pool[:].indirect(page_slots(g)))
             c = sb([P, PACK], F32, "vs_cols%d" % g)
-            nc.sync.dma_start(c[:], vs_row[0:1, :])
+            nc.sync.dma_start(c[:], vs_rows[0:1, g * PAGE : (g + 1) * PAGE])
             vs_cols.append(c)
 
         for i, g in enumerate(TURNED_PAGES):

@@ -11,15 +11,14 @@ PAGES = N // PAGE
 POOL_PAGES = T // PAGE
 Q_TILES = NQ // P
 ROW = P - 1
-POS_AT = 4 * T
-VS_AT = POS_AT
-KS_AT = VS_AT + 4 * T
-ROWS_AT = KS_AT + 5 * POOL_PAGES * DV
-P_AT = ROWS_AT + 4 * N
-DIRECT_PAGES = [0]
-TURNED_PAGES = [1, 2]
 MASKED = 30000.0
-STEEP = 2.0 ** 80
+SLOPE = 2.0 ** -15
+STEEP = 2.0 ** 126
+
+ROW_AT = 4 * T
+VS_AT = ROW_AT + 4 * T
+KS_AT = VS_AT + 4 * T
+P_AT = KS_AT + T
 
 FLOPS = 2 * NQ * N * D + 2 * NQ * N * DV
 
@@ -43,8 +42,8 @@ def tile_attend_pkv8q_soft_draft_kernel(
         shared = ctx.enter_context(tc.tile_pool(name="shared", bufs=1))
         psum = ctx.enter_context(tc.psum_pool(name="psum", bufs=1))
 
-        def sb(shape, dtype, name, tag=""):
-            return keep.tile(shape, dtype, name=name, tag=tag or name, align_bytes=64)
+        def sb(shape, dtype, name):
+            return keep.tile(shape, dtype, name=name, tag=name, align_bytes=64)
 
         def placed(shape, dtype, name, offset):
             return shared.tile(shape, dtype, name=name, offset=offset, align_bytes=64)
@@ -60,47 +59,96 @@ def tile_attend_pkv8q_soft_draft_kernel(
 
         slots = keep.tile([P, N // 16], U16, name="slots")
         nc.sync.dma_start(slots[:], offs)
-        pos_pool = placed([P, T], F32, "pos_pool", POS_AT)
+        pos_pool = placed([P, T], F32, "pos_pool", ROW_AT)
         nc.sync.dma_start(pos_pool[ROW:P, :], pos[0:1, :])
         kw_pool = placed([P, T], U32, "kw_pool", 0)
-        nc.sync.dma_start(kw_pool[:].bitcast(I32), k_words[0].rearrange("g t r -> g (t r)").bitcast(I32))
+        nc.sync.dma_start(kw_pool[:].bitcast(I32), k_words[0].rearrange("g t r -> g (t r)").bitcast(I32), max_dma_last_dim=4096)
         vcols = keep.tile([P, PAGES * DV // 16], U16, name="vcols")
         nc.sync.dma_start(vcols[:], voffs)
 
         qpos_cols = sb([P, Q_TILES], F32, "qpos_cols")
         with nc.allow_non_contiguous_dma(reason="one place a partition and query tile"):
             nc.scalar.dma_start(qpos_cols[:], qpos[0].rearrange("(u p) o -> p (u o)", p=P))
-        qw = sb([P, NQ], U32, "qw")
-        nc.scalar.dma_start(qw[:].bitcast(I32), q_words[0, 0].rearrange("g q r -> g (q r)").bitcast(I32))
 
         ks_pool = placed([P, T], U8, "ks_pool", KS_AT)
         nc.vector.memset(ks_pool[:].bitcast(I32), 0)
         for quad in range(4):
             nc.scalar.dma_start(scale_rows(ks_pool, quad), k_scales[0, 4 * quad : 4 * quad + 4, :].bitcast(I32))
-        nc.vector.memset(pos_pool[0:ROW, :], 0.0)
         qs = sb([P, NQ], U8, "qs")
         nc.vector.memset(qs[:].bitcast(I32), 0)
+        vsc_pool = sb([P, POOL_PAGES * DV], U8, "vsc_pool")
+        nc.vector.memset(vsc_pool[:].bitcast(I32), 0)
+        nc.vector.memset(pos_pool[0:ROW, :], 0.0)
+        qw = sb([P, NQ], U32, "qw")
+        nc.sync.dma_start(qw[:].bitcast(I32), q_words[0, 0].rearrange("g q r -> g (q r)").bitcast(I32))
         for quad in range(4):
             nc.sync.dma_start(scale_rows(qs, quad), q_scales[0, 0, 4 * quad : 4 * quad + 4, :].bitcast(I32))
+        vw_pool = sb([P, POOL_PAGES * DV], U32, "vw_pool")
+        nc.sync.dma_start(
+            vw_pool[:].bitcast(I32).rearrange("g (u e) -> g u e", e=DV),
+            v_words.rearrange("u g e r -> g u (e r)").bitcast(I32),
+        )
+        for quad in range(4):
+            nc.sync.dma_start(
+                scale_rows(vsc_pool, quad).rearrange("f (u e) -> f u e", u=POOL_PAGES),
+                v_scales[:, 4 * quad : 4 * quad + 4, :].rearrange("u f e -> f u e").bitcast(I32),
+            )
 
         ident = sb([P, P], F32, "ident")
         make_identity(nc, ident[:])
 
-        limit = sb([P, Q_TILES], F32, "limit")
-        nc.scalar.activation(limit[:], qpos_cols[:], ACT.Copy, scale=-STEEP)
-        spread = bank([P, NQ], "spread", 6)
+        half = sb([P, 1], F32, "half")
+        nc.gpsimd.memset(half[:], -SLOPE / 2)
+        q_rank = placed([P, Q_TILES], F32, "q_rank", VS_AT)
+        nc.scalar.activation(q_rank[:], qpos_cols[:], ACT.Sigmoid, scale=-SLOPE, bias=half[:])
+        spread = bank([P, NQ], "spread", 7)
         for u in range(Q_TILES):
-            nc.tensor.transpose(spread[:, u * P : (u + 1) * P], qpos_cols[:, u : u + 1].to_broadcast([P, P]), ident[:])
-        qpos_rows = sb([P, NQ], F32, "qpos_rows")
-        nc.scalar.activation(qpos_rows[:], spread[:], ACT.Copy)
+            nc.tensor.transpose(spread[:, u * P : (u + 1) * P], q_rank[:, u : u + 1].to_broadcast([P, P]), ident[:])
+        q_rows = sb([P, NQ], F32, "q_rows")
+        nc.scalar.activation(q_rows[:], spread[:], ACT.Copy)
 
-        hidden = {}
+        rank_cols = []
+        for g in range(PAGES):
+            rank_row = sb([P, PAGE], F32, "rank_row%d" % g)
+            nc.scalar.activation(rank_row[:], pos_pool[:].indirect(page_slots(g)), ACT.Sigmoid, scale=-SLOPE)
+            turned = bank([P, PACK, P], "turned", (6, 5, 4)[g])
+            for j in range(PACK):
+                nc.tensor.transpose(turned[:, j, :], rank_row[:, j * P : (j + 1) * P], ident[:])
+            cols = sb([P, PACK], F32, "rank_cols%d" % g)
+            nc.scalar.activation(cols[:], turned[:, :, ROW], ACT.Copy, scale=-STEEP)
+            rank_cols.append(cols)
+
+        vs_pool = placed([P, T], F32, "vs_pool", VS_AT)
+        nc.gpsimd.memset(vs_pool[0:ROW, :], 0.0)
+        nc.sync.dma_start(vs_pool[ROW:P, :], vs[0:1, :])
+
+        ks = sb([P, N], U8, "ks")
+        nc.vector.tensor_copy(ks[:], ks_pool[:].indirect(slots[:]))
+        kw = []
+        for g in range(PAGES):
+            words = sb([P, PAGE], U32, "kw%d" % g)
+            nc.vector.tensor_copy(words[:], kw_pool[:].indirect(page_slots(g)))
+            kw.append(words)
+        vs_rows = placed([P, N], F32, "vs_rows", 0)
+        nc.vector.tensor_copy(vs_rows[:], vs_pool[:].indirect(slots[:]))
+        vs_cols = []
+        for g in range(PAGES):
+            c = sb([P, PACK], F32, "vs_cols%d" % g)
+            nc.sync.dma_start(c[:], vs_rows[ROW:P, g * PAGE : (g + 1) * PAGE])
+            vs_cols.append(c)
+
         across = {}
+        neg = {}
         x = {}
 
-        def open_sums(g, first_bank):
+        def hide(g):
+            across[g] = sb([P, PACK, NQ], F32, "across%d" % g)
+            for j in range(PACK):
+                nc.scalar.activation(across[g][:, j, :], q_rows[:], ACT.Relu, bias=rank_cols[g][:, j : j + 1], scale=STEEP)
+
+        def open_sums(g):
             for u in range(Q_TILES):
-                x[u, g] = bank([P, PAGE], "x", first_bank + u)
+                x[u, g] = bank([P, PAGE], "x", Q_TILES * g + u)
             for j in range(PACK):
                 for u in range(Q_TILES):
                     nc.tensor.matmul(
@@ -108,87 +156,11 @@ def tile_attend_pkv8q_soft_draft_kernel(
                         start=(j == 0), stop=False, is_transpose=True,
                     )
 
-        for i, g in enumerate(DIRECT_PAGES + TURNED_PAGES):
-            pos_row = placed([P, PAGE], F32, "pos_row%d" % g, ROWS_AT + 4 * PAGE * i)
-            nc.vector.tensor_copy(pos_row[:], pos_pool[:].indirect(page_slots(g)))
-            turned = bank([P, PACK, P], "turned", (7, 3, 6)[i])
-            for j in range(PACK):
-                nc.tensor.transpose(turned[:, j, :], pos_row[:, j * P : (j + 1) * P], ident[:])
-            pos_cols = sb([P, PACK], F32, "pos_cols%d" % g)
-            nc.scalar.activation(pos_cols[:], turned[:, :, ROW], ACT.Copy, scale=STEEP)
-            if g in DIRECT_PAGES:
-                spread = bank([P, PAGE], "spread", 2)
-                for j in range(PACK):
-                    nc.tensor.transpose(spread[:, j * P : (j + 1) * P], pos_cols[:, j : j + 1].to_broadcast([P, P]), ident[:])
-                for u in range(Q_TILES):
-                    hidden[u, g] = sb([P, PACK, P], F32, "hidden%d_%d" % (u, g))
-                    nc.scalar.activation(
-                        hidden[u, g][:], spread[:].rearrange("q (s t) -> q t s", t=PACK), ACT.Relu, bias=limit[:, u : u + 1]
-                    )
-            else:
-                across[g] = sb([P, PACK, NQ], F32, "across%d" % g)
-                for j in range(PACK):
-                    nc.scalar.activation(across[g][:, j, :], qpos_rows[:], ACT.Relu, bias=pos_cols[:, j : j + 1], scale=-STEEP)
-                if g == TURNED_PAGES[0]:
-                    open_sums(g, 0)
-
-        vs_pool = placed([P, T], F32, "vs_pool", VS_AT)
-        nc.sync.dma_start(vs_pool[:], vs)
-
-        ks = placed([P, N], U8, "ks", ROWS_AT)
-        nc.vector.tensor_copy(ks[:], ks_pool[:].indirect(slots[:]))
-        vw_pool = placed([P, POOL_PAGES * DV], U32, "vw_pool", KS_AT + POOL_PAGES * DV)
-        nc.sync.dma_start(
-            vw_pool[:].bitcast(I32).rearrange("g (u e) -> g u e", e=DV),
-            v_words.rearrange("u g e r -> g u (e r)").bitcast(I32),
-        )
-
-        vsc_pool = placed([P, POOL_PAGES * DV], U8, "vsc_pool", ROWS_AT + 4 * PAGE * (PAGES - 1))
-        nc.vector.memset(vsc_pool[:].bitcast(I32), 0)
-        for quad in range(4):
-            nc.sync.dma_start(
-                scale_rows(vsc_pool, quad).rearrange("f (u e) -> f u e", u=POOL_PAGES),
-                v_scales[:, 4 * quad : 4 * quad + 4, :].rearrange("u f e -> f u e").bitcast(I32),
-            )
-
-        kw = {}
-        for g in DIRECT_PAGES + TURNED_PAGES:
-            kw[g] = sb([P, PAGE], U32, "kw%d" % g)
-            nc.vector.tensor_copy(kw[g][:], kw_pool[:].indirect(page_slots(g)))
-
-        down = {}
-        low = [MASKED] * Q_TILES
-
-        def lowest(u, g, source):
-            lower = sb([P, 1], F32, "low%d_%d" % (u, g))
-            nc.vector.tensor_scalar(down[u, g][:], source, MASKED, low[u], op0=ALU.min, op1=ALU.min, accum_out=lower[:])
-            low[u] = lower[:]
-
-        summed = {}
-        for g in DIRECT_PAGES:
-            for u in range(Q_TILES):
-                a = bank([P, PAGE], "a", 4 + u)
-                nc.tensor.matmul_mx(
-                    out=a[:],
-                    lhsT=qw[:, u * P : (u + 1) * P].bitcast(FP8X4),
-                    lhsT_scale=qs[:, u * P : (u + 1) * P],
-                    rhs=kw[g][:].bitcast(FP8X4),
-                    rhs_scale=ks[:, g * PAGE : (g + 1) * PAGE],
-                    start=True,
-                    stop=True,
-                )
-                summed[u, g] = placed([P, PACK, P], F32, "summed%d" % u, 4 * N * u)
-                nc.vector.tensor_tensor(summed[u, g][:], hidden[u, g][:], a[:].rearrange("q (s t) -> q t s", t=PACK), ALU.subtract)
-            for u in range(Q_TILES):
-                down[u, g] = sb([P, PACK, P], F32, "down%d_%d" % (u, g))
-                lowest(u, g, summed[u, g][:])
-
-        neg = {}
-        for i, g in enumerate(TURNED_PAGES):
-            for half in range(2):
-                scores = bank([P, 2, NQ], "scores", (7 - half, 2 + half)[i])
+        def score(g, first_bank):
+            for half_page in range(2):
+                scores = bank([P, 2, NQ], "scores", first_bank + half_page)
                 for jj in range(2):
-                    j = 2 * half + jj
+                    j = 2 * half_page + jj
                     nc.tensor.matmul_mx(
                         out=scores[:, jj, :],
                         lhsT=kw[g][:, j * P : (j + 1) * P].bitcast(FP8X4),
@@ -198,31 +170,43 @@ def tile_attend_pkv8q_soft_draft_kernel(
                         start=True,
                         stop=True,
                     )
-                neg[g, half] = sb([P, 2, NQ], F32, "neg%d_%d" % (g, half))
-                nc.scalar.activation(neg[g, half][:], scores[:], ACT.Copy, scale=-1.0)
-        open_sums(TURNED_PAGES[1], 4)
-        for g in TURNED_PAGES:
-            for half in range(2):
+                neg[g, half_page] = sb([P, 2, NQ], F32, "neg%d_%d" % (g, half_page))
+                nc.scalar.activation(neg[g, half_page][:], scores[:], ACT.Copy, scale=-1.0)
+
+        def close_sums(g):
+            for half_page in range(2):
                 for u in range(Q_TILES):
                     for jj in range(2):
-                        j = 2 * half + jj
+                        j = 2 * half_page + jj
                         nc.tensor.matmul(
-                            x[u, g][:, j * P : (j + 1) * P], neg[g, half][:, jj, u * P : (u + 1) * P], ident[:],
+                            x[u, g][:, j * P : (j + 1) * P], neg[g, half_page][:, jj, u * P : (u + 1) * P], ident[:],
                             start=False, stop=(j == PACK - 1), is_transpose=True,
                         )
 
-        vs_cols = []
-        vs_rows = placed([P, N], F32, "vs_rows", 0)
-        nc.vector.tensor_copy(vs_rows[:], vs_pool[:].indirect(slots[:]))
-        for g in range(PAGES):
-            c = sb([P, PACK], F32, "vs_cols%d" % g)
-            nc.sync.dma_start(c[:], vs_rows[0:1, g * PAGE : (g + 1) * PAGE])
-            vs_cols.append(c)
+        hide(0)
+        open_sums(0)
+        hide(1)
+        open_sums(1)
+        score(0, 6)
+        hide(2)
+        score(1, 4)
+        close_sums(0)
+        score(2, 6)
+        close_sums(1)
+        open_sums(2)
+        close_sums(2)
 
-        for i, g in enumerate(TURNED_PAGES):
+        down = {}
+        low = [MASKED] * Q_TILES
+        for g in range(PAGES):
             for u in range(Q_TILES):
-                down[u, g] = placed([P, PACK, P], F32, "down%d_%d" % (u, g), VS_AT + 4 * PAGE * (Q_TILES * i + u))
-                lowest(u, g, x[u, g][:].rearrange("q (s t) -> q t s", t=PACK))
+                down[u, g] = placed([P, PACK, P], F32, "down%d_%d" % (u, g), VS_AT + 4 * PAGE * (Q_TILES * g + u))
+                lower = sb([P, 1], F32, "low%d_%d" % (u, g))
+                nc.vector.tensor_scalar(
+                    down[u, g][:], x[u, g][:].rearrange("q (s t) -> q t s", t=PACK), MASKED, low[u],
+                    op0=ALU.min, op1=ALU.min, accum_out=lower[:],
+                )
+                low[u] = lower[:]
 
         vw = placed([P, PAGES * DV], U32, "vw", VS_AT + 8 * N)
         nc.vector.tensor_copy(vw[:], vw_pool[:].indirect(vcols[:]))
@@ -269,7 +253,7 @@ def tile_attend_pkv8q_soft_draft_kernel(
         quantise(len(units) - 1)
 
         for u in range(Q_TILES):
-            y = bank([P, DV], "y", 2 - u)
+            y = bank([P, DV], "y", 4 + u)
             for g in range(PAGES):
                 codes, scales = quantised[PAGES * u + g]
                 nc.tensor.matmul_mx(

@@ -19,6 +19,12 @@ ROW_AT = 4 * T
 VS_AT = ROW_AT + 4 * T
 KS_AT = VS_AT + 4 * T
 P_AT = KS_AT + T
+NEG_AT = P_AT + 4 * PAGE * (Q_TILES * PAGES + 1)
+
+NEG_SLOT = [0, 2, 3]
+RANK_AT = NEG_AT + 4 * PAGE * 8
+KW_AT = RANK_AT + 4 * PAGE * 2 + 4 * PACK * NQ
+ACROSS_AT = KW_AT + 4 * PACK * NQ * PAGES
 
 FLOPS = 2 * NQ * N * D + 2 * NQ * N * DV
 
@@ -88,6 +94,8 @@ def tile_attend_pkv8q_soft_draft_kernel(
             vw_pool[:].bitcast(I32).rearrange("g (u e) -> g u e", e=DV),
             v_words.rearrange("u g e r -> g u (e r)").bitcast(I32),
         )
+        vs_pool = placed([P, T], F32, "vs_pool", VS_AT)
+        nc.sync.dma_start(vs_pool[:], vs)
         for quad in range(4):
             nc.sync.dma_start(
                 scale_rows(vsc_pool, quad).rearrange("f (u e) -> f u e", u=POOL_PAGES),
@@ -97,54 +105,53 @@ def tile_attend_pkv8q_soft_draft_kernel(
         ident = sb([P, P], F32, "ident")
         make_identity(nc, ident[:])
 
-        half = sb([P, 1], F32, "half")
-        nc.gpsimd.memset(half[:], -SLOPE / 2)
-        q_rank = placed([P, Q_TILES], F32, "q_rank", VS_AT)
-        nc.scalar.activation(q_rank[:], qpos_cols[:], ACT.Sigmoid, scale=-SLOPE, bias=half[:])
+        q_rank = sb([P, Q_TILES], F32, "q_rank")
+        nc.scalar.activation(q_rank[:], qpos_cols[:], ACT.Sigmoid, scale=-SLOPE)
         spread = bank([P, NQ], "spread", 7)
         for u in range(Q_TILES):
             nc.tensor.transpose(spread[:, u * P : (u + 1) * P], q_rank[:, u : u + 1].to_broadcast([P, P]), ident[:])
         q_rows = sb([P, NQ], F32, "q_rows")
-        nc.scalar.activation(q_rows[:], spread[:], ACT.Copy)
+        nc.scalar.activation(q_rows[:], spread[:], ACT.Copy, scale=1.0 - SLOPE / 8)
 
-        rank_cols = []
-        for g in range(PAGES):
-            rank_row = sb([P, PAGE], F32, "rank_row%d" % g)
-            nc.scalar.activation(rank_row[:], pos_pool[:].indirect(page_slots(g)), ACT.Sigmoid, scale=-SLOPE)
-            turned = bank([P, PACK, P], "turned", (6, 5, 4)[g])
+        rank_row = {}
+        rank_cols = {}
+
+        def rank(g, at):
+            rank_row[g] = placed([P, PAGE], F32, "rank_row%d" % g, at)
+            nc.scalar.activation(rank_row[g][:], pos_pool[:].indirect(page_slots(g)), ACT.Sigmoid, scale=-SLOPE)
+
+        def turn_ranks(g, number):
+            turned = bank([P, PACK, P], "turned", number)
             for j in range(PACK):
-                nc.tensor.transpose(turned[:, j, :], rank_row[:, j * P : (j + 1) * P], ident[:])
-            cols = sb([P, PACK], F32, "rank_cols%d" % g)
-            nc.scalar.activation(cols[:], turned[:, :, ROW], ACT.Copy, scale=-STEEP)
-            rank_cols.append(cols)
+                nc.tensor.transpose(turned[:, j, :], rank_row[g][:, j * P : (j + 1) * P], ident[:])
+            rank_cols[g] = placed([P, PACK], F32, "rank_cols%d" % g, KW_AT + 4 * PACK * NQ * (g - 1) + (4 * PAGE if g != 1 else 0))
+            nc.scalar.activation(rank_cols[g][:], turned[:, :, ROW], ACT.Copy, scale=-STEEP)
 
-        vs_pool = placed([P, T], F32, "vs_pool", VS_AT)
-        nc.gpsimd.memset(vs_pool[0:ROW, :], 0.0)
-        nc.sync.dma_start(vs_pool[ROW:P, :], vs[0:1, :])
+        rank(0, RANK_AT)
+        turn_ranks(0, 6)
+        rank(1, RANK_AT + 4 * PAGE)
 
         ks = sb([P, N], U8, "ks")
         nc.vector.tensor_copy(ks[:], ks_pool[:].indirect(slots[:]))
         kw = []
         for g in range(PAGES):
-            words = sb([P, PAGE], U32, "kw%d" % g)
+            words = placed([P, PAGE], U32, "kw%d" % g, KW_AT + 4 * PACK * NQ * g)
             nc.vector.tensor_copy(words[:], kw_pool[:].indirect(page_slots(g)))
             kw.append(words)
-        vs_rows = placed([P, N], F32, "vs_rows", 0)
-        nc.vector.tensor_copy(vs_rows[:], vs_pool[:].indirect(slots[:]))
-        vs_cols = []
-        for g in range(PAGES):
-            c = sb([P, PACK], F32, "vs_cols%d" % g)
-            nc.sync.dma_start(c[:], vs_rows[ROW:P, g * PAGE : (g + 1) * PAGE])
-            vs_cols.append(c)
+        vw = sb([P, PAGES * DV], U32, "vw")
+        nc.vector.tensor_copy(vw[:], vw_pool[:].indirect(vcols[:]))
 
         across = {}
         neg = {}
         x = {}
+        scores = {}
+        down = {}
+        low = [MASKED] * Q_TILES
 
         def hide(g):
-            across[g] = sb([P, PACK, NQ], F32, "across%d" % g)
             for j in range(PACK):
-                nc.scalar.activation(across[g][:, j, :], q_rows[:], ACT.Relu, bias=rank_cols[g][:, j : j + 1], scale=STEEP)
+                across[g, j] = placed([P, NQ], F32, "across%d_%d" % (g, j), ACROSS_AT + 4 * NQ * (PACK * g + j))
+                nc.scalar.activation(across[g, j][:], q_rows[:], ACT.Relu, bias=rank_cols[g][:, j : j + 1], scale=STEEP)
 
         def open_sums(g):
             for u in range(Q_TILES):
@@ -152,17 +159,17 @@ def tile_attend_pkv8q_soft_draft_kernel(
             for j in range(PACK):
                 for u in range(Q_TILES):
                     nc.tensor.matmul(
-                        x[u, g][:, j * P : (j + 1) * P], across[g][:, j, u * P : (u + 1) * P], ident[:],
+                        x[u, g][:, j * P : (j + 1) * P], across[g, j][:, u * P : (u + 1) * P], ident[:],
                         start=(j == 0), stop=False, is_transpose=True,
                     )
 
         def score(g, first_bank):
             for half_page in range(2):
-                scores = bank([P, 2, NQ], "scores", first_bank + half_page)
+                scores[g, half_page] = bank([P, 2, NQ], "scores", first_bank + half_page)
                 for jj in range(2):
                     j = 2 * half_page + jj
                     nc.tensor.matmul_mx(
-                        out=scores[:, jj, :],
+                        out=scores[g, half_page][:, jj, :],
                         lhsT=kw[g][:, j * P : (j + 1) * P].bitcast(FP8X4),
                         lhsT_scale=ks[:, g * PAGE + j * P : g * PAGE + (j + 1) * P],
                         rhs=qw[:].bitcast(FP8X4),
@@ -170,8 +177,12 @@ def tile_attend_pkv8q_soft_draft_kernel(
                         start=True,
                         stop=True,
                     )
-                neg[g, half_page] = sb([P, 2, NQ], F32, "neg%d_%d" % (g, half_page))
-                nc.scalar.activation(neg[g, half_page][:], scores[:], ACT.Copy, scale=-1.0)
+
+        def negate(g):
+            for half_page in range(2):
+                at = NEG_AT + 4 * PAGE * (2 * NEG_SLOT[g] + half_page)
+                neg[g, half_page] = placed([P, 2, NQ], F32, "neg%d_%d" % (g, half_page), at)
+                nc.scalar.activation(neg[g, half_page][:], scores[g, half_page][:], ACT.Copy, scale=-1.0)
 
         def close_sums(g):
             for half_page in range(2):
@@ -183,24 +194,9 @@ def tile_attend_pkv8q_soft_draft_kernel(
                             start=False, stop=(j == PACK - 1), is_transpose=True,
                         )
 
-        hide(0)
-        open_sums(0)
-        hide(1)
-        open_sums(1)
-        score(0, 6)
-        hide(2)
-        score(1, 4)
-        close_sums(0)
-        score(2, 6)
-        close_sums(1)
-        open_sums(2)
-        close_sums(2)
-
-        down = {}
-        low = [MASKED] * Q_TILES
-        for g in range(PAGES):
+        def lowest(g, at):
             for u in range(Q_TILES):
-                down[u, g] = placed([P, PACK, P], F32, "down%d_%d" % (u, g), VS_AT + 4 * PAGE * (Q_TILES * g + u))
+                down[u, g] = placed([P, PACK, P], F32, "down%d_%d" % (u, g), at + 4 * PAGE * u)
                 lower = sb([P, 1], F32, "low%d_%d" % (u, g))
                 nc.vector.tensor_scalar(
                     down[u, g][:], x[u, g][:].rearrange("q (s t) -> q t s", t=PACK), MASKED, low[u],
@@ -208,9 +204,34 @@ def tile_attend_pkv8q_soft_draft_kernel(
                 )
                 low[u] = lower[:]
 
-        vw = placed([P, PAGES * DV], U32, "vw", VS_AT + 8 * N)
-        nc.vector.tensor_copy(vw[:], vw_pool[:].indirect(vcols[:]))
-        vsc = placed([P, PAGES * DV], U8, "vsc", VS_AT + 9 * N)
+        hide(0)
+        open_sums(0)
+        rank(2, ACROSS_AT)
+        score(0, 6)
+        negate(0)
+        turn_ranks(1, 5)
+        score(1, 4)
+        close_sums(0)
+        lowest(0, 0)
+        vs_rows = placed([P, N], F32, "vs_rows", NEG_AT)
+        nc.vector.tensor_copy(vs_rows[:], vs_pool[:].indirect(slots[:]))
+        vs_cols = []
+        for g in range(PAGES):
+            c = sb([P, PACK], F32, "vs_cols%d" % g)
+            nc.sync.dma_start(c[:], vs_rows[0:1, g * PAGE : (g + 1) * PAGE])
+            vs_cols.append(c)
+        turn_ranks(2, 6)
+        score(2, 6)
+        for g in range(1, PAGES):
+            hide(g)
+            if g == 1:
+                open_sums(g)
+            negate(g)
+            if g == 2:
+                open_sums(g)
+            close_sums(g)
+            lowest(g, VS_AT + 4 * PAGE * Q_TILES * g)
+        vsc = placed([P, PAGES * DV], U8, "vsc", NEG_AT + 4 * PAGE * 2 * NEG_SLOT[2])
         nc.vector.tensor_copy(vsc[:], vsc_pool[:].indirect(vcols[:]))
 
         units = [(u, g) for u in range(Q_TILES) for g in range(PAGES)]

@@ -12,7 +12,7 @@ POOL_PAGES = T // PAGE
 Q_TILES = NQ // P
 ROW = P - 1
 MASKED = 30000.0
-SLOPE = 2.0 ** -15
+SLOPE = 2.0 ** -17
 STEEP = 2.0 ** 126
 
 ROW_AT = 4 * T
@@ -20,11 +20,6 @@ VS_AT = ROW_AT + 4 * T
 KS_AT = VS_AT + 4 * T
 P_AT = KS_AT + T
 NEG_AT = P_AT + 4 * PAGE * (Q_TILES * PAGES + 1)
-
-NEG_SLOT = [0, 2, 3]
-RANK_AT = NEG_AT + 4 * PAGE * 8
-KW_AT = RANK_AT + 4 * PAGE * 2 + 4 * PACK * NQ
-ACROSS_AT = KW_AT + 4 * PACK * NQ * PAGES
 
 FLOPS = 2 * NQ * N * D + 2 * NQ * N * DV
 
@@ -89,13 +84,13 @@ def tile_attend_pkv8q_soft_draft_kernel(
         nc.sync.dma_start(qw[:].bitcast(I32), q_words[0, 0].rearrange("g q r -> g (q r)").bitcast(I32))
         for quad in range(4):
             nc.sync.dma_start(scale_rows(qs, quad), q_scales[0, 0, 4 * quad : 4 * quad + 4, :].bitcast(I32))
+        vs_pool = placed([P, T], F32, "vs_pool", VS_AT)
+        nc.sync.dma_start(vs_pool[:], vs)
         vw_pool = sb([P, POOL_PAGES * DV], U32, "vw_pool")
         nc.sync.dma_start(
             vw_pool[:].bitcast(I32).rearrange("g (u e) -> g u e", e=DV),
             v_words.rearrange("u g e r -> g u (e r)").bitcast(I32),
         )
-        vs_pool = placed([P, T], F32, "vs_pool", VS_AT)
-        nc.sync.dma_start(vs_pool[:], vs)
         for quad in range(4):
             nc.sync.dma_start(
                 scale_rows(vsc_pool, quad).rearrange("f (u e) -> f u e", u=POOL_PAGES),
@@ -113,33 +108,26 @@ def tile_attend_pkv8q_soft_draft_kernel(
         q_rows = sb([P, NQ], F32, "q_rows")
         nc.scalar.activation(q_rows[:], spread[:], ACT.Copy, scale=1.0 - SLOPE / 8)
 
-        rank_row = {}
-        rank_cols = {}
-
-        def rank(g, at):
-            rank_row[g] = placed([P, PAGE], F32, "rank_row%d" % g, at)
-            nc.scalar.activation(rank_row[g][:], pos_pool[:].indirect(page_slots(g)), ACT.Sigmoid, scale=-SLOPE)
-
-        def turn_ranks(g, number):
-            turned = bank([P, PACK, P], "turned", number)
+        rank_cols = []
+        for g in range(PAGES):
+            rank_row = sb([P, PAGE], F32, "rank_row%d" % g)
+            nc.scalar.activation(rank_row[:], pos_pool[:].indirect(page_slots(g)), ACT.Sigmoid, scale=-SLOPE)
+            turned = bank([P, PACK, P], "turned", 6 - g)
             for j in range(PACK):
-                nc.tensor.transpose(turned[:, j, :], rank_row[g][:, j * P : (j + 1) * P], ident[:])
-            rank_cols[g] = placed([P, PACK], F32, "rank_cols%d" % g, KW_AT + 4 * PACK * NQ * (g - 1) + (4 * PAGE if g != 1 else 0))
-            nc.scalar.activation(rank_cols[g][:], turned[:, :, ROW], ACT.Copy, scale=-STEEP)
-
-        rank(0, RANK_AT)
-        turn_ranks(0, 6)
-        rank(1, RANK_AT + 4 * PAGE)
+                nc.tensor.transpose(turned[:, j, :], rank_row[:, j * P : (j + 1) * P], ident[:])
+            cols = sb([P, PACK], F32, "rank_cols%d" % g)
+            nc.scalar.activation(cols[:], turned[:, :, ROW], ACT.Copy, scale=-STEEP)
+            rank_cols.append(cols)
 
         ks = sb([P, N], U8, "ks")
         nc.vector.tensor_copy(ks[:], ks_pool[:].indirect(slots[:]))
         kw = []
         for g in range(PAGES):
-            words = placed([P, PAGE], U32, "kw%d" % g, KW_AT + 4 * PACK * NQ * g)
+            words = sb([P, PAGE], U32, "kw%d" % g)
             nc.vector.tensor_copy(words[:], kw_pool[:].indirect(page_slots(g)))
             kw.append(words)
-        vw = sb([P, PAGES * DV], U32, "vw")
-        nc.vector.tensor_copy(vw[:], vw_pool[:].indirect(vcols[:]))
+        vs_rows = placed([P, N], F32, "vs_rows", 0)
+        nc.vector.tensor_copy(vs_rows[:], vs_pool[:].indirect(slots[:]))
 
         across = {}
         neg = {}
@@ -150,12 +138,12 @@ def tile_attend_pkv8q_soft_draft_kernel(
 
         def hide(g):
             for j in range(PACK):
-                across[g, j] = placed([P, NQ], F32, "across%d_%d" % (g, j), ACROSS_AT + 4 * NQ * (PACK * g + j))
+                across[g, j] = sb([P, NQ], F32, "across%d_%d" % (g, j))
                 nc.scalar.activation(across[g, j][:], q_rows[:], ACT.Relu, bias=rank_cols[g][:, j : j + 1], scale=STEEP)
 
         def open_sums(g):
             for u in range(Q_TILES):
-                x[u, g] = bank([P, PAGE], "x", Q_TILES * g + u)
+                x[u, g] = bank([P, PAGE], "x", (0, 6, 4)[g] + u)
             for j in range(PACK):
                 for u in range(Q_TILES):
                     nc.tensor.matmul(
@@ -180,7 +168,7 @@ def tile_attend_pkv8q_soft_draft_kernel(
 
         def negate(g):
             for half_page in range(2):
-                at = NEG_AT + 4 * PAGE * (2 * NEG_SLOT[g] + half_page)
+                at = NEG_AT + 4 * PAGE * (2 * g + half_page)
                 neg[g, half_page] = placed([P, 2, NQ], F32, "neg%d_%d" % (g, half_page), at)
                 nc.scalar.activation(neg[g, half_page][:], scores[g, half_page][:], ACT.Copy, scale=-1.0)
 
@@ -194,45 +182,30 @@ def tile_attend_pkv8q_soft_draft_kernel(
                             start=False, stop=(j == PACK - 1), is_transpose=True,
                         )
 
-        def lowest(g, at):
+        def lowest(g):
             for u in range(Q_TILES):
-                down[u, g] = placed([P, PACK, P], F32, "down%d_%d" % (u, g), at + 4 * PAGE * u)
+                down[u, g] = placed([P, 2, P, 2], F32, "down%d_%d" % (u, g), VS_AT + 4 * PAGE * (Q_TILES * g + u))
                 lower = sb([P, 1], F32, "low%d_%d" % (u, g))
                 nc.vector.tensor_scalar(
-                    down[u, g][:], x[u, g][:].rearrange("q (s t) -> q t s", t=PACK), MASKED, low[u],
+                    down[u, g][:], x[u, g][:].rearrange("q (s h e) -> q h s e", h=2, e=2), MASKED, low[u],
                     op0=ALU.min, op1=ALU.min, accum_out=lower[:],
                 )
                 low[u] = lower[:]
 
-        hide(0)
-        open_sums(0)
-        rank(2, ACROSS_AT)
-        score(0, 6)
-        negate(0)
-        turn_ranks(1, 5)
-        score(1, 4)
-        close_sums(0)
-        lowest(0, 0)
-        vs_rows = placed([P, N], F32, "vs_rows", NEG_AT)
-        nc.vector.tensor_copy(vs_rows[:], vs_pool[:].indirect(slots[:]))
-        vs_cols = []
         for g in range(PAGES):
-            c = sb([P, PACK], F32, "vs_cols%d" % g)
-            nc.sync.dma_start(c[:], vs_rows[0:1, g * PAGE : (g + 1) * PAGE])
-            vs_cols.append(c)
-        turn_ranks(2, 6)
-        score(2, 6)
-        for g in range(1, PAGES):
             hide(g)
-            if g == 1:
-                open_sums(g)
+        open_sums(0)
+        for g in range(PAGES):
+            score(g, 6 - 2 * g)
+        for g in range(PAGES):
             negate(g)
-            if g == 2:
+            if g:
                 open_sums(g)
             close_sums(g)
-            lowest(g, VS_AT + 4 * PAGE * Q_TILES * g)
-        vsc = placed([P, PAGES * DV], U8, "vsc", NEG_AT + 4 * PAGE * 2 * NEG_SLOT[2])
-        nc.vector.tensor_copy(vsc[:], vsc_pool[:].indirect(vcols[:]))
+        for g in range(PAGES):
+            lowest(g)
+        vw = placed([P, PAGES * DV], U32, "vw", NEG_AT + 4 * PAGE * 4)
+        nc.vector.tensor_copy(vw[:], vw_pool[:].indirect(vcols[:]))
 
         units = [(u, g) for u in range(Q_TILES) for g in range(PAGES)]
         sums = [sb([P, PAGES], F32, "sums%d" % u) for u in range(Q_TILES)]
@@ -241,37 +214,41 @@ def tile_attend_pkv8q_soft_draft_kernel(
 
         def weigh(k):
             u, g = units[k]
-            p = placed([P, PACK, P], F32, "p%d" % k, P_AT + 4 * PAGE * k)
+            p = placed([P, 2, P, 2], F32, "p%d" % k, P_AT + 4 * PAGE * k)
             nc.scalar.activation(p[:], down[u, g][:], ACT.Exp, bias=low[u], scale=-1.0, accum_out=sums[u][:, g : g + 1])
-            turned = bank([P, PACK, P], "turned", (6 + k) % 8)
-            for t in range(PACK):
-                nc.tensor.transpose(turned[:, t, :], p[:, t, :], ident[:])
-            w = sb([P, P, PACK], BF16, "w%d" % k)
+            w = sb([P, 2, P, 2], BF16, "w%d" % k)
             nc.vector.tensor_tensor(
-                w[:],
-                turned[:].rearrange("s t q -> s q t"),
-                vs_cols[g][:].unsqueeze(1).to_broadcast([P, P, PACK]),
-                ALU.mult,
+                w[:], p[:], vs_rows[:, g * PAGE : (g + 1) * PAGE].rearrange("q (s h e) -> q h s e", h=2, e=2), ALU.mult
             )
             weights.append(w)
 
         def quantise(k):
-            codes = placed([P, P], U32, "codes%d" % k, P_AT + 4 * PAGE * (k + 1))
+            pairs = weights[k][:].rearrange("q h s e -> q (h s e)").bitcast(F32)
+            turned = bank([P, 2, P], "turned", (0, 1, 2, 3, 6, 7)[k])
+            for h in range(2):
+                nc.tensor.transpose(turned[:, h, :], pairs[:, h * P : (h + 1) * P], ident[:])
+            grouped = sb([P, P * PACK], BF16, "grouped%d" % k)
+            nc.scalar.copy(grouped[:].bitcast(F32).rearrange("s (q h) -> s q h", h=2), turned[:].rearrange("s h q -> s q h"))
+            codes = sb([P, P], U32, "codes%d" % k)
             scales = sb([P, P], U8, "scales%d" % k)
-            nc.vector.quantize_mx(out=codes[:].bitcast(FP8X4), scales=scales[:], in_=weights[k][:].rearrange("s q t -> s (q t)"))
+            nc.vector.quantize_mx(out=codes[:].bitcast(FP8X4), scales=scales[:], in_=grouped[:])
             quantised.append((codes, scales))
 
-        weigh(0)
-        for k in range(1, len(units)):
+        lag = 2
+        for k in range(len(units)):
             weigh(k)
-            quantise(k - 1)
+            if k >= lag:
+                quantise(k - lag)
+        vsc = placed([P, PAGES * DV], U8, "vsc", P_AT + 4 * PAGE * (len(units) - 2))
+        nc.vector.tensor_copy(vsc[:], vsc_pool[:].indirect(vcols[:]))
         total = sb([P, Q_TILES], F32, "total")
         for u in range(Q_TILES):
             parts = sb([P, PAGES], F32, "parts%d" % u)
             nc.scalar.activation(parts[:], sums[u][:], ACT.Copy, accum_out=total[:, u : u + 1])
         inverse = sb([P, Q_TILES], F32, "inverse")
         nc.vector.reciprocal(inverse[:], total[:])
-        quantise(len(units) - 1)
+        for k in range(len(units) - lag, len(units)):
+            quantise(k)
 
         for u in range(Q_TILES):
             y = bank([P, DV], "y", 4 + u)

@@ -21,6 +21,10 @@ KS_AT = VS_AT + 4 * T
 P_AT = KS_AT + T
 NEG_AT = P_AT + 4 * PAGE * (Q_TILES * PAGES + 1)
 
+KW_AT = NEG_AT + 4 * PAGE * 2 * PAGES
+
+RANK_AT = KW_AT + 4 * PAGE * PAGES
+
 FLOPS = 2 * NQ * N * D + 2 * NQ * N * DV
 
 F32 = mybir.dt.float32
@@ -55,47 +59,49 @@ def tile_attend_pkv8q_soft_draft_kernel(
         def scale_rows(plane, quad):
             return plane[32 * quad : 32 * quad + 4, :].bitcast(I32)
 
+        def dealt(row):
+            return row.rearrange("q (s h e) -> q h s e", h=2, e=2)
+
         def page_slots(g):
             return slots[:, g * PAGE // 16 : (g + 1) * PAGE // 16]
 
+        vcols = keep.tile([P, PAGES * DV // 16], U16, name="vcols")
+        nc.sync.dma_start(vcols[:], voffs)
         slots = keep.tile([P, N // 16], U16, name="slots")
         nc.sync.dma_start(slots[:], offs)
         pos_pool = placed([P, T], F32, "pos_pool", ROW_AT)
         nc.sync.dma_start(pos_pool[ROW:P, :], pos[0:1, :])
-        kw_pool = placed([P, T], U32, "kw_pool", 0)
-        nc.sync.dma_start(kw_pool[:].bitcast(I32), k_words[0].rearrange("g t r -> g (t r)").bitcast(I32), max_dma_last_dim=4096)
-        vcols = keep.tile([P, PAGES * DV // 16], U16, name="vcols")
-        nc.sync.dma_start(vcols[:], voffs)
-
         qpos_cols = sb([P, Q_TILES], F32, "qpos_cols")
         with nc.allow_non_contiguous_dma(reason="one place a partition and query tile"):
-            nc.scalar.dma_start(qpos_cols[:], qpos[0].rearrange("(u p) o -> p (u o)", p=P))
-
-        ks_pool = placed([P, T], U8, "ks_pool", KS_AT)
-        nc.vector.memset(ks_pool[:].bitcast(I32), 0)
-        for quad in range(4):
-            nc.scalar.dma_start(scale_rows(ks_pool, quad), k_scales[0, 4 * quad : 4 * quad + 4, :].bitcast(I32))
-        qs = sb([P, NQ], U8, "qs")
-        nc.vector.memset(qs[:].bitcast(I32), 0)
-        vsc_pool = sb([P, POOL_PAGES * DV], U8, "vsc_pool")
-        nc.vector.memset(vsc_pool[:].bitcast(I32), 0)
-        nc.vector.memset(pos_pool[0:ROW, :], 0.0)
-        qw = sb([P, NQ], U32, "qw")
-        nc.sync.dma_start(qw[:].bitcast(I32), q_words[0, 0].rearrange("g q r -> g (q r)").bitcast(I32))
-        for quad in range(4):
-            nc.sync.dma_start(scale_rows(qs, quad), q_scales[0, 0, 4 * quad : 4 * quad + 4, :].bitcast(I32))
-        vs_pool = placed([P, T], F32, "vs_pool", VS_AT)
-        nc.sync.dma_start(vs_pool[:], vs)
+            nc.sync.dma_start(qpos_cols[:], qpos[0].rearrange("(u p) o -> p (u o)", p=P))
         vw_pool = sb([P, POOL_PAGES * DV], U32, "vw_pool")
         nc.sync.dma_start(
             vw_pool[:].bitcast(I32).rearrange("g (u e) -> g u e", e=DV),
             v_words.rearrange("u g e r -> g u (e r)").bitcast(I32),
         )
+
+        ks_pool = placed([P, T], U8, "ks_pool", KS_AT)
+        nc.vector.memset(ks_pool[:].bitcast(I32), 0)
+        for quad in range(4):
+            nc.sync.dma_start(scale_rows(ks_pool, quad), k_scales[0, 4 * quad : 4 * quad + 4, :].bitcast(I32))
+        kw_pool = placed([P, T], U32, "kw_pool", 0)
+        nc.sync.dma_start(kw_pool[:].bitcast(I32), k_words[0].rearrange("g t r -> g (t r)").bitcast(I32))
+        qw = sb([P, NQ], U32, "qw")
+        nc.sync.dma_start(qw[:].bitcast(I32), q_words[0, 0].rearrange("g q r -> g (q r)").bitcast(I32))
+        qs = sb([P, NQ], U8, "qs")
+        nc.vector.memset(qs[:].bitcast(I32), 0)
+        for quad in range(4):
+            nc.sync.dma_start(scale_rows(qs, quad), q_scales[0, 0, 4 * quad : 4 * quad + 4, :].bitcast(I32))
+        vs_pool = placed([P, T], F32, "vs_pool", VS_AT)
+        nc.sync.dma_start(vs_pool[:], vs)
+        vsc_pool = sb([P, POOL_PAGES * DV], U8, "vsc_pool")
+        nc.vector.memset(vsc_pool[:].bitcast(I32), 0)
         for quad in range(4):
             nc.sync.dma_start(
                 scale_rows(vsc_pool, quad).rearrange("f (u e) -> f u e", u=POOL_PAGES),
                 v_scales[:, 4 * quad : 4 * quad + 4, :].rearrange("u f e -> f u e").bitcast(I32),
             )
+        nc.vector.memset(pos_pool[0:ROW, :], 0.0)
 
         ident = sb([P, P], F32, "ident")
         make_identity(nc, ident[:])
@@ -108,26 +114,37 @@ def tile_attend_pkv8q_soft_draft_kernel(
         q_rows = sb([P, NQ], F32, "q_rows")
         nc.scalar.activation(q_rows[:], spread[:], ACT.Copy, scale=1.0 - SLOPE / 8)
 
-        rank_cols = []
-        for g in range(PAGES):
-            rank_row = sb([P, PAGE], F32, "rank_row%d" % g)
-            nc.scalar.activation(rank_row[:], pos_pool[:].indirect(page_slots(g)), ACT.Sigmoid, scale=-SLOPE)
-            turned = bank([P, PACK, P], "turned", 6 - g)
-            for j in range(PACK):
-                nc.tensor.transpose(turned[:, j, :], rank_row[:, j * P : (j + 1) * P], ident[:])
-            cols = sb([P, PACK], F32, "rank_cols%d" % g)
-            nc.scalar.activation(cols[:], turned[:, :, ROW], ACT.Copy, scale=-STEEP)
-            rank_cols.append(cols)
+        limit = sb([P, Q_TILES], F32, "limit")
+        nc.scalar.activation(limit[:], q_rank[:], ACT.Copy, scale=STEEP * (1.0 - SLOPE / 8))
 
+        rank_cols = {}
+        turned_ranks = {}
+
+        def rank(g, at):
+            rank_row = placed([P, PAGE], F32, "rank_row%d" % g, at)
+            nc.scalar.activation(rank_row[:], pos_pool[:].indirect(page_slots(g)), ACT.Sigmoid, scale=-SLOPE)
+            turned_ranks[g] = bank([P, PACK, P], "turned", (6, 4, 3)[g])
+            for j in range(PACK):
+                nc.tensor.transpose(turned_ranks[g][:, j, :], rank_row[:, j * P : (j + 1) * P], ident[:])
+
+        def columns(g):
+            rank_cols[g] = sb([P, PACK], F32, "rank_cols%d" % g)
+            nc.scalar.activation(rank_cols[g][:], turned_ranks[g][:, :, ROW], ACT.Copy, scale=-STEEP)
+
+        for g in range(2):
+            rank(g, RANK_AT + 4 * PAGE * g)
+        for g in range(2):
+            columns(g)
+
+        vw = sb([P, PAGES * DV], U32, "vw")
+        nc.vector.tensor_copy(vw[:], vw_pool[:].indirect(vcols[:]))
         ks = sb([P, N], U8, "ks")
         nc.vector.tensor_copy(ks[:], ks_pool[:].indirect(slots[:]))
         kw = []
         for g in range(PAGES):
-            words = sb([P, PAGE], U32, "kw%d" % g)
+            words = placed([P, PAGE], U32, "kw%d" % g, KW_AT + 4 * PAGE * g)
             nc.vector.tensor_copy(words[:], kw_pool[:].indirect(page_slots(g)))
             kw.append(words)
-        vs_rows = placed([P, N], F32, "vs_rows", 0)
-        nc.vector.tensor_copy(vs_rows[:], vs_pool[:].indirect(slots[:]))
 
         across = {}
         neg = {}
@@ -143,7 +160,7 @@ def tile_attend_pkv8q_soft_draft_kernel(
 
         def open_sums(g):
             for u in range(Q_TILES):
-                x[u, g] = bank([P, PAGE], "x", (0, 6, 4)[g] + u)
+                x[u, g] = bank([P, PAGE], "x", 2 * (g - 1) + u)
             for j in range(PACK):
                 for u in range(Q_TILES):
                     nc.tensor.matmul(
@@ -182,30 +199,56 @@ def tile_attend_pkv8q_soft_draft_kernel(
                             start=False, stop=(j == PACK - 1), is_transpose=True,
                         )
 
-        def lowest(g):
+        def lowest(g, at, sources):
             for u in range(Q_TILES):
-                down[u, g] = placed([P, 2, P, 2], F32, "down%d_%d" % (u, g), VS_AT + 4 * PAGE * (Q_TILES * g + u))
+                down[u, g] = placed([P, 2, P, 2], F32, "down%d_%d" % (u, g), at + 4 * PAGE * u)
                 lower = sb([P, 1], F32, "low%d_%d" % (u, g))
                 nc.vector.tensor_scalar(
-                    down[u, g][:], x[u, g][:].rearrange("q (s h e) -> q h s e", h=2, e=2), MASKED, low[u],
+                    down[u, g][:], sources[u], MASKED, low[u],
                     op0=ALU.min, op1=ALU.min, accum_out=lower[:],
                 )
                 low[u] = lower[:]
 
-        for g in range(PAGES):
-            hide(g)
-        open_sums(0)
-        for g in range(PAGES):
-            score(g, 6 - 2 * g)
-        for g in range(PAGES):
-            negate(g)
-            if g:
-                open_sums(g)
-            close_sums(g)
-        for g in range(PAGES):
-            lowest(g)
-        vw = placed([P, PAGES * DV], U32, "vw", NEG_AT + 4 * PAGE * 4)
-        nc.vector.tensor_copy(vw[:], vw_pool[:].indirect(vcols[:]))
+        spread_ranks = bank([P, PAGE], "spread", 5)
+        for j in range(PACK):
+            nc.tensor.transpose(spread_ranks[:, j * P : (j + 1) * P], rank_cols[0][:, j : j + 1].to_broadcast([P, P]), ident[:])
+        hide(1)
+        open_sums(1)
+        hidden = []
+        summed = []
+        for u in range(Q_TILES):
+            term = sb([P, 2, P, 2], F32, "hidden%d" % u)
+            nc.scalar.activation(term[:], dealt(spread_ranks[:]), ACT.Relu, bias=limit[:, u : u + 1])
+            hidden.append(term)
+        for u in range(Q_TILES):
+            a = bank([P, PAGE], "a", 6 + u)
+            nc.tensor.matmul_mx(
+                out=a[:],
+                lhsT=qw[:, u * P : (u + 1) * P].bitcast(FP8X4),
+                lhsT_scale=qs[:, u * P : (u + 1) * P],
+                rhs=kw[0][:].bitcast(FP8X4),
+                rhs_scale=ks[:, 0:PAGE],
+                start=True,
+                stop=True,
+            )
+            summed.append(placed([P, 2, P, 2], F32, "summed%d" % u, 4 * N * u))
+            nc.vector.tensor_tensor(summed[u][:], hidden[u][:], dealt(a[:]), ALU.subtract)
+        lowest(0, NEG_AT, [tile[:] for tile in summed])
+        vs_rows = placed([P, N], F32, "vs_rows", 0)
+        nc.vector.tensor_copy(vs_rows[:], vs_pool[:].indirect(slots[:]))
+
+        score(1, 4)
+        rank(2, KW_AT)
+        negate(1)
+        columns(2)
+        hide(2)
+        score(2, 6)
+        close_sums(1)
+        open_sums(2)
+        negate(2)
+        close_sums(2)
+        for g in range(1, PAGES):
+            lowest(g, VS_AT + 4 * PAGE * Q_TILES * g, [dealt(x[u, g][:]) for u in range(Q_TILES)])
 
         units = [(u, g) for u in range(Q_TILES) for g in range(PAGES)]
         sums = [sb([P, PAGES], F32, "sums%d" % u) for u in range(Q_TILES)]
@@ -218,7 +261,7 @@ def tile_attend_pkv8q_soft_draft_kernel(
             nc.scalar.activation(p[:], down[u, g][:], ACT.Exp, bias=low[u], scale=-1.0, accum_out=sums[u][:, g : g + 1])
             w = sb([P, 2, P, 2], BF16, "w%d" % k)
             nc.vector.tensor_tensor(
-                w[:], p[:], vs_rows[:, g * PAGE : (g + 1) * PAGE].rearrange("q (s h e) -> q h s e", h=2, e=2), ALU.mult
+                w[:], p[:], dealt(vs_rows[:, g * PAGE : (g + 1) * PAGE]), ALU.mult
             )
             weights.append(w)
 
@@ -234,21 +277,19 @@ def tile_attend_pkv8q_soft_draft_kernel(
             nc.vector.quantize_mx(out=codes[:].bitcast(FP8X4), scales=scales[:], in_=grouped[:])
             quantised.append((codes, scales))
 
-        lag = 2
         for k in range(len(units)):
             weigh(k)
-            if k >= lag:
-                quantise(k - lag)
         vsc = placed([P, PAGES * DV], U8, "vsc", P_AT + 4 * PAGE * (len(units) - 2))
         nc.vector.tensor_copy(vsc[:], vsc_pool[:].indirect(vcols[:]))
+        for k in range(len(units) - 1):
+            quantise(k)
         total = sb([P, Q_TILES], F32, "total")
         for u in range(Q_TILES):
             parts = sb([P, PAGES], F32, "parts%d" % u)
             nc.scalar.activation(parts[:], sums[u][:], ACT.Copy, accum_out=total[:, u : u + 1])
         inverse = sb([P, Q_TILES], F32, "inverse")
         nc.vector.reciprocal(inverse[:], total[:])
-        for k in range(len(units) - lag, len(units)):
-            quantise(k)
+        quantise(len(units) - 1)
 
         for u in range(Q_TILES):
             y = bank([P, DV], "y", 4 + u)

@@ -65,20 +65,13 @@ def tile_attend_pkv8q_soft_draft_kernel(
         def page_slots(g):
             return slots[:, g * PAGE // 16 : (g + 1) * PAGE // 16]
 
-        vcols = keep.tile([P, PAGES * DV // 16], U16, name="vcols")
-        nc.sync.dma_start(vcols[:], voffs)
         slots = keep.tile([P, N // 16], U16, name="slots")
         nc.sync.dma_start(slots[:], offs)
         pos_pool = placed([P, T], F32, "pos_pool", ROW_AT)
         nc.sync.dma_start(pos_pool[ROW:P, :], pos[0:1, :])
         qpos_cols = sb([P, Q_TILES], F32, "qpos_cols")
         with nc.allow_non_contiguous_dma(reason="one place a partition and query tile"):
-            nc.sync.dma_start(qpos_cols[:], qpos[0].rearrange("(u p) o -> p (u o)", p=P))
-        vw_pool = sb([P, POOL_PAGES * DV], U32, "vw_pool")
-        nc.sync.dma_start(
-            vw_pool[:].bitcast(I32).rearrange("g (u e) -> g u e", e=DV),
-            v_words.rearrange("u g e r -> g u (e r)").bitcast(I32),
-        )
+            nc.scalar.dma_start(qpos_cols[:], qpos[0].rearrange("(u p) o -> p (u o)", p=P))
 
         ks_pool = placed([P, T], U8, "ks_pool", KS_AT)
         nc.vector.memset(ks_pool[:].bitcast(I32), 0)
@@ -94,6 +87,13 @@ def tile_attend_pkv8q_soft_draft_kernel(
             nc.sync.dma_start(scale_rows(qs, quad), q_scales[0, 0, 4 * quad : 4 * quad + 4, :].bitcast(I32))
         vs_pool = placed([P, T], F32, "vs_pool", VS_AT)
         nc.sync.dma_start(vs_pool[:], vs)
+        vcols = keep.tile([P, PAGES * DV // 16], U16, name="vcols")
+        nc.sync.dma_start(vcols[:], voffs)
+        vw_pool = sb([P, POOL_PAGES * DV], U32, "vw_pool")
+        nc.sync.dma_start(
+            vw_pool[:].bitcast(I32).rearrange("g (u e) -> g u e", e=DV),
+            v_words.rearrange("u g e r -> g u (e r)").bitcast(I32),
+        )
         vsc_pool = sb([P, POOL_PAGES * DV], U8, "vsc_pool")
         nc.vector.memset(vsc_pool[:].bitcast(I32), 0)
         for quad in range(4):
@@ -136,8 +136,6 @@ def tile_attend_pkv8q_soft_draft_kernel(
         for g in range(2):
             columns(g)
 
-        vw = sb([P, PAGES * DV], U32, "vw")
-        nc.vector.tensor_copy(vw[:], vw_pool[:].indirect(vcols[:]))
         ks = sb([P, N], U8, "ks")
         nc.vector.tensor_copy(ks[:], ks_pool[:].indirect(slots[:]))
         kw = []
@@ -236,6 +234,8 @@ def tile_attend_pkv8q_soft_draft_kernel(
         lowest(0, NEG_AT, [tile[:] for tile in summed])
         vs_rows = placed([P, N], F32, "vs_rows", 0)
         nc.vector.tensor_copy(vs_rows[:], vs_pool[:].indirect(slots[:]))
+        vw = sb([P, PAGES * DV], U32, "vw")
+        nc.vector.tensor_copy(vw[:], vw_pool[:].indirect(vcols[:]))
 
         score(1, 4)
         rank(2, KW_AT)

@@ -234,11 +234,9 @@ def tile_attend_pkv8q_soft_draft_kernel(
         lowest(0, NEG_AT, [tile[:] for tile in summed])
         vs_rows = placed([P, N], F32, "vs_rows", 0)
         nc.vector.tensor_copy(vs_rows[:], vs_pool[:].indirect(slots[:]))
-        vw = sb([P, PAGES * DV], U32, "vw")
-        nc.vector.tensor_copy(vw[:], vw_pool[:].indirect(vcols[:]))
 
         score(1, 4)
-        rank(2, KW_AT)
+        rank(2, KW_AT + 4 * PAGE)
         negate(1)
         columns(2)
         hide(2)
@@ -250,46 +248,50 @@ def tile_attend_pkv8q_soft_draft_kernel(
         for g in range(1, PAGES):
             lowest(g, VS_AT + 4 * PAGE * Q_TILES * g, [dealt(x[u, g][:]) for u in range(Q_TILES)])
 
+        vw = placed([P, PAGES * DV], U32, "vw", VS_AT + 8 * N)
+        nc.vector.tensor_copy(vw[:], vw_pool[:].indirect(vcols[:]))
+
         units = [(u, g) for u in range(Q_TILES) for g in range(PAGES)]
-        sums = [sb([P, PAGES], F32, "sums%d" % u) for u in range(Q_TILES)]
+        sums = sb([P, Q_TILES, PAGES], F32, "sums")
         weights = []
         quantised = []
 
         def weigh(k):
             u, g = units[k]
             p = placed([P, 2, P, 2], F32, "p%d" % k, P_AT + 4 * PAGE * k)
-            nc.scalar.activation(p[:], down[u, g][:], ACT.Exp, bias=low[u], scale=-1.0, accum_out=sums[u][:, g : g + 1])
+            nc.scalar.activation(p[:], down[u, g][:], ACT.Exp, bias=low[u], scale=-1.0, accum_out=sums[:, u, g : g + 1])
             w = sb([P, 2, P, 2], BF16, "w%d" % k)
             nc.vector.tensor_tensor(
                 w[:], p[:], dealt(vs_rows[:, g * PAGE : (g + 1) * PAGE]), ALU.mult
             )
             weights.append(w)
 
-        def quantise(k):
-            pairs = weights[k][:].rearrange("q h s e -> q (h s e)").bitcast(F32)
-            turned = bank([P, 2, P], "turned", (0, 1, 2, 3, 6, 7)[k])
-            for h in range(2):
-                nc.tensor.transpose(turned[:, h, :], pairs[:, h * P : (h + 1) * P], ident[:])
-            grouped = sb([P, P * PACK], BF16, "grouped%d" % k)
-            nc.scalar.copy(grouped[:].bitcast(F32).rearrange("s (q h) -> s q h", h=2), turned[:].rearrange("s h q -> s q h"))
-            codes = sb([P, P], U32, "codes%d" % k)
-            scales = sb([P, P], U8, "scales%d" % k)
-            nc.vector.quantize_mx(out=codes[:].bitcast(FP8X4), scales=scales[:], in_=grouped[:])
-            quantised.append((codes, scales))
+        def quantise(first, count):
+            grouped = sb([P, count, P * PACK], BF16, "grouped%d" % first)
+            for i in range(count):
+                pairs = weights[first + i][:].rearrange("q h s e -> q (h s e)").bitcast(F32)
+                turned = bank([P, 2, P], "turned", (0, 1, 2, 3, 6, 7)[first + i])
+                for h in range(2):
+                    nc.tensor.transpose(turned[:, h, :], pairs[:, h * P : (h + 1) * P], ident[:])
+                nc.scalar.copy(grouped[:, i, :].bitcast(F32).rearrange("s (q h) -> s q h", h=2), turned[:].rearrange("s h q -> s q h"))
+            codes = sb([P, count * P], U32, "codes%d" % first)
+            scales = sb([P, count * P], U8, "scales%d" % first)
+            nc.vector.quantize_mx(out=codes[:].bitcast(FP8X4), scales=scales[:], in_=grouped[:].rearrange("s i c -> s (i c)"))
+            for i in range(count):
+                quantised.append((codes[:, i * P : (i + 1) * P], scales[:, i * P : (i + 1) * P]))
 
         for k in range(len(units)):
             weigh(k)
         vsc = placed([P, PAGES * DV], U8, "vsc", P_AT + 4 * PAGE * (len(units) - 2))
         nc.vector.tensor_copy(vsc[:], vsc_pool[:].indirect(vcols[:]))
-        for k in range(len(units) - 1):
-            quantise(k)
         total = sb([P, Q_TILES], F32, "total")
-        for u in range(Q_TILES):
-            parts = sb([P, PAGES], F32, "parts%d" % u)
-            nc.scalar.activation(parts[:], sums[u][:], ACT.Copy, accum_out=total[:, u : u + 1])
+        nc.vector.tensor_reduce(total[:], sums[:], mybir.AxisListType.X, ALU.add)
+        quantise(0, 2)
         inverse = sb([P, Q_TILES], F32, "inverse")
         nc.vector.reciprocal(inverse[:], total[:])
-        quantise(len(units) - 1)
+        quantise(2, 2)
+        quantise(4, 1)
+        quantise(5, 1)
 
         for u in range(Q_TILES):
             y = bank([P, DV], "y", 4 + u)
@@ -297,8 +299,8 @@ def tile_attend_pkv8q_soft_draft_kernel(
                 codes, scales = quantised[PAGES * u + g]
                 nc.tensor.matmul_mx(
                     out=y[:],
-                    lhsT=codes[:].bitcast(FP8X4),
-                    lhsT_scale=scales[:],
+                    lhsT=codes.bitcast(FP8X4),
+                    lhsT_scale=scales,
                     rhs=vw[:, g * DV : (g + 1) * DV].bitcast(FP8X4),
                     rhs_scale=vsc[:, g * DV : (g + 1) * DV],
                     start=(g == 0),

@@ -14,6 +14,7 @@ ROW = P - 1
 MASKED = 30000.0
 SLOPE = 2.0 ** -17
 STEEP = 2.0 ** 126
+PLAIN_STEEP = 2.0 ** 80
 
 ROW_AT = 4 * T
 VS_AT = ROW_AT + 4 * T
@@ -22,8 +23,7 @@ P_AT = KS_AT + T
 NEG_AT = P_AT + 4 * PAGE * (Q_TILES * PAGES + 1)
 
 KW_AT = NEG_AT + 4 * PAGE * 2 * PAGES
-
-RANK_AT = KW_AT + 4 * PAGE * PAGES
+ACROSS_AT = KW_AT + 4 * PAGE * PAGES
 
 FLOPS = 2 * NQ * N * D + 2 * NQ * N * DV
 
@@ -77,6 +77,7 @@ def tile_attend_pkv8q_soft_draft_kernel(
         nc.vector.memset(ks_pool[:].bitcast(I32), 0)
         for quad in range(4):
             nc.sync.dma_start(scale_rows(ks_pool, quad), k_scales[0, 4 * quad : 4 * quad + 4, :].bitcast(I32))
+        nc.vector.memset(pos_pool[0:ROW, :], 0.0)
         kw_pool = placed([P, T], U32, "kw_pool", 0)
         nc.sync.dma_start(kw_pool[:].bitcast(I32), k_words[0].rearrange("g t r -> g (t r)").bitcast(I32))
         qw = sb([P, NQ], U32, "qw")
@@ -101,7 +102,6 @@ def tile_attend_pkv8q_soft_draft_kernel(
                 scale_rows(vsc_pool, quad).rearrange("f (u e) -> f u e", u=POOL_PAGES),
                 v_scales[:, 4 * quad : 4 * quad + 4, :].rearrange("u f e -> f u e").bitcast(I32),
             )
-        nc.vector.memset(pos_pool[0:ROW, :], 0.0)
 
         ident = sb([P, P], F32, "ident")
         make_identity(nc, ident[:])
@@ -115,26 +115,20 @@ def tile_attend_pkv8q_soft_draft_kernel(
         nc.scalar.activation(q_rows[:], spread[:], ACT.Copy, scale=1.0 - SLOPE / 8)
 
         limit = sb([P, Q_TILES], F32, "limit")
-        nc.scalar.activation(limit[:], q_rank[:], ACT.Copy, scale=STEEP * (1.0 - SLOPE / 8))
+        nc.scalar.activation(limit[:], qpos_cols[:], ACT.Copy, scale=-PLAIN_STEEP)
 
-        rank_cols = {}
-        turned_ranks = {}
-
-        def rank(g, at):
-            rank_row = placed([P, PAGE], F32, "rank_row%d" % g, at)
-            nc.scalar.activation(rank_row[:], pos_pool[:].indirect(page_slots(g)), ACT.Sigmoid, scale=-SLOPE)
-            turned_ranks[g] = bank([P, PACK, P], "turned", (6, 4, 3)[g])
+        rows = [sb([P, PAGE], F32, "row%d" % g) for g in range(PAGES)]
+        nc.vector.tensor_copy(rows[0][:], pos_pool[:].indirect(page_slots(0)))
+        for g in range(1, PAGES):
+            nc.scalar.activation(rows[g][:], pos_pool[:].indirect(page_slots(g)), ACT.Sigmoid, scale=-SLOPE)
+        rank_cols = []
+        for g in range(PAGES):
+            turned = bank([P, PACK, P], "turned", (6, 4, 3)[g])
             for j in range(PACK):
-                nc.tensor.transpose(turned_ranks[g][:, j, :], rank_row[:, j * P : (j + 1) * P], ident[:])
-
-        def columns(g):
-            rank_cols[g] = sb([P, PACK], F32, "rank_cols%d" % g)
-            nc.scalar.activation(rank_cols[g][:], turned_ranks[g][:, :, ROW], ACT.Copy, scale=-STEEP)
-
-        for g in range(2):
-            rank(g, RANK_AT + 4 * PAGE * g)
-        for g in range(2):
-            columns(g)
+                nc.tensor.transpose(turned[:, j, :], rows[g][:, j * P : (j + 1) * P], ident[:])
+            cols = sb([P, PACK], F32, "rank_cols%d" % g)
+            nc.scalar.activation(cols[:], turned[:, :, ROW], ACT.Copy, scale=-STEEP if g else PLAIN_STEEP)
+            rank_cols.append(cols)
 
         ks = sb([P, N], U8, "ks")
         nc.vector.tensor_copy(ks[:], ks_pool[:].indirect(slots[:]))
@@ -151,15 +145,13 @@ def tile_attend_pkv8q_soft_draft_kernel(
         down = {}
         low = [MASKED] * Q_TILES
 
-        def hide(g):
-            for j in range(PACK):
-                across[g, j] = sb([P, NQ], F32, "across%d_%d" % (g, j))
+        def hide(g, blocks, at):
+            for i, j in enumerate(blocks):
+                across[g, j] = placed([P, NQ], F32, "across%d_%d" % (g, j), at + 4 * NQ * i)
                 nc.scalar.activation(across[g, j][:], q_rows[:], ACT.Relu, bias=rank_cols[g][:, j : j + 1], scale=STEEP)
 
-        def open_sums(g):
-            for u in range(Q_TILES):
-                x[u, g] = bank([P, PAGE], "x", 2 * (g - 1) + u)
-            for j in range(PACK):
+        def turn_terms(g, blocks):
+            for j in blocks:
                 for u in range(Q_TILES):
                     nc.tensor.matmul(
                         x[u, g][:, j * P : (j + 1) * P], across[g, j][:, u * P : (u + 1) * P], ident[:],
@@ -210,8 +202,13 @@ def tile_attend_pkv8q_soft_draft_kernel(
         spread_ranks = bank([P, PAGE], "spread", 5)
         for j in range(PACK):
             nc.tensor.transpose(spread_ranks[:, j * P : (j + 1) * P], rank_cols[0][:, j : j + 1].to_broadcast([P, P]), ident[:])
-        hide(1)
-        open_sums(1)
+        for g in range(1, PAGES):
+            for u in range(Q_TILES):
+                x[u, g] = bank([P, PAGE], "x", 2 * (g - 1) + u)
+        hide(1, range(PACK), ACROSS_AT)
+        turn_terms(1, range(PACK))
+        hide(2, range(2), ACROSS_AT + 4 * NQ * PACK)
+        turn_terms(2, range(2))
         hidden = []
         summed = []
         for u in range(Q_TILES):
@@ -236,15 +233,12 @@ def tile_attend_pkv8q_soft_draft_kernel(
         nc.vector.tensor_copy(vs_rows[:], vs_pool[:].indirect(slots[:]))
 
         score(1, 4)
-        rank(2, KW_AT + 4 * PAGE)
-        negate(1)
-        columns(2)
-        hide(2)
+        hide(2, range(2, PACK), KW_AT)
+        turn_terms(2, range(2, PACK))
         score(2, 6)
-        close_sums(1)
-        open_sums(2)
-        negate(2)
-        close_sums(2)
+        for g in range(1, PAGES):
+            negate(g)
+            close_sums(g)
         for g in range(1, PAGES):
             lowest(g, VS_AT + 4 * PAGE * Q_TILES * g, [dealt(x[u, g][:]) for u in range(Q_TILES)])
 

@@ -12,18 +12,13 @@ POOL_PAGES = T // PAGE
 Q_TILES = NQ // P
 ROW = P - 1
 MASKED = 30000.0
-SLOPE = 2.0 ** -17
-STEEP = 2.0 ** 126
-PLAIN_STEEP = 2.0 ** 80
+STEEP = 2.0 ** 80
+DIRECT = 0
+TURNED = (1, 2)
 
-ROW_AT = 4 * T
-VS_AT = ROW_AT + 4 * T
-KS_AT = VS_AT + 4 * T
-P_AT = KS_AT + T
-NEG_AT = P_AT + 4 * PAGE * (Q_TILES * PAGES + 1)
-
-KW_AT = NEG_AT + 4 * PAGE * 2 * PAGES
-ACROSS_AT = KW_AT + 4 * PAGE * PAGES
+KW_AT = 0
+NEG_AT = KW_AT + 4 * N
+P_AT = NEG_AT + 4 * PAGE * 2 * len(TURNED)
 
 FLOPS = 2 * NQ * N * D + 2 * NQ * N * DV
 
@@ -56,8 +51,8 @@ def tile_attend_pkv8q_soft_draft_kernel(
         def bank(shape, name, number):
             return psum.tile(shape, F32, name=name, tag="bank%d" % number)
 
-        def scale_rows(plane, quad):
-            return plane[32 * quad : 32 * quad + 4, :].bitcast(I32)
+        def scale_rows(plane, r):
+            return plane[r:P:32, :].bitcast(I32)
 
         def dealt(row):
             return row.rearrange("q (s h e) -> q h s e", h=2, e=2)
@@ -67,26 +62,26 @@ def tile_attend_pkv8q_soft_draft_kernel(
 
         slots = keep.tile([P, N // 16], U16, name="slots")
         nc.sync.dma_start(slots[:], offs)
-        pos_pool = placed([P, T], F32, "pos_pool", ROW_AT)
+        pos_pool = sb([P, T], F32, "pos_pool")
         nc.sync.dma_start(pos_pool[ROW:P, :], pos[0:1, :])
         qpos_cols = sb([P, Q_TILES], F32, "qpos_cols")
         with nc.allow_non_contiguous_dma(reason="one place a partition and query tile"):
             nc.scalar.dma_start(qpos_cols[:], qpos[0].rearrange("(u p) o -> p (u o)", p=P))
 
-        ks_pool = placed([P, T], U8, "ks_pool", KS_AT)
+        ks_pool = sb([P, T], U8, "ks_pool")
         nc.vector.memset(ks_pool[:].bitcast(I32), 0)
-        for quad in range(4):
-            nc.sync.dma_start(scale_rows(ks_pool, quad), k_scales[0, 4 * quad : 4 * quad + 4, :].bitcast(I32))
+        for r in range(4):
+            nc.sync.dma_start(scale_rows(ks_pool, r), k_scales[0, r:16:4, :].bitcast(I32))
         nc.vector.memset(pos_pool[0:ROW, :], 0.0)
-        kw_pool = placed([P, T], U32, "kw_pool", 0)
+        kw_pool = sb([P, T], U32, "kw_pool")
         nc.sync.dma_start(kw_pool[:].bitcast(I32), k_words[0].rearrange("g t r -> g (t r)").bitcast(I32))
         qw = sb([P, NQ], U32, "qw")
         nc.sync.dma_start(qw[:].bitcast(I32), q_words[0, 0].rearrange("g q r -> g (q r)").bitcast(I32))
         qs = sb([P, NQ], U8, "qs")
         nc.vector.memset(qs[:].bitcast(I32), 0)
-        for quad in range(4):
-            nc.sync.dma_start(scale_rows(qs, quad), q_scales[0, 0, 4 * quad : 4 * quad + 4, :].bitcast(I32))
-        vs_pool = placed([P, T], F32, "vs_pool", VS_AT)
+        for r in range(4):
+            nc.sync.dma_start(scale_rows(qs, r), q_scales[0, 0, r:16:4, :].bitcast(I32))
+        vs_pool = sb([P, T], F32, "vs_pool")
         nc.sync.dma_start(vs_pool[:], vs)
         vcols = keep.tile([P, PAGES * DV // 16], U16, name="vcols")
         nc.sync.dma_start(vcols[:], voffs)
@@ -97,38 +92,32 @@ def tile_attend_pkv8q_soft_draft_kernel(
         )
         vsc_pool = sb([P, POOL_PAGES * DV], U8, "vsc_pool")
         nc.vector.memset(vsc_pool[:].bitcast(I32), 0)
-        for quad in range(4):
+        for r in range(4):
             nc.sync.dma_start(
-                scale_rows(vsc_pool, quad).rearrange("f (u e) -> f u e", u=POOL_PAGES),
-                v_scales[:, 4 * quad : 4 * quad + 4, :].rearrange("u f e -> f u e").bitcast(I32),
+                scale_rows(vsc_pool, r).rearrange("f (u e) -> f u e", u=POOL_PAGES),
+                v_scales[:, r:16:4, :].rearrange("u f e -> f u e").bitcast(I32),
             )
 
         ident = sb([P, P], F32, "ident")
         make_identity(nc, ident[:])
 
-        q_rank = sb([P, Q_TILES], F32, "q_rank")
-        nc.scalar.activation(q_rank[:], qpos_cols[:], ACT.Sigmoid, scale=-SLOPE)
         spread = bank([P, NQ], "spread", 7)
         for u in range(Q_TILES):
-            nc.tensor.transpose(spread[:, u * P : (u + 1) * P], q_rank[:, u : u + 1].to_broadcast([P, P]), ident[:])
+            nc.tensor.transpose(spread[:, u * P : (u + 1) * P], qpos_cols[:, u : u + 1].to_broadcast([P, P]), ident[:])
         q_rows = sb([P, NQ], F32, "q_rows")
-        nc.scalar.activation(q_rows[:], spread[:], ACT.Copy, scale=1.0 - SLOPE / 8)
-
+        nc.scalar.activation(q_rows[:], spread[:], ACT.Copy)
         limit = sb([P, Q_TILES], F32, "limit")
-        nc.scalar.activation(limit[:], qpos_cols[:], ACT.Copy, scale=-PLAIN_STEEP)
+        nc.scalar.activation(limit[:], qpos_cols[:], ACT.Copy, scale=-STEEP)
 
-        rows = [sb([P, PAGE], F32, "row%d" % g) for g in range(PAGES)]
-        nc.vector.tensor_copy(rows[0][:], pos_pool[:].indirect(page_slots(0)))
-        for g in range(1, PAGES):
-            nc.scalar.activation(rows[g][:], pos_pool[:].indirect(page_slots(g)), ACT.Sigmoid, scale=-SLOPE)
-        rank_cols = []
-        for g in range(PAGES):
-            turned = bank([P, PACK, P], "turned", (6, 4, 3)[g])
+        place_cols = {}
+        for g, number in zip(TURNED + (DIRECT,), (6, 4, 3)):
+            row = sb([P, PAGE], F32, "row%d" % g)
+            nc.scalar.activation(row[:], pos_pool[:].indirect(page_slots(g)), ACT.Copy)
+            turned = bank([P, PACK, P], "turned", number)
             for j in range(PACK):
-                nc.tensor.transpose(turned[:, j, :], rows[g][:, j * P : (j + 1) * P], ident[:])
-            cols = sb([P, PACK], F32, "rank_cols%d" % g)
-            nc.scalar.activation(cols[:], turned[:, :, ROW], ACT.Copy, scale=-STEEP if g else PLAIN_STEEP)
-            rank_cols.append(cols)
+                nc.tensor.transpose(turned[:, j, :], row[:, j * P : (j + 1) * P], ident[:])
+            place_cols[g] = sb([P, PACK], F32, "place_cols%d" % g)
+            nc.scalar.activation(place_cols[g][:], turned[:, :, ROW], ACT.Copy, scale=STEEP)
 
         ks = sb([P, N], U8, "ks")
         nc.vector.tensor_copy(ks[:], ks_pool[:].indirect(slots[:]))
@@ -138,33 +127,27 @@ def tile_attend_pkv8q_soft_draft_kernel(
             nc.vector.tensor_copy(words[:], kw_pool[:].indirect(page_slots(g)))
             kw.append(words)
 
-        across = {}
-        neg = {}
         x = {}
-        scores = {}
+        neg = {}
         down = {}
         low = [MASKED] * Q_TILES
 
-        def hide(g, blocks, at):
-            for i, j in enumerate(blocks):
-                across[g, j] = placed([P, NQ], F32, "across%d_%d" % (g, j), at + 4 * NQ * i)
-                nc.scalar.activation(across[g, j][:], q_rows[:], ACT.Relu, bias=rank_cols[g][:, j : j + 1], scale=STEEP)
-
-        def turn_terms(g, blocks):
-            for j in blocks:
-                for u in range(Q_TILES):
-                    nc.tensor.matmul(
-                        x[u, g][:, j * P : (j + 1) * P], across[g, j][:, u * P : (u + 1) * P], ident[:],
-                        start=(j == 0), stop=False, is_transpose=True,
-                    )
+        def hide(g, j, term):
+            nc.scalar.activation(term[:], q_rows[:], ACT.Relu, bias=place_cols[g][:, j : j + 1], scale=-STEEP)
+            for u in range(Q_TILES):
+                nc.tensor.matmul(
+                    x[u, g][:, j * P : (j + 1) * P], term[:, u * P : (u + 1) * P], ident[:],
+                    start=(j == 0), stop=False, is_transpose=True,
+                )
 
         def score(g, first_bank):
+            halves = []
             for half_page in range(2):
-                scores[g, half_page] = bank([P, 2, NQ], "scores", first_bank + half_page)
+                half = bank([P, 2, NQ], "scores", first_bank + half_page)
                 for jj in range(2):
                     j = 2 * half_page + jj
                     nc.tensor.matmul_mx(
-                        out=scores[g, half_page][:, jj, :],
+                        out=half[:, jj, :],
                         lhsT=kw[g][:, j * P : (j + 1) * P].bitcast(FP8X4),
                         lhsT_scale=ks[:, g * PAGE + j * P : g * PAGE + (j + 1) * P],
                         rhs=qw[:].bitcast(FP8X4),
@@ -172,14 +155,13 @@ def tile_attend_pkv8q_soft_draft_kernel(
                         start=True,
                         stop=True,
                     )
+                halves.append(half)
+            return halves
 
-        def negate(g):
+        def add_scores(i, g, halves):
             for half_page in range(2):
-                at = NEG_AT + 4 * PAGE * (2 * g + half_page)
-                neg[g, half_page] = placed([P, 2, NQ], F32, "neg%d_%d" % (g, half_page), at)
-                nc.scalar.activation(neg[g, half_page][:], scores[g, half_page][:], ACT.Copy, scale=-1.0)
-
-        def close_sums(g):
+                neg[g, half_page] = placed([P, 2, NQ], F32, "neg%d_%d" % (g, half_page), NEG_AT + 4 * PAGE * (2 * i + half_page))
+                nc.scalar.activation(neg[g, half_page][:], halves[half_page][:], ACT.Copy, scale=-1.0)
             for half_page in range(2):
                 for u in range(Q_TILES):
                     for jj in range(2):
@@ -189,9 +171,9 @@ def tile_attend_pkv8q_soft_draft_kernel(
                             start=False, stop=(j == PACK - 1), is_transpose=True,
                         )
 
-        def lowest(g, at, sources):
+        def lowest(g, sources):
             for u in range(Q_TILES):
-                down[u, g] = placed([P, 2, P, 2], F32, "down%d_%d" % (u, g), at + 4 * PAGE * u)
+                down[u, g] = sb([P, 2, P, 2], F32, "down%d_%d" % (u, g))
                 lower = sb([P, 1], F32, "low%d_%d" % (u, g))
                 nc.vector.tensor_scalar(
                     down[u, g][:], sources[u], MASKED, low[u],
@@ -199,50 +181,51 @@ def tile_attend_pkv8q_soft_draft_kernel(
                 )
                 low[u] = lower[:]
 
-        spread_ranks = bank([P, PAGE], "spread", 5)
-        for j in range(PACK):
-            nc.tensor.transpose(spread_ranks[:, j * P : (j + 1) * P], rank_cols[0][:, j : j + 1].to_broadcast([P, P]), ident[:])
-        for g in range(1, PAGES):
+        for i, g in enumerate(TURNED):
             for u in range(Q_TILES):
-                x[u, g] = bank([P, PAGE], "x", 2 * (g - 1) + u)
-        hide(1, range(PACK), ACROSS_AT)
-        turn_terms(1, range(PACK))
-        hide(2, range(2), ACROSS_AT + 4 * NQ * PACK)
-        turn_terms(2, range(2))
-        hidden = []
+                x[u, g] = bank([P, PAGE], "x", Q_TILES * i + u)
+        first, last = TURNED
+        for j in range(PACK):
+            hide(first, j, sb([P, NQ], F32, "term%d_%d" % (first, j)))
+        spread_places = bank([P, PAGE], "spread", 5)
+        for j in range(PACK):
+            nc.tensor.transpose(
+                spread_places[:, j * P : (j + 1) * P], place_cols[DIRECT][:, j : j + 1].to_broadcast([P, P]), ident[:]
+            )
+        for j in range(2):
+            hide(last, j, sb([P, NQ], F32, "term%d_%d" % (last, j)))
+
         summed = []
         for u in range(Q_TILES):
-            term = sb([P, 2, P, 2], F32, "hidden%d" % u)
-            nc.scalar.activation(term[:], dealt(spread_ranks[:]), ACT.Relu, bias=limit[:, u : u + 1])
-            hidden.append(term)
-        for u in range(Q_TILES):
+            hidden = sb([P, 2, P, 2], F32, "hidden%d" % u)
+            nc.scalar.activation(hidden[:], dealt(spread_places[:]), ACT.Relu, bias=limit[:, u : u + 1])
             a = bank([P, PAGE], "a", 6 + u)
             nc.tensor.matmul_mx(
                 out=a[:],
                 lhsT=qw[:, u * P : (u + 1) * P].bitcast(FP8X4),
                 lhsT_scale=qs[:, u * P : (u + 1) * P],
-                rhs=kw[0][:].bitcast(FP8X4),
-                rhs_scale=ks[:, 0:PAGE],
+                rhs=kw[DIRECT][:].bitcast(FP8X4),
+                rhs_scale=ks[:, DIRECT * PAGE : (DIRECT + 1) * PAGE],
                 start=True,
                 stop=True,
             )
-            summed.append(placed([P, 2, P, 2], F32, "summed%d" % u, 4 * N * u))
-            nc.vector.tensor_tensor(summed[u][:], hidden[u][:], dealt(a[:]), ALU.subtract)
-        lowest(0, NEG_AT, [tile[:] for tile in summed])
-        vs_rows = placed([P, N], F32, "vs_rows", 0)
-        nc.vector.tensor_copy(vs_rows[:], vs_pool[:].indirect(slots[:]))
+            summed.append(sb([P, 2, P, 2], F32, "summed%d" % u))
+            nc.vector.tensor_tensor(summed[u][:], hidden[:], dealt(a[:]), ALU.subtract)
+        lowest(DIRECT, [tile[:] for tile in summed])
 
-        score(1, 4)
-        hide(2, range(2, PACK), KW_AT)
-        turn_terms(2, range(2, PACK))
-        score(2, 6)
-        for g in range(1, PAGES):
-            negate(g)
-            close_sums(g)
-        for g in range(1, PAGES):
-            lowest(g, VS_AT + 4 * PAGE * Q_TILES * g, [dealt(x[u, g][:]) for u in range(Q_TILES)])
+        first_scores = score(first, 4)
+        for j in range(2, PACK):
+            hide(last, j, placed([P, NQ], F32, "term%d_%d" % (last, j), KW_AT + 4 * PAGE * DIRECT + 4 * NQ * (j - 2)))
+        last_scores = score(last, 6)
+        add_scores(0, first, first_scores)
+        add_scores(1, last, last_scores)
+        for g in TURNED:
+            lowest(g, [dealt(x[u, g][:]) for u in range(Q_TILES)])
 
-        vw = placed([P, PAGES * DV], U32, "vw", VS_AT + 8 * N)
+        vs_rows = placed([P, N], F32, "vs_rows", KW_AT)
+        for g in range(PAGES):
+            nc.scalar.activation(vs_rows[:, g * PAGE : (g + 1) * PAGE], vs_pool[:].indirect(page_slots(g)), ACT.Copy)
+        vw = placed([P, PAGES * DV], U32, "vw", P_AT - 4 * PAGE)
         nc.vector.tensor_copy(vw[:], vw_pool[:].indirect(vcols[:]))
 
         units = [(u, g) for u in range(Q_TILES) for g in range(PAGES)]
@@ -255,21 +238,19 @@ def tile_attend_pkv8q_soft_draft_kernel(
             p = placed([P, 2, P, 2], F32, "p%d" % k, P_AT + 4 * PAGE * k)
             nc.scalar.activation(p[:], down[u, g][:], ACT.Exp, bias=low[u], scale=-1.0, accum_out=sums[:, u, g : g + 1])
             w = sb([P, 2, P, 2], BF16, "w%d" % k)
-            nc.vector.tensor_tensor(
-                w[:], p[:], dealt(vs_rows[:, g * PAGE : (g + 1) * PAGE]), ALU.mult
-            )
+            nc.vector.tensor_tensor(w[:], p[:], dealt(vs_rows[:, g * PAGE : (g + 1) * PAGE]), ALU.mult)
             weights.append(w)
 
-        def quantise(first, count):
-            grouped = sb([P, count, P * PACK], BF16, "grouped%d" % first)
+        def quantise(begin, count):
+            grouped = sb([P, count, P * PACK], BF16, "grouped%d" % begin)
             for i in range(count):
-                pairs = weights[first + i][:].rearrange("q h s e -> q (h s e)").bitcast(F32)
-                turned = bank([P, 2, P], "turned", (0, 1, 2, 3, 6, 7)[first + i])
+                pairs = weights[begin + i][:].rearrange("q h s e -> q (h s e)").bitcast(F32)
+                turned = bank([P, 2, P], "turned", (0, 1, 2, 3, 6, 7)[begin + i])
                 for h in range(2):
                     nc.tensor.transpose(turned[:, h, :], pairs[:, h * P : (h + 1) * P], ident[:])
                 nc.scalar.copy(grouped[:, i, :].bitcast(F32).rearrange("s (q h) -> s q h", h=2), turned[:].rearrange("s h q -> s q h"))
-            codes = sb([P, count * P], U32, "codes%d" % first)
-            scales = sb([P, count * P], U8, "scales%d" % first)
+            codes = sb([P, count * P], U32, "codes%d" % begin)
+            scales = sb([P, count * P], U8, "scales%d" % begin)
             nc.vector.quantize_mx(out=codes[:].bitcast(FP8X4), scales=scales[:], in_=grouped[:].rearrange("s i c -> s (i c)"))
             for i in range(count):
                 quantised.append((codes[:, i * P : (i + 1) * P], scales[:, i * P : (i + 1) * P]))

@@ -112,7 +112,10 @@ def tile_attend_pkv8q_soft_draft_kernel(
         place_cols = {}
         for g, number in zip(TURNED + (DIRECT,), (6, 4, 3)):
             row = sb([P, PAGE], F32, "row%d" % g)
-            nc.scalar.activation(row[:], pos_pool[:].indirect(page_slots(g)), ACT.Copy)
+            if g == TURNED[0]:
+                nc.vector.tensor_copy(row[:], pos_pool[:].indirect(page_slots(g)))
+            else:
+                nc.scalar.activation(row[:], pos_pool[:].indirect(page_slots(g)), ACT.Copy)
             turned = bank([P, PACK, P], "turned", number)
             for j in range(PACK):
                 nc.tensor.transpose(turned[:, j, :], row[:, j * P : (j + 1) * P], ident[:])

@@ -17,7 +17,8 @@ DIRECT = 0
 TURNED = (1, 2)
 
 KW_AT = 0
-NEG_AT = KW_AT + 4 * N
+HIDDEN_AT = KW_AT + 4 * N
+NEG_AT = HIDDEN_AT + 4 * PAGE * Q_TILES
 P_AT = NEG_AT + 4 * PAGE * 2 * len(TURNED)
 
 FLOPS = 2 * NQ * N * D + 2 * NQ * N * DV
@@ -77,11 +78,42 @@ def tile_attend_pkv8q_soft_draft_kernel(
         nc.sync.dma_start(kw_pool[:].bitcast(I32), k_words[0].rearrange("g t r -> g (t r)").bitcast(I32))
         qw = sb([P, NQ], U32, "qw")
         nc.sync.dma_start(qw[:].bitcast(I32), q_words[0, 0].rearrange("g q r -> g (q r)").bitcast(I32))
+
+        ident = sb([P, P], F32, "ident")
+        make_identity(nc, ident[:])
+
+        spread = bank([P, NQ], "spread", 7)
+        for u in range(Q_TILES):
+            nc.tensor.transpose(spread[:, u * P : (u + 1) * P], qpos_cols[:, u : u + 1].to_broadcast([P, P]), ident[:])
+        q_rows = sb([P, NQ], F32, "q_rows")
+        nc.scalar.activation(q_rows[:], spread[:], ACT.Copy)
+        limit = sb([P, Q_TILES], F32, "limit")
+        nc.scalar.activation(limit[:], qpos_cols[:], ACT.Copy, scale=-STEEP)
+
+        first, last = TURNED
+        place_cols = {}
+        for g, number in zip((first, last, DIRECT), (6, 4, 3)):
+            turned = bank([P, PACK, P], "turned", number)
+            parts = 1 if g == last else 2
+            width = PAGE // parts
+            for part in range(parts):
+                begin = g * PAGE + part * width
+                row = sb([P, width], F32, "row%d_%d" % (g, part))
+                window = pos_pool[:].indirect(slots[:, begin // 16 : (begin + width) // 16])
+                if g == first or (g == DIRECT and part == 0):
+                    nc.vector.tensor_copy(row[:], window)
+                else:
+                    nc.scalar.activation(row[:], window, ACT.Copy)
+                for j in range(width // P):
+                    nc.tensor.transpose(turned[:, part * width // P + j, :], row[:, j * P : (j + 1) * P], ident[:])
+            place_cols[g] = sb([P, PACK], F32, "place_cols%d" % g)
+            nc.scalar.activation(place_cols[g][:], turned[:, :, ROW], ACT.Copy, scale=STEEP)
+
         qs = sb([P, NQ], U8, "qs")
         nc.vector.memset(qs[:].bitcast(I32), 0)
         for r in range(4):
             nc.sync.dma_start(scale_rows(qs, r), q_scales[0, 0, r:16:4, :].bitcast(I32))
-        vs_pool = sb([P, T], F32, "vs_pool")
+        vs_pool = placed([P, T], F32, "vs_pool", P_AT)
         nc.sync.dma_start(vs_pool[:], vs)
         vcols = keep.tile([P, PAGES * DV // 16], U16, name="vcols")
         nc.sync.dma_start(vcols[:], voffs)
@@ -97,30 +129,6 @@ def tile_attend_pkv8q_soft_draft_kernel(
                 scale_rows(vsc_pool, r).rearrange("f (u e) -> f u e", u=POOL_PAGES),
                 v_scales[:, r:16:4, :].rearrange("u f e -> f u e").bitcast(I32),
             )
-
-        ident = sb([P, P], F32, "ident")
-        make_identity(nc, ident[:])
-
-        spread = bank([P, NQ], "spread", 7)
-        for u in range(Q_TILES):
-            nc.tensor.transpose(spread[:, u * P : (u + 1) * P], qpos_cols[:, u : u + 1].to_broadcast([P, P]), ident[:])
-        q_rows = sb([P, NQ], F32, "q_rows")
-        nc.scalar.activation(q_rows[:], spread[:], ACT.Copy)
-        limit = sb([P, Q_TILES], F32, "limit")
-        nc.scalar.activation(limit[:], qpos_cols[:], ACT.Copy, scale=-STEEP)
-
-        place_cols = {}
-        for g, number in zip(TURNED + (DIRECT,), (6, 4, 3)):
-            row = sb([P, PAGE], F32, "row%d" % g)
-            if g == TURNED[0]:
-                nc.vector.tensor_copy(row[:], pos_pool[:].indirect(page_slots(g)))
-            else:
-                nc.scalar.activation(row[:], pos_pool[:].indirect(page_slots(g)), ACT.Copy)
-            turned = bank([P, PACK, P], "turned", number)
-            for j in range(PACK):
-                nc.tensor.transpose(turned[:, j, :], row[:, j * P : (j + 1) * P], ident[:])
-            place_cols[g] = sb([P, PACK], F32, "place_cols%d" % g)
-            nc.scalar.activation(place_cols[g][:], turned[:, :, ROW], ACT.Copy, scale=STEEP)
 
         ks = sb([P, N], U8, "ks")
         nc.vector.tensor_copy(ks[:], ks_pool[:].indirect(slots[:]))
@@ -143,10 +151,10 @@ def tile_attend_pkv8q_soft_draft_kernel(
                     start=(j == 0), stop=False, is_transpose=True,
                 )
 
-        def score(g, first_bank):
+        def score(g, banks):
             halves = []
             for half_page in range(2):
-                half = bank([P, 2, NQ], "scores", first_bank + half_page)
+                half = bank([P, 2, NQ], "scores", banks[half_page])
                 for jj in range(2):
                     j = 2 * half_page + jj
                     nc.tensor.matmul_mx(
@@ -165,14 +173,12 @@ def tile_attend_pkv8q_soft_draft_kernel(
             for half_page in range(2):
                 neg[g, half_page] = placed([P, 2, NQ], F32, "neg%d_%d" % (g, half_page), NEG_AT + 4 * PAGE * (2 * i + half_page))
                 nc.scalar.activation(neg[g, half_page][:], halves[half_page][:], ACT.Copy, scale=-1.0)
-            for half_page in range(2):
-                for u in range(Q_TILES):
-                    for jj in range(2):
-                        j = 2 * half_page + jj
-                        nc.tensor.matmul(
-                            x[u, g][:, j * P : (j + 1) * P], neg[g, half_page][:, jj, u * P : (u + 1) * P], ident[:],
-                            start=False, stop=(j == PACK - 1), is_transpose=True,
-                        )
+            for u in range(Q_TILES):
+                for j in range(PACK):
+                    nc.tensor.matmul(
+                        x[u, g][:, j * P : (j + 1) * P], neg[g, j // 2][:, j % 2, u * P : (u + 1) * P], ident[:],
+                        start=False, stop=(j == PACK - 1), is_transpose=True,
+                    )
 
         def lowest(g, sources):
             for u in range(Q_TILES):
@@ -187,7 +193,6 @@ def tile_attend_pkv8q_soft_draft_kernel(
         for i, g in enumerate(TURNED):
             for u in range(Q_TILES):
                 x[u, g] = bank([P, PAGE], "x", Q_TILES * i + u)
-        first, last = TURNED
         for j in range(PACK):
             hide(first, j, sb([P, NQ], F32, "term%d_%d" % (first, j)))
         spread_places = bank([P, PAGE], "spread", 5)
@@ -195,12 +200,12 @@ def tile_attend_pkv8q_soft_draft_kernel(
             nc.tensor.transpose(
                 spread_places[:, j * P : (j + 1) * P], place_cols[DIRECT][:, j : j + 1].to_broadcast([P, P]), ident[:]
             )
-        for j in range(2):
+        for j in range(PACK):
             hide(last, j, sb([P, NQ], F32, "term%d_%d" % (last, j)))
 
         summed = []
         for u in range(Q_TILES):
-            hidden = sb([P, 2, P, 2], F32, "hidden%d" % u)
+            hidden = placed([P, 2, P, 2], F32, "hidden%d" % u, HIDDEN_AT + 4 * PAGE * u)
             nc.scalar.activation(hidden[:], dealt(spread_places[:]), ACT.Relu, bias=limit[:, u : u + 1])
             a = bank([P, PAGE], "a", 6 + u)
             nc.tensor.matmul_mx(
@@ -216,16 +221,14 @@ def tile_attend_pkv8q_soft_draft_kernel(
             nc.vector.tensor_tensor(summed[u][:], hidden[:], dealt(a[:]), ALU.subtract)
         lowest(DIRECT, [tile[:] for tile in summed])
 
-        first_scores = score(first, 4)
-        for j in range(2, PACK):
-            hide(last, j, placed([P, NQ], F32, "term%d_%d" % (last, j), KW_AT + 4 * PAGE * DIRECT + 4 * NQ * (j - 2)))
-        last_scores = score(last, 6)
+        first_scores = score(first, (4, 5))
+        last_scores = score(last, (4, 6))
         add_scores(0, first, first_scores)
         add_scores(1, last, last_scores)
         for g in TURNED:
             lowest(g, [dealt(x[u, g][:]) for u in range(Q_TILES)])
 
-        vs_rows = placed([P, N], F32, "vs_rows", KW_AT)
+        vs_rows = placed([P, N], F32, "vs_rows", NEG_AT - 4 * N)
         for g in range(PAGES):
             nc.scalar.activation(vs_rows[:, g * PAGE : (g + 1) * PAGE], vs_pool[:].indirect(page_slots(g)), ACT.Copy)
         vw = placed([P, PAGES * DV], U32, "vw", P_AT - 4 * PAGE)

@@ -229,8 +229,7 @@ def tile_attend_pkv8q_soft_draft_kernel(
             lowest(g, [dealt(x[u, g][:]) for u in range(Q_TILES)])
 
         vs_rows = placed([P, N], F32, "vs_rows", NEG_AT - 4 * N)
-        for g in range(PAGES):
-            nc.scalar.activation(vs_rows[:, g * PAGE : (g + 1) * PAGE], vs_pool[:].indirect(page_slots(g)), ACT.Copy)
+        nc.scalar.activation(vs_rows[:], vs_pool[:].indirect(slots[:]), ACT.Copy)
         vw = placed([P, PAGES * DV], U32, "vw", P_AT - 4 * PAGE)
         nc.vector.tensor_copy(vw[:], vw_pool[:].indirect(vcols[:]))
 

@@ -20,6 +20,7 @@ KW_AT = 0
 HIDDEN_AT = KW_AT + 4 * N
 NEG_AT = HIDDEN_AT + 4 * PAGE * Q_TILES
 P_AT = NEG_AT + 4 * PAGE * 2 * len(TURNED)
+KS_AT = P_AT + 4 * T
 
 FLOPS = 2 * NQ * N * D + 2 * NQ * N * DV
 
@@ -86,7 +87,7 @@ def tile_attend_pkv8q_soft_draft_kernel(
         for u in range(Q_TILES):
             nc.tensor.transpose(spread[:, u * P : (u + 1) * P], qpos_cols[:, u : u + 1].to_broadcast([P, P]), ident[:])
         q_rows = sb([P, NQ], F32, "q_rows")
-        nc.scalar.activation(q_rows[:], spread[:], ACT.Copy)
+        nc.scalar.activation(q_rows[:], spread[:], ACT.Copy, scale=STEEP)
         limit = sb([P, Q_TILES], F32, "limit")
         nc.scalar.activation(limit[:], qpos_cols[:], ACT.Copy, scale=-STEEP)
 
@@ -106,7 +107,10 @@ def tile_attend_pkv8q_soft_draft_kernel(
                     nc.scalar.activation(row[:], window, ACT.Copy)
                 for j in range(width // P):
                     nc.tensor.transpose(turned[:, part * width // P + j, :], row[:, j * P : (j + 1) * P], ident[:])
-            place_cols[g] = sb([P, PACK], F32, "place_cols%d" % g)
+            if g == first:
+                place_cols[g] = placed([P, PACK], F32, "place_cols%d" % g, KS_AT)
+            else:
+                place_cols[g] = sb([P, PACK], F32, "place_cols%d" % g)
             nc.scalar.activation(place_cols[g][:], turned[:, :, ROW], ACT.Copy, scale=STEEP)
 
         qs = sb([P, NQ], U8, "qs")
@@ -130,8 +134,11 @@ def tile_attend_pkv8q_soft_draft_kernel(
                 v_scales[:, r:16:4, :].rearrange("u f e -> f u e").bitcast(I32),
             )
 
-        ks = sb([P, N], U8, "ks")
-        nc.vector.tensor_copy(ks[:], ks_pool[:].indirect(slots[:]))
+        ks_first = sb([P, PAGE], U8, "ks_first")
+        nc.vector.tensor_copy(ks_first[:], ks_pool[:].indirect(page_slots(0)))
+        ks_rest = placed([P, N - PAGE], U8, "ks_rest", KS_AT)
+        nc.vector.tensor_copy(ks_rest[:], ks_pool[:].indirect(slots[:, PAGE // 16 :]))
+        ks = [ks_first[:], ks_rest[:, :PAGE], ks_rest[:, PAGE:]]
         kw = []
         for g in range(PAGES):
             words = placed([P, PAGE], U32, "kw%d" % g, KW_AT + 4 * PAGE * g)
@@ -144,7 +151,10 @@ def tile_attend_pkv8q_soft_draft_kernel(
         low = [MASKED] * Q_TILES
 
         def hide(g, j, term):
-            nc.scalar.activation(term[:], q_rows[:], ACT.Relu, bias=place_cols[g][:, j : j + 1], scale=-STEEP)
+            if g == first:
+                nc.vector.tensor_scalar(term[:], q_rows[:], place_cols[g][:, j : j + 1], STEEP, op0=ALU.is_lt, op1=ALU.mult)
+            else:
+                nc.scalar.activation(term[:], q_rows[:], ACT.Relu, bias=place_cols[g][:, j : j + 1], scale=-1.0)
             for u in range(Q_TILES):
                 nc.tensor.matmul(
                     x[u, g][:, j * P : (j + 1) * P], term[:, u * P : (u + 1) * P], ident[:],
@@ -160,7 +170,7 @@ def tile_attend_pkv8q_soft_draft_kernel(
                     nc.tensor.matmul_mx(
                         out=half[:, jj, :],
                         lhsT=kw[g][:, j * P : (j + 1) * P].bitcast(FP8X4),
-                        lhsT_scale=ks[:, g * PAGE + j * P : g * PAGE + (j + 1) * P],
+                        lhsT_scale=ks[g][:, j * P : (j + 1) * P],
                         rhs=qw[:].bitcast(FP8X4),
                         rhs_scale=qs[:],
                         start=True,
@@ -213,7 +223,7 @@ def tile_attend_pkv8q_soft_draft_kernel(
                 lhsT=qw[:, u * P : (u + 1) * P].bitcast(FP8X4),
                 lhsT_scale=qs[:, u * P : (u + 1) * P],
                 rhs=kw[DIRECT][:].bitcast(FP8X4),
-                rhs_scale=ks[:, DIRECT * PAGE : (DIRECT + 1) * PAGE],
+                rhs_scale=ks[DIRECT],
                 start=True,
                 stop=True,
             )

from contextlib import ExitStack

import concourse.mybir as mybir
from concourse.masks import make_identity

N, T, D, DV, NQ = 1536, 4096, 512, 128, 256
PAGE = 512
P = 128
PACK = 4
PAGES = N // PAGE
POOL_PAGES = T // PAGE
Q_TILES = NQ // P
ROW = P - 1
MASKED = 30000.0
STEEP = 2.0 ** 80
DIRECT = 0
TURNED = (1, 2)

KW_AT = 0
HIDDEN_AT = KW_AT + 4 * N
NEG_AT = HIDDEN_AT + 4 * PAGE * Q_TILES
P_AT = NEG_AT + 4 * PAGE * 2 * len(TURNED)
KS_AT = P_AT + 4 * T

FLOPS = 2 * NQ * N * D + 2 * NQ * N * DV

F32 = mybir.dt.float32
BF16 = mybir.dt.bfloat16
I32 = mybir.dt.int32
U32 = mybir.dt.uint32
U16 = mybir.dt.uint16
U8 = mybir.dt.uint8
FP8X4 = mybir.dt.float8_e4m3fn_x4
ALU = mybir.AluOpType
ACT = mybir.ActivationFunctionType


def tile_attend_pkv8q_soft_draft_kernel(
    tc, q_words, q_scales, k_words, k_scales, v_words, v_scales, vs, pos, qpos, offs, voffs, out
):
    nc = tc.nc
    with ExitStack() as ctx:
        keep = ctx.enter_context(tc.tile_pool(name="keep", bufs=1))
        shared = ctx.enter_context(tc.tile_pool(name="shared", bufs=1))
        psum = ctx.enter_context(tc.psum_pool(name="psum", bufs=1))

        def sb(shape, dtype, name):
            return keep.tile(shape, dtype, name=name, tag=name, align_bytes=64)

        def placed(shape, dtype, name, offset):
            return shared.tile(shape, dtype, name=name, offset=offset, align_bytes=64)

        def bank(shape, name, number):
            return psum.tile(shape, F32, name=name, tag="bank%d" % number)

        def scale_rows(plane, r):
            return plane[r:P:32, :].bitcast(I32)

        def dealt(row):
            return row.rearrange("q (s h e) -> q h s e", h=2, e=2)

        def page_slots(g):
            return slots[:, g * PAGE // 16 : (g + 1) * PAGE // 16]

        slots = keep.tile([P, N // 16], U16, name="slots")
        nc.sync.dma_start(slots[:], offs)
        pos_pool = sb([P, T], F32, "pos_pool")
        nc.sync.dma_start(pos_pool[ROW:P, :], pos[0:1, :])
        qpos_cols = sb([P, Q_TILES], F32, "qpos_cols")
        with nc.allow_non_contiguous_dma(reason="one place a partition and query tile"):
            nc.scalar.dma_start(qpos_cols[:], qpos[0].rearrange("(u p) o -> p (u o)", p=P))

        ks_pool = sb([P, T], U8, "ks_pool")
        nc.vector.memset(ks_pool[:].bitcast(I32), 0)
        for r in range(4):
            nc.sync.dma_start(scale_rows(ks_pool, r), k_scales[0, r:16:4, :].bitcast(I32))
        nc.vector.memset(pos_pool[0:ROW, :], 0.0)
        kw_pool = sb([P, T], U32, "kw_pool")
        nc.sync.dma_start(kw_pool[:].bitcast(I32), k_words[0].rearrange("g t r -> g (t r)").bitcast(I32))
        qw = sb([P, NQ], U32, "qw")
        nc.sync.dma_start(qw[:].bitcast(I32), q_words[0, 0].rearrange("g q r -> g (q r)").bitcast(I32))

        ident = sb([P, P], F32, "ident")
        make_identity(nc, ident[:])

        spread = bank([P, NQ], "spread", 7)
        for u in range(Q_TILES):
            nc.tensor.transpose(spread[:, u * P : (u + 1) * P], qpos_cols[:, u : u + 1].to_broadcast([P, P]), ident[:])
        q_rows = sb([P, NQ], F32, "q_rows")
        nc.scalar.activation(q_rows[:], spread[:], ACT.Copy, scale=STEEP)
        limit = sb([P, Q_TILES], F32, "limit")
        nc.scalar.activation(limit[:], qpos_cols[:], ACT.Copy, scale=-STEEP)

        first, last = TURNED
        place_cols = {}
        for g, number in zip((first, last, DIRECT), (6, 4, 3)):
            turned = bank([P, PACK, P], "turned", number)
            parts = 1 if g == last else 2
            width = PAGE // parts
            for part in range(parts):
                begin = g * PAGE + part * width
                row = sb([P, width], F32, "row%d_%d" % (g, part))
                window = pos_pool[:].indirect(slots[:, begin // 16 : (begin + width) // 16])
                if g == first or (g == DIRECT and part == 0):
                    nc.vector.tensor_copy(row[:], window)
                else:
                    nc.scalar.activation(row[:], window, ACT.Copy)
                for j in range(width // P):
                    nc.tensor.transpose(turned[:, part * width // P + j, :], row[:, j * P : (j + 1) * P], ident[:])
            if g == first:
                place_cols[g] = placed([P, PACK], F32, "place_cols%d" % g, KS_AT)
            else:
                place_cols[g] = sb([P, PACK], F32, "place_cols%d" % g)
            nc.scalar.activation(place_cols[g][:], turned[:, :, ROW], ACT.Copy, scale=STEEP)

        qs = sb([P, NQ], U8, "qs")
        nc.vector.memset(qs[:].bitcast(I32), 0)
        for r in range(4):
            nc.sync.dma_start(scale_rows(qs, r), q_scales[0, 0, r:16:4, :].bitcast(I32))
        vs_pool = placed([P, T], F32, "vs_pool", P_AT)
        nc.sync.dma_start(vs_pool[:], vs)
        vcols = keep.tile([P, PAGES * DV // 16], U16, name="vcols")
        nc.sync.dma_start(vcols[:], voffs)
        vw_pool = sb([P, POOL_PAGES * DV], U32, "vw_pool")
        nc.sync.dma_start(
            vw_pool[:].bitcast(I32).rearrange("g (u e) -> g u e", e=DV),
            v_words.rearrange("u g e r -> g u (e r)").bitcast(I32),
        )
        vsc_pool = sb([P, POOL_PAGES * DV], U8, "vsc_pool")
        nc.vector.memset(vsc_pool[:].bitcast(I32), 0)
        for r in range(4):
            nc.sync.dma_start(
                scale_rows(vsc_pool, r).rearrange("f (u e) -> f u e", u=POOL_PAGES),
                v_scales[:, r:16:4, :].rearrange("u f e -> f u e").bitcast(I32),
            )

        ks_first = sb([P, PAGE], U8, "ks_first")
        nc.vector.tensor_copy(ks_first[:], ks_pool[:].indirect(page_slots(0)))
        ks_rest = placed([P, N - PAGE], U8, "ks_rest", KS_AT)
        nc.vector.tensor_copy(ks_rest[:], ks_pool[:].indirect(slots[:, PAGE // 16 :]))
        ks = [ks_first[:], ks_rest[:, :PAGE], ks_rest[:, PAGE:]]
        kw = []
        for g in range(PAGES):
            words = placed([P, PAGE], U32, "kw%d" % g, KW_AT + 4 * PAGE * g)
            nc.vector.tensor_copy(words[:], kw_pool[:].indirect(page_slots(g)))
            kw.append(words)

        x = {}
        neg = {}
        down = {}
        low = [MASKED] * Q_TILES

        def hide(g, j, term):
            if g == first:
                nc.vector.tensor_scalar(term[:], q_rows[:], place_cols[g][:, j : j + 1], STEEP, op0=ALU.is_lt, op1=ALU.mult)
            else:
                nc.scalar.activation(term[:], q_rows[:], ACT.Relu, bias=place_cols[g][:, j : j + 1], scale=-1.0)
            for u in range(Q_TILES):
                nc.tensor.matmul(
                    x[u, g][:, j * P : (j + 1) * P], term[:, u * P : (u + 1) * P], ident[:],
                    start=(j == 0), stop=False, is_transpose=True,
                )

        def score(g, banks):
            halves = []
            for half_page in range(2):
                half = bank([P, 2, NQ], "scores", banks[half_page])
                for jj in range(2):
                    j = 2 * half_page + jj
                    nc.tensor.matmul_mx(
                        out=half[:, jj, :],
                        lhsT=kw[g][:, j * P : (j + 1) * P].bitcast(FP8X4),
                        lhsT_scale=ks[g][:, j * P : (j + 1) * P],
                        rhs=qw[:].bitcast(FP8X4),
                        rhs_scale=qs[:],
                        start=True,
                        stop=True,
                    )
                halves.append(half)
            return halves

        def add_scores(i, g, halves):
            for half_page in range(2):
                neg[g, half_page] = placed([P, 2, NQ], F32, "neg%d_%d" % (g, half_page), NEG_AT + 4 * PAGE * (2 * i + half_page))
                nc.scalar.activation(neg[g, half_page][:], halves[half_page][:], ACT.Copy, scale=-1.0)
            for u in range(Q_TILES):
                for j in range(PACK):
                    nc.tensor.matmul(
                        x[u, g][:, j * P : (j + 1) * P], neg[g, j // 2][:, j % 2, u * P : (u + 1) * P], ident[:],
                        start=False, stop=(j == PACK - 1), is_transpose=True,
                    )

        def lowest(g, sources):
            for u in range(Q_TILES):
                down[u, g] = sb([P, 2, P, 2], F32, "down%d_%d" % (u, g))
                lower = sb([P, 1], F32, "low%d_%d" % (u, g))
                nc.vector.tensor_scalar(
                    down[u, g][:], sources[u], MASKED, low[u],
                    op0=ALU.min, op1=ALU.min, accum_out=lower[:],
                )
                low[u] = lower[:]

        for i, g in enumerate(TURNED):
            for u in range(Q_TILES):
                x[u, g] = bank([P, PAGE], "x", Q_TILES * i + u)
        for j in range(PACK):
            hide(first, j, sb([P, NQ], F32, "term%d_%d" % (first, j)))
        spread_places = bank([P, PAGE], "spread", 5)
        for j in range(PACK):
            nc.tensor.transpose(
                spread_places[:, j * P : (j + 1) * P], place_cols[DIRECT][:, j : j + 1].to_broadcast([P, P]), ident[:]
            )
        for j in range(PACK):
            hide(last, j, sb([P, NQ], F32, "term%d_%d" % (last, j)))

        summed = []
        for u in range(Q_TILES):
            hidden = placed([P, 2, P, 2], F32, "hidden%d" % u, HIDDEN_AT + 4 * PAGE * u)
            nc.scalar.activation(hidden[:], dealt(spread_places[:]), ACT.Relu, bias=limit[:, u : u + 1])
            a = bank([P, PAGE], "a", 6 + u)
            nc.tensor.matmul_mx(
                out=a[:],
                lhsT=qw[:, u * P : (u + 1) * P].bitcast(FP8X4),
                lhsT_scale=qs[:, u * P : (u + 1) * P],
                rhs=kw[DIRECT][:].bitcast(FP8X4),
                rhs_scale=ks[DIRECT],
                start=True,
                stop=True,
            )
            summed.append(sb([P, 2, P, 2], F32, "summed%d" % u))
            nc.vector.tensor_tensor(summed[u][:], hidden[:], dealt(a[:]), ALU.subtract)
        lowest(DIRECT, [tile[:] for tile in summed])

        first_scores = score(first, (4, 5))
        last_scores = score(last, (4, 6))
        add_scores(0, first, first_scores)
        add_scores(1, last, last_scores)
        for g in TURNED:
            lowest(g, [dealt(x[u, g][:]) for u in range(Q_TILES)])

        vs_rows = placed([P, N], F32, "vs_rows", NEG_AT - 4 * N)
        nc.scalar.activation(vs_rows[:], vs_pool[:].indirect(slots[:]), ACT.Copy)
        vw = placed([P, PAGES * DV], U32, "vw", P_AT - 4 * PAGE)
        nc.vector.tensor_copy(vw[:], vw_pool[:].indirect(vcols[:]))

        units = [(u, g) for u in range(Q_TILES) for g in range(PAGES)]
        sums = sb([P, Q_TILES, PAGES], F32, "sums")
        weights = []
        quantised = []

        def weigh(k):
            u, g = units[k]
            p = placed([P, 2, P, 2], F32, "p%d" % k, P_AT + 4 * PAGE * k)
            nc.scalar.activation(p[:], down[u, g][:], ACT.Exp, bias=low[u], scale=-1.0, accum_out=sums[:, u, g : g + 1])
            w = sb([P, 2, P, 2], BF16, "w%d" % k)
            nc.vector.tensor_tensor(w[:], p[:], dealt(vs_rows[:, g * PAGE : (g + 1) * PAGE]), ALU.mult)
            weights.append(w)

        def quantise(begin, count):
            grouped = sb([P, count, P * PACK], BF16, "grouped%d" % begin)
            for i in range(count):
                pairs = weights[begin + i][:].rearrange("q h s e -> q (h s e)").bitcast(F32)
                turned = bank([P, 2, P], "turned", (0, 1, 2, 3, 6, 7)[begin + i])
                for h in range(2):
                    nc.tensor.transpose(turned[:, h, :], pairs[:, h * P : (h + 1) * P], ident[:])
                nc.scalar.copy(grouped[:, i, :].bitcast(F32).rearrange("s (q h) -> s q h", h=2), turned[:].rearrange("s h q -> s q h"))
            codes = sb([P, count * P], U32, "codes%d" % begin)
            scales = sb([P, count * P], U8, "scales%d" % begin)
            nc.vector.quantize_mx(out=codes[:].bitcast(FP8X4), scales=scales[:], in_=grouped[:].rearrange("s i c -> s (i c)"))
            for i in range(count):
                quantised.append((codes[:, i * P : (i + 1) * P], scales[:, i * P : (i + 1) * P]))

        for k in range(len(units)):
            weigh(k)
        vsc = placed([P, PAGES * DV], U8, "vsc", P_AT + 4 * PAGE * (len(units) - 2))
        nc.vector.tensor_copy(vsc[:], vsc_pool[:].indirect(vcols[:]))
        total = sb([P, Q_TILES], F32, "total")
        nc.vector.tensor_reduce(total[:], sums[:], mybir.AxisListType.X, ALU.add)
        quantise(0, 2)
        inverse = sb([P, Q_TILES], F32, "inverse")
        nc.vector.reciprocal(inverse[:], total[:])
        quantise(2, 2)
        quantise(4, 1)
        quantise(5, 1)

        for u in range(Q_TILES):
            y = bank([P, DV], "y", 4 + u)
            for g in range(PAGES):
                codes, scales = quantised[PAGES * u + g]
                nc.tensor.matmul_mx(
                    out=y[:],
                    lhsT=codes.bitcast(FP8X4),
                    lhsT_scale=scales,
                    rhs=vw[:, g * DV : (g + 1) * DV].bitcast(FP8X4),
                    rhs_scale=vsc[:, g * DV : (g + 1) * DV],
                    start=(g == 0),
                    stop=(g == PAGES - 1),
                )
            result = sb([P, DV], F32, "result%d" % u)
            nc.scalar.activation(result[:], y[:], ACT.Copy, scale=inverse[:, u : u + 1])
            nc.sync.dma_start(out[0, u * P : (u + 1) * P, :], result[:])
